import numpy as np, ml_dtypes
CORES = [9,25,41,57]
N = 4
BF = ml_dtypes.bfloat16
def gentries(a):
    return np.ascontiguousarray(a.reshape(8, 16, -1).transpose(0, 2, 1)).reshape(8, -1)
def gtable(e):
    e = np.asarray(e); return np.ascontiguousarray(e.reshape(8, -1, 16).transpose(0, 2, 1)).reshape(128, -1).astype(np.int32)
V, X, SW, RO, CAP = 896, 128, 3, 2, 48
E = (N - 1) * X
Q = 4 ** SW
def base(rng, top):
    b = rng.integers(top // 10, top * 9 // 10, (N, 8, 1, V))
    debt = np.clip(b + rng.integers(-(top // 16), top // 16 + 1, (N, 8, 16, V)), 1, top)
    c = rng.integers(1, top // 5 + 1, (N, 8, 1, 4 * V)); few = rng.random((N, 8, 1, 4 * V)) < 0.5
    coll = np.where(few, 0, np.clip(c + rng.integers(-16, 17, (N, 8, 16, 4 * V)), 0, top // 5))
    o = np.argsort(rng.random((N, 8, 4 * V)), axis=-1)
    rest = np.concatenate([o[..., E:], np.broadcast_to(4 * V + np.arange(E), (N, 8, E))], axis=-1)
    sg = np.take_along_axis(rest, np.argsort(rng.random((N, 8, 4 * V)), axis=-1), 2)
    return {"cash": rng.integers(0, top // 8 + 1, (N, 8, 16, V)), "debt": debt, "coll": coll, "sg": sg, "xp": np.ascontiguousarray(o[..., :E]),
            "th": Q + rng.integers(0, Q // 4 + 1, (N, 8, 16)), "val": real(rng, 0)}
def real(rng, w):
    s = np.exp2(rng.integers(-w, w + 1, (N, 8, 1, V)))
    return (s * (0.5 + rng.random((N, 8, 16, V)))).astype(np.float32)
def lay(rng, S, C, F, at=None):
    S = np.asarray(S, np.int64).reshape(-1); C = np.asarray(C, np.int64).reshape(-1); F = np.asarray(F, np.int64).reshape(-1)
    left = rng.permutation(np.setdiff1d(np.arange(4 * V), np.concatenate([C, F]))); m = E - len(F)
    x = np.full(E, -1, np.int64); x[rng.permutation(E)[:len(F)] if at is None else at] = F; x[x < 0] = left[:m]
    s = np.full(4 * V, -1, np.int64); s[S] = C
    s[s < 0] = rng.permutation(np.concatenate([left[m:], np.setdiff1d(4 * V + np.arange(E), C)]))
    return s, x
def four_of(b):
    return (4 * np.asarray(b, np.int64)[:, None] + np.arange(4)).reshape(-1)
def pack(d):
    return {"cash": d["cash"].reshape(N, 128, V).astype(np.int32), "debt": d["debt"].reshape(N, 128, V).astype(np.int32),
            "coll": d["coll"].reshape(N, 128, 4 * V).astype(np.float32).astype(BF), "sig": np.stack([gtable(a) for a in d["sg"]]),
            "xpt": np.stack([gtable(a) for a in d["xp"]]), "th": d["th"].reshape(N, 128, 1).astype(np.int32), "val": np.ascontiguousarray(d["val"].reshape(N, 128, V)).astype(np.float32)}
def setup_inputs(rng):
    return pack(base(rng, 1000))
def setup_inputs_spread(rng):
    d = base(rng, 1000); one = (N, 8, 1, V); full = (N, 8, 16, V)
    b = np.where(rng.random(one) < 0.5, np.exp2(10 * rng.random(one)), 1 + 1023 * rng.random(one))
    d["debt"] = np.clip((b * (0.75 + 0.5 * rng.random(full))).astype(np.int64), 1, 1023)
    d["cash"] = np.clip((np.exp2(10 * rng.random(one) ** 2) * rng.random(full)).astype(np.int64), 0, 1023)
    c = np.exp2(8 * rng.random((N, 8, 1, 4 * V))) * (rng.random((N, 8, 1, 4 * V)) < 0.5)
    d["coll"] = np.clip((c * rng.random((N, 8, 16, 4 * V))).astype(np.int64), 0, 255)
    d["th"] = Q + (SW * Q * rng.random((N, 8, 16)) ** 4).astype(np.int64)
    d["val"] = 32.0 * real(rng, 1)
    return pack(d)
def setup_inputs_ends(rng):
    d = base(rng, 1000); full = (N, 8, 16, V)
    z = np.where(rng.random((N, 8, 1, V)) < 0.5, rng.random((N, 8, 1, V)), rng.random(full))
    d["cash"] = np.where(z < 0.8, 0, 1023); d["debt"] = np.where((z < 0.6) | (z > 0.87), 1023, 1)
    c = np.where(rng.random((N, 8, 1, 4 * V)) < 0.5, rng.random((N, 8, 1, 4 * V)), rng.random((N, 8, 16, 4 * V)))
    d["coll"] = np.where(c < 0.25, 255, 0)
    d["val"] = np.where(rng.random(full) < 0.75, 128.0, 8.0)
    n = rng.choice(np.array([0, 8, 9, 16]), (N, 8, 1)); n[:, 0] = 16; n[:, 1] = 9; n[:, 2] = 8; n[:, 7] = 0
    d["th"] = np.where(np.argsort(rng.random((N, 8, 16)), axis=-1) < n, Q, Q * (1 + SW))
    slots = [np.concatenate([np.array([0, E - 1]), 1 + rng.permutation(E - 2)[:8 * RO - 2]]) for j in range(4)]
    top = np.concatenate([4 * np.array([0, 1, V // 4 - 2, V // 4 - 1]) + 3 - t for t in range(RO)])
    b = 4 * np.arange(V // 4); inner = b[(4 * b >= E // 2) & (4 * b + 3 < 4 * V - (E - E // 2))]
    for q in range(N):
        for g in range(8):
            at = slots[(g - 1) // 2]; S = []; C = []; T = []; hold = []; i = 0; k = 4 * RO
            if g % 2:
                more = rng.permutation(b); feed = (4 * top[:, None] + np.arange(2)).reshape(-1); F = feed + 2; T.append(top); hold.append(four_of(top))
            else:
                more = rng.permutation(inner); feed = 4 * V + at; F = np.concatenate([np.arange(E // 2), np.arange(4 * V - (E - E // 2), 4 * V)])
            for j in range(SW):
                nxt = more[i:i + k]; i += k; k *= 2
                S.append((4 * nxt[:, None] + np.arange(2)).reshape(-1)); C.append(feed); feed = four_of(nxt)
                T.append(nxt); hold.append((4 * nxt[:, None] + np.arange(2, 4)).reshape(-1))
            T = np.concatenate(T); hold = np.concatenate(hold); leak = more[i:i + len(hold) // 4]
            S.append(hold); C.append(four_of(leak))
            d["sg"][q, g], d["xp"][q, g] = lay(rng, np.concatenate(S), np.concatenate(C), F, at if g % 2 else None)
            d["cash"][q, g][:, T] = 0; d["debt"][q, g][:, T] = 1023; d["coll"][q, g][:, four_of(T)] = 0; d["val"][q, g][:, T] = 128.0
            d["cash"][q, g][:, leak] = 0; d["debt"][q, g][:, leak] = 1
    return pack(d)
def setup_inputs_corners(rng):
    d = base(rng, 600); d["debt"] = d["debt"] & -4
    d["val"] = ((2 ** 16 + rng.integers(0, 2 ** 14, (N, 8, 16, V)) + 0.4921875) * 2.0 ** -20).astype(np.float32)
    d["th"][:] = Q; d["th"][:, 3::4] = Q * (1 + SW)
    for q in range(N):
        for g in range(8):
            cash, debt, coll = d["cash"][q, g], d["debt"][q, g], d["coll"][q, g]
            S = []; C = []; F = []; vs = []; h = 4 * rng.permutation(V // 4)
            for t in range(RO):
                i = np.sort(np.concatenate([np.array([0]), 1 + rng.permutation(V // 4 - 2)[:10], np.array([V // 4 - 1])]))
                v = 4 * i + 3 - t; u = h[8 * t:8 * t + 8]; vs.append(v)
                S += [4 * v[1] + 1, 4 * v[2] + 1, 4 * u[0] + 2, 4 * u[1], 4 * u[1] + 3, 4 * v[5] + 2, 4 * u[2] + 1, 4 * u[3] + 1, 4 * u[4] + 1, 4 * u[5] + 1, 4 * v[9] + 3 if g % 2 == 0 else 4 * u[6]]
                C += [4 * v[j] for j in (0, 1, 2, 3, 4, 5, 7, 8, 9, 10, 11)]; F.append(4 * v[6])
            o1, o2, leak = h[32], h[33], h[34]
            S += [4 * o1 + j for j in range(4)] + [4 * o2 + j for j in range(4)]
            C += [4 * o1, 4 * o1 + 1, 4 * o1 + 2, 4 * leak, 4 * o2, 4 * o2 + 1, 4 * o2 + 2, 4 * o1 + 3]
            d["sg"][q, g], d["xp"][q, g] = lay(rng, S, C, F)
            if g % 2:
                s = d["sg"][q, g]; own = np.flatnonzero((s < 4 * V) & (rng.random(4 * V) < 0.25))
                coll[:, own] = (debt[:, s[own] >> 2] >> 2) - rng.integers(0, 2, (16, len(own)))
            for v in vs:
                cash[:, v] = 0; debt[:, v] = 1023
                cash[rng.permutation(16)[:8], v[7]] = 1023; cash[rng.permutation(16)[:7], v[8]] = 1023
                coll[:, 4 * v[9] + np.arange(4)] = 200; coll[:, 4 * v[10] + np.arange(4)] = np.array([0, 0, 0, 200])
            b = h[24:32]; c = rng.integers(0, 21, (16, 8))
            cash[:, b] = c; debt[:, b] = 800 + c + rng.integers(0, 2, (16, 8)); coll[:, four_of(b)] = 200
            cash[:, h[32:35]] = 0; debt[:, h[32:34]] = 1023; debt[:, leak] = 1; coll[:, four_of(h[32:34])] = 0
    return pack(d)
def setup_inputs_crowd(rng):
    d = base(rng, 600); d["th"][:] = Q; d["th"][:, 3] = Q + rng.integers(0, Q // 4 + 1, (N, 16)); n = V // 32
    for q in range(N):
        for g in range(8):
            cash, debt, coll = d["cash"][q, g], d["debt"][q, g], d["coll"][q, g]; h = 4 * rng.permutation(V // 4); S = []; C = []; lane = rng.permutation(16)
            for t in range(RO):
                v = 4 * rng.permutation(V // 4)[:4 * n] + 3 - t; w = h[t * n:(t + 1) * n]
                S.append(four_of(w)); C.append(4 * v)
                cash[:, v] = 0; debt[:, v] = 1023
                coll[:, 4 * v] = 0; coll[:, 4 * v + 1] = 200; coll[:, 4 * v + 2] = 200; coll[:, 4 * v + 3] = 0; coll[lane[0], 4 * v + 1] = 0
                if g % 2: cash[lane[1], v] = 1023
                cash[:, v.reshape(n, 4)[::2, 3]] = 1023
            d["sg"][q, g], d["xp"][q, g] = lay(rng, np.concatenate(S), np.concatenate(C), [])
    return pack(d)
def setup_inputs_calm(rng):
    d = base(rng, 600)
    n = 9 + rng.integers(0, 8, (N, 8, 1)); d["th"] = np.where(np.argsort(rng.random((N, 8, 16)), axis=-1) < n, Q, Q + rng.integers(0, SW * Q + 1, (N, 8, 16)))
    for q in range(N):
        for g in range(8):
            cash, debt, coll = d["cash"][q, g], d["debt"][q, g], d["coll"][q, g]; h = 4 * rng.permutation(V // 4); S = []; C = []; at = 0
            for t in range(RO):
                k = (g + q + t) % 4 if g < 6 else (0 if t < RO - 1 else V // 4 - (g - 6))
                i = 4 * rng.permutation(V // 4) + 3 - t; v = i[:k]; rest = i[k:]; w = h[at:at + k]; at += k
                m = np.argsort(rng.random((16, len(rest))), axis=0) < 8
                cash[:, rest] = np.where(m, 1023, cash[:, rest])
                c = rng.integers(0, 21, (16, k)); cash[:, v] = c; debt[:, v] = 800 + c + CAP + rng.integers(0, 2, (16, k)); coll[:, four_of(v)] = 200
                S += [4 * w + 3, 4 * v + 1, 4 * v + 2]; C += [4 * v, 4 * w + 1, 4 * w + 2]
                if g >= 6 and t == RO - 1:
                    z = np.concatenate([4 * v, 4 * w])[:E]; S.append(z); C.append(4 * V + rng.permutation(E)[:len(z)])
            d["sg"][q, g], d["xp"][q, g] = lay(rng, np.concatenate(S), np.concatenate(C), [])
    return pack(d)
def check_ranges(d):
    bad = []
    for k, lo, hi in (("cash", 0, 1023), ("debt", 1, 1023), ("coll", 0, 255), ("sig", 0, 4 * V + E - 1), ("xpt", 0, 4 * V - 1), ("th", Q, Q * (1 + SW))):
        a = np.asarray(d[k]).astype(np.float64)
        if not (np.min(a) >= lo and np.max(a) <= hi): bad.append("range of " + k)
        elif np.any(a != np.floor(a)): bad.append("whole numbers of " + k)
    x = np.asarray(d["val"]).astype(np.float64)
    if not (np.min(x) >= 2.0 ** -4 and np.max(x) <= 128): bad.append("range of val")
    elif np.max(x) > 16 * np.min(x): bad.append("uneven sizes of val")
    for q in range(N):
        both = np.sort(np.concatenate([gentries(np.asarray(d["sig"][q])), gentries(np.asarray(d["xpt"][q]))], axis=1), axis=1)
        if np.any(both != np.arange(4 * V + E)[None, :]): bad.append("sig and xpt of rank " + str(q) + " are not every number once")
    return bad
def take(a, i):
    return np.take_along_axis(a, i[:, :, None, :], 3)
def four(y):
    return ((y[..., 0::4] + y[..., 1::4]) + y[..., 2::4]) + y[..., 3::4]
def forth(a):
    out = np.empty_like(a)
    for q in range(N):
        for d in range(1, N):
            b = slice((d - 1) * X, d * X); out[(q + d) % N, :, :, b] = np.roll(a[q, :, :, b], 1, axis=0)
    return out
def home(a):
    out = np.empty_like(a)
    for q in range(N):
        for d in range(1, N):
            b = slice((d - 1) * X, d * X); out[q, :, :, b] = np.roll(a[(q + d) % N, :, :, b], -1, axis=0)
    return out
def clear(e, L, c, sg, xp):
    at = np.where(sg < 4 * V, sg >> 2, sg - 3 * V); p = L
    for k in range(SW):
        y = np.maximum(0.25 * take(np.concatenate([p, forth(take(p, xp >> 2))], axis=3), at), c)
        p = np.minimum(L, e + four(y))
    return p, p < L, y > c
def inverse(sg, xp):
    inv = np.zeros((N, 8, 4 * V + E), np.int64)
    np.put_along_axis(inv, sg, np.arange(4 * V)[None, None, :], 2); np.put_along_axis(inv, xp, 4 * V + np.arange(E)[None, None, :], 2)
    return inv
def threat(D, M, inv, a):
    m = np.where(D, a, 0.0)
    for k in range(SW):
        c = np.where(M, np.repeat(m, 4, axis=3), 0.0)
        z = take(np.concatenate([c, home(take(c, inv[:, :, 4 * V:]))], axis=3), inv[:, :, :4 * V])
        m = np.where(D, a + 0.25 * four(z), 0.0)
    return m
def novate(t, m, M, e, sg, inv, lim):
    v = np.arange(3 - t, V, 4); votes = np.sum(Q * m[..., v] >= lim, axis=2)
    s = inv[:, :, 4 * v]; w = s >> 2; act = (votes >= 9) & (s < 4 * V) & (w != v)
    k = np.argmax(np.sum(~M.reshape(N, 8, 16, V, 4)[:, :, :, v], axis=2), axis=3)
    low = np.full((N, 8, V), V, np.int64); r, g, i = np.nonzero(act)
    low[r, g, v[i]] = v[i]; np.minimum.at(low, (r, g, w[r, g, i]), v[i])
    ok = (low[r, g, v[i]] == v[i]) & (low[r, g, w[r, g, i]] == v[i])
    r, g, i = r[ok], g[ok], i[ok]; e = np.array(e); sg = np.array(sg)
    e[r, g, :, v[i]] += CAP
    a = 4 * v[i] + k[r, g, i]; b = 4 * w[r, g, i] + k[r, g, i]
    sg[r, g, a], sg[r, g, b] = sg[r, g, b], sg[r, g, a]
    return e, sg
def reference(cash, debt, coll, sig, xpt, th, val):
    e = cash.astype(np.float64).reshape(N, 8, 16, V); L = debt.astype(np.float64).reshape(N, 8, 16, V)
    c = coll.astype(np.float32).astype(np.float64).reshape(N, 8, 16, 4 * V); lim = th.astype(np.float64).reshape(N, 8, 16, 1)
    sg = np.stack([gentries(a) for a in sig]).astype(np.int64); xp = np.stack([gentries(a) for a in xpt]).astype(np.int64)
    for t in range(RO):
        p, D, M = clear(e, L, c, sg, xp); inv = inverse(sg, xp)
        e, sg = novate(t, threat(D, M, inv, 1.0), M, e, sg, inv, lim)
    p, D, M = clear(e, L, c, sg, xp)
    m = threat(D, M, inverse(sg, xp), val.astype(np.float64).reshape(N, 8, 16, V))
    return {"pay": p.reshape(N, 128, V).astype(np.float32), "mu": m.reshape(N, 128, V).astype(np.float32)}

def check_inputs(d):
    bad = list(check_ranges(d))
    if not bad:
        for name, y in reference(**d).items():
            for q in range(N):
                v = np.abs(np.asarray(y[q], np.float64)); s = np.sqrt(np.mean(v * v))
                if v.max() > 7 * s or s < 2.0 ** -5: bad.append('%s of rank %d is uneven or too small' % (name, q))
    return bad

@@ -1,0 +1,845 @@
+import math
+from concourse.bass import DstId, RemoteDMATransfer
+from concourse.mybir import AluOpType as ALU, ActivationFunctionType as AF
+
+V, X, E, NC, NX, NA = 896, 128, 384, 3584, 3968, 224
+RO = 2
+DM = 448
+F32, BF, F16, I32, U16 = "float32", "bfloat16", "float16", "int32", "uint16"
+XDT = [F16] + [F16, F32, BF, BF, BF] * RO + [F16, F32, F32, F32, F32]
+
+_SB = {
+    "sigI": (248, I32), "lstU": (248, U16), "sigO": (224, U16), "atO": (224, U16), "xbU": (24, U16),
+    "invO": (248, U16), "wbU": (24, U16), "ta": (256, I32), "tb": (224, I32),
+    "debtI": (V, I32), "cashI": (V, I32), "thI": (1, I32), "thr": (1, F32), "colS": (NC, BF), "valS": (V, F32),
+    "Lq": (V + E, F32), "e16": (V, F16), "LB": (V, F32), "cm": (NX, BF),
+    "S14": (NA + V + E, F32), "q1": (V + E, F32), "q2": (V, F32), "y16": (NC, F16), "W": (NX, F32), "R": (NC, F32),
+    "rw": (E, F32), "Db": (V, BF), "C0b": (NX, BF), "Zb1": (NC, BF),
+    "mb1": (V, BF), "mb2": (V + E, BF), "Cf": (NX, F32), "Zf": (NC, F32),
+    "vinit": (NX, BF), "invT": (DM + NX, BF), "sigT": (DM + NX, BF), "cp": (DM + NX, BF),
+    "ioA": (128, I32), "ioC": (256, F32), "tf": (256, F32), "tc": (128, I32), "pI": (1, I32), "pJ": (2, I32), "OH": (16, F32),
+    "col": (24, F32), "Ib": (128, BF), "nIb": (128, BF), "qIb": (128, BF), "sIb": (128, BF), "qIh": (128, F16), "nIh": (128, F16),
+    "If": (128, F32), "nIf": (128, F32), "aIf": (128, F32), "bIf": (128, F32), "Fh": (128, F16), "Ff": (128, F32),
+    "Bb": (128, BF), "Bf": (128, F32), "mats": (6 * 144 + 256, BF), "one": (512, BF), "c01": (16, BF), "blkT": (256, BF),
+    "mIb": (128, BF), "cIb": (128, BF), "dIb": (128, BF), "i9": (126, F32), "iB": (14, BF), "kc": (56, F32), "kk": (126, F32),
+    "MA": (V, BF), "mk": (V, BF), "z3": (V, BF), "aU": (56, U16), "vF": (28, F32), "ne": (14, F32),
+    "kI": (56, I32), "n1": (126, F32), "n2": (126, F32), "cU": (126, U16), "wU": (14, U16), "vdU": (14, U16),
+    "g4U": (56, U16), "rF": (28, F32), "rU": (28, U16), "sU": (28, U16), "lU": (28, U16),
+    "vS": (DM, BF), "vN": (DM, BF), "vC": (DM, BF),
+    "vdR": (NA, BF), "vote": (NA, BF), "actW": (240, BF), "okF": (V, BF),
+    "xw": (14, F32), "xx": (56, F32), "o1": (14, F32), "o4": (56, F32), "owU": (14, U16), "oU": (56, U16),
+}
+ALIAS = {"C1b": ("vinit", 0, NX), "Zb2": ("colS", 0, NC), "cg": ("colS", 0, 9 * NA), "gw": ("z3", 0, V), "mf": ("q2", 0, V),
+         "vL": ("Zf", 0, DM), "yn": ("Zf", DM, DM), "dv": ("Zf", 2 * DM, NA), "nw": ("Zf", 2 * DM + NA, NA),
+         "val14": ("S14", NA, V), "Lf": ("Cf", 0, V), "pO": ("q1", 0, V), "vw": ("q1", V, E), "nM": ("mb2", 0, V),
+         "EX": ("mats", 0, 144), "EE": ("mats", 144, 144), "EW": ("mats", 288, 144), "KI": ("mats", 432, 144), "KS": ("mats", 576, 144),
+         "E4": ("mats", 720, 144), "NE": ("mats", 864, 128), "blk": ("mats", 992, 128)}
+for _d, _s in ((F16, "h"), (F32, "f"), (BF, "b")):
+    _k = [i for i, d in enumerate(XDT) if d == _d]
+    _SB["snd" + _s] = (E * len(_k), _d)
+    _SB["lnd" + _s] = (E * len(_k), _d)
+    for _j, _i in enumerate(_k):
+        ALIAS["snd%d" % _i] = ("snd" + _s, E * _j, E)
+        ALIAS["lnd%d" % _i] = ("lnd" + _s, E * _j, E)
+SCRATCH = {k: ("sbuf", [128, n], d) for k, (n, d) in _SB.items()}
+for _i in range(8):
+    SCRATCH["P%d" % _i] = ("psum", [128, 512], F32)
+_DMAS = ["d%d" % i for i in range(10)]
+SEMAPHORES = ["sv", "ss", "sp", "sg", "sent"] + ["arr%d" % i for i in range(len(XDT))] + _DMAS
+
+HALF = ((0, 512), (512, V))
+CH32 = (("v", 0, 256), ("s", 256, 512), ("v", 512, 1024), ("s", 1024, 1536), ("v", 1536, 2048), ("s", 2048, 2560), ("v", 2560, 2816),
+        ("s", 2816, 3328), ("s", 3328, NC))
+CH16 = (("v", 0, 1024), ("s", 1024, 2048), ("v", 2048, 2560), ("s", 2560, 3072), ("v", 3072, 3328), ("s", 3328, NC))
+SIDE3 = ((("P4",), ("P5",)), (("P4", "P5"), ("P6",)))
+PIECE = 32
+COST = dict(gather=1.56, scatter=3.8, pe=0.5, flight=3500.0, hop=80.0, call=60.0)
+ROUNDS = 6
+TRIES = 500
+
+
+def A(name, a=0, b=None, step=1):
+    off = 0
+    if name in ALIAS:
+        name, off, n = ALIAS[name]
+    else:
+        n = SCRATCH[name][1][1]
+    return ("ap", name, off + a, off + (n if b is None else b), step)
+
+
+def IND(win, off):
+    return ("ind", win, off)
+
+
+def build():
+    ops = []
+
+    def span(x):
+        if isinstance(x, tuple) and x[0] == "ap":
+            return [(x[1], x[2], x[3], x[4])]
+        if isinstance(x, tuple) and x[0] == "ind":
+            return span(x[1])
+        return []
+
+    def offs(x):
+        return span(x[2]) if isinstance(x, tuple) and x[0] == "ind" else []
+
+    def put(q, kind, out, ins, args):
+        rd = offs(out)
+        for x in ins:
+            rd = rd + span(x) + offs(x)
+        ops.append((q, kind, args, rd, span(out)))
+
+    def cpy(out, x):
+        put("v", "copy", out, [x], (out, x))
+
+    def ts(out, x, s1, op0, s2=None, op1=None):
+        put("v", "ts", out, [x, s1, s2], (out, x, s1, s2, op0, op1))
+
+    def tt(out, x, y, op):
+        put("v", "tt", out, [x, y], (out, x, y, op))
+
+    def act(out, x, func=AF.Identity, bias=0.0, scale=1.0):
+        put("s", "act", out, [x, bias, scale], (out, x, func, bias, scale))
+
+    def mm(out, w, x, start, stop, line=None):
+        put("p", "mm", out, [w, x], (out, w, x, start, stop, line))
+
+    def fill(out, c):
+        put("v", "fill", out, [], (out, c))
+
+    def iota(out, pat, base, cm):
+        put("g", "iota", out, [], (out, pat, base, cm))
+
+    def select(out, pat, op, c, base, cm):
+        put("g", "sel", out, [out], (out, pat, op, c, base, cm))
+
+    nd = [0]
+
+    def dma(q, out, x):
+        put(q, "dma", out, [x], (out, x, _DMAS[nd[0]]))
+        nd[0] += 1
+
+    nx = [0]
+
+    def snd():
+        return "snd%d" % nx[0]
+
+    def send(back):
+        put("g", "send", None, [A(snd())], (nx[0], back))
+        nx[0] += 1
+        return nx[0] - 1
+
+    def export(win, lst):
+        cpy(A(snd(), 0, 192), IND(win, A(lst, 0, 12)))
+        act(A(snd(), 192, E), IND(win, A(lst, 12, 24)))
+
+    def turn(n, w):
+        ops.append(("p", "arrive", (n,), [], span(A("lnd%d" % n))))
+        mm(A("P7", 0, E), A(w), A("lnd%d" % n), True, True)
+        return A("P7", 0, E)
+
+    def extract(out, w, tab, first, n, step, start=True, stop=True):
+        for r in range(16):
+            f = first(r)
+            mm(out, A(w, 15 - r, 143 - r), A(tab, f, f + step * (n - 1) + 1, step), start and r == 0, stop and r == 15)
+
+    def pb(banks, lo, hi):
+        h = 0 if lo < 512 else 1
+        return A(banks[h], lo - 512 * h, hi - 512 * h)
+
+    def col(j):
+        return A("col", j, j + 1)
+
+    def oh(j):
+        return A("OH", j, j + 1)
+
+    dma("y", A("sigI", 224, 248), ("in", "xpt"))
+    dma("s", A("debtI"), ("in", "debt"))
+    dma("y", A("sigI", 0, 224), ("in", "sig"))
+    dma("s", A("colS"), ("in", "coll"))
+    dma("y", A("cashI"), ("in", "cash"))
+    dma("y", A("thI"), ("in", "th"))
+    dma("y", A("valS"), ("in", "val"))
+    iota(A("pI"), [[0, 1]], 0, 1)
+    iota(A("ioC"), [[1, 256]], 0, 0)
+    iota(A("ioA"), [[1, 128]], 0, -1)
+    fill(A("mats", 0, 992), 0.0)
+    fill(A("invT", 0, DM), 0.0)
+    ts(A("pJ", 0, 1), A("pI"), 15, ALU.bitwise_and)
+    cpy(col(0), A("pJ", 0, 1))
+    ts(A("OH"), A("ioC", 0, 16), col(0), ALU.is_equal)
+    act(col(1), oh(2), bias=oh(1), scale=1.0 / 16)
+    act(col(4), oh(0), bias=oh(4))
+    act(col(2), oh(3), bias=col(1), scale=1.0 / 16)
+    act(col(5), col(4), scale=2.0)
+    act(col(1), oh(5), bias=col(2), scale=0.25)
+    act(col(6), col(4), scale=4.0)
+    act(col(2), oh(7), bias=col(1), scale=0.25)
+    act(col(7), col(4), scale=8.0)
+    act(col(3), col(2), bias=-0.5, scale=0.5)
+    ts(A("tc"), A("ioA"), 112, ALU.add)
+    ts(A("Ib"), A("ioA"), 0, ALU.is_equal)
+    ts(A("tc"), A("tc"), 127, ALU.bitwise_and)
+    ts(A("qIh"), A("ioA"), 0, ALU.is_equal, 0.25, ALU.mult)
+    ts(A("Fh"), A("tc"), 0, ALU.is_equal)
+    ts(A("nIh"), A("ioA"), 0, ALU.is_equal, -1.0, ALU.mult)
+    ts(A("ta", 0, 24), A("sigI", 224, 248), 2, ALU.arith_shift_right)
+    cpy(A("xbU"), A("ta", 0, 24))
+    ts(A(snd()), IND(A("debtI"), A("xbU")), 0.25, ALU.mult, -128.0, ALU.add)
+    x0 = send(False)
+    ts(A("tf"), A("ioC"), col(2), ALU.mult, col(3), ALU.add)
+    cpy(A("lstU"), A("sigI"))
+    cpy(A("ta"), A("tf"))
+    ts(A("Lq", 0, V), A("debtI"), 0.25, ALU.mult, -128.0, ALU.add)
+    cpy(A("vinit", 0, 256), A("ta"))
+    ts(A("tb"), A("sigI", 0, 224), -3 * V, ALU.add)
+    act(A("vinit", 256, 512), A("vinit", 0, 256), bias=col(4))
+    ts(A("ta", 0, 224), A("sigI", 0, 224), 2, ALU.arith_shift_right)
+    act(A("vinit", 512, 1024), A("vinit", 0, 512), bias=col(5))
+    tt(A("ta", 0, 224), A("ta", 0, 224), A("tb"), ALU.max)
+    act(A("cm", 1024, NC), A("colS", 1024, NC), bias=-128.0)
+    cpy(A("atO"), A("ta", 0, 224))
+    cpy(A("e16"), A("cashI"))
+    act(A("cm", 0, 1024), A("colS", 0, 1024), bias=-128.0)
+    act(A("vinit", 1024, 2048), A("vinit", 0, 1024), bias=col(6))
+    act(col(8), oh(7), bias=col(2), scale=0.75)
+    act(col(9), col(8), bias=-0.5, scale=0.5)
+    act(col(10), col(4), bias=oh(6), scale=14.0)
+    act(col(12), oh(4), bias=col(10), scale=4.0)
+    act(col(11), oh(0), bias=col(12))
+    act(A("tf"), A("ioC"), bias=col(9), scale=col(8))
+    act(A("vinit", 2048, NC), A("vinit", 0, NC - 2048), bias=col(7))
+    cpy(A("ta"), A("tf"))
+    cpy(A("blkT"), A("ta"))
+    act(A("vinit", NC, NC + 256), A("blkT"), bias=col(10))
+    act(A("vinit", NC + 256, NX), A("blkT", 0, 128), bias=col(11))
+    for c in range(0, 248, PIECE):
+        cpy(IND(A("invT", DM, DM + NX), A("lstU", c, min(c + PIECE, 248))), A("vinit", 16 * c, 16 * min(c + PIECE, 248)))
+    for c in range(0, 224, 56):
+        act(A("sigT", DM + 16 * c, DM + 16 * c + V), IND(A("vinit"), A("lstU", c, c + 56)))
+    act(A("Lf"), A("Lq", 0, V), bias=512.0, scale=4.0)
+    act(A("nIb"), A("Ib"), scale=-1.0)
+    act(A("cm", NC, NX), A("cm", 0, E), scale=0.0)
+    for h, (lo, hi) in enumerate(HALF):
+        o = A("P%d" % (2 + h), 0, hi - lo)
+        mm(o, A("nIh"), A("e16", lo, hi), True, False)
+        for k in range(4):
+            mm(o, A("nIb"), A("colS", 4 * lo + k, 4 * hi, 4), False, k == 3)
+        tt(A("LB", lo, hi), o, A("Lf", lo, hi), ALU.add)
+    fill(A("mats", 992, 1120), 1.0)
+    for w, rows in (("EX", ((0, 256), (1, 1))), ("EE", ((4, 64), (7, 1))), ("EW", ((0, 256), (5, 4))),
+                    ("KI", ((0, 16), (2, 1), (3, -4096), (5, 1024))), ("KS", ((0, 16), (1, 256), (2, 1), (3, -4096)))):
+        for r, c in rows:
+            select(A(w, 15, 143, 16), [[-16, 8]], ALU.not_equal, float(c), -r, 1)
+    select(A("NE"), [[-16, 8], [0, 16]], ALU.not_equal, -64.0, -6, 1)
+    select(A("blk"), [[-16, 8], [0, 16]], ALU.is_ge, 0.0, 0, 1)
+    select(A("blk"), [[16, 8], [0, 16]], ALU.is_ge, 0.0, 15, -1)
+    iota(A("i9", 0, 112), [[0, 2], [4, 56]], 0, 0)
+    iota(A("i9", 112, 126), [[16, 14]], 0, 0)
+    iota(A("kc"), [[1, 4], [0, 14]], 0, 0)
+
+    def load_cm():
+        for c in range(5):
+            mm(A("P%d" % (2 + c)), A("Ib"), A("cm", 1024 + 512 * c, 1536 + 512 * c), True, True)
+
+    def claim_sweep(win, out, acted):
+        def total(c):
+            o = pb(("P0", "P1"), 128 * c, 128 * c + 128)
+            mm(o, A("qIh"), A("e16", 128 * c, 128 * c + 128), True, False)
+            if acted:
+                mm(o, A("cIb"), A("okF", 128 * c, 128 * c + 128), False, False)
+            for k in range(4):
+                mm(o, A("qIh"), A("y16", 512 * c + k, 512 * c + 512, 4), False, k == 3)
+
+        def top(c):
+            tt(A("y16", 512 * c, 512 * c + 512), A("Zf", 512 * c, 512 * c + 512), A("P%d" % c), ALU.max)
+            total(c)
+
+        tt(A("y16", 0, 1024), IND(win, A("atO", 0, 64)), A("cm", 0, 1024), ALU.max)
+        for c in range(2, 7):
+            act(A("Zf", 512 * c, 512 * c + 512), IND(win, A("atO", 32 * c, 32 * c + 32)))
+        total(0)
+        total(1)
+        top(2)
+        top(3)
+        top(4)
+        tt(A(out, 0, 512), A("P0"), A("Lq", 0, 512), ALU.min)
+        top(5)
+        top(6)
+        tt(A(out, 512, V), A("P1", 0, V - 512), A("Lq", 512, V), ALU.min)
+
+    def gather32(win, lst, out, scale, relu, banks, w, after):
+        for q, lo, hi in CH32:
+            src = IND(win, A(lst, lo // 16, hi // 16))
+            if q == "v":
+                if relu:
+                    ts(A(out, lo, hi), src, scale, ALU.mult, 0.0, ALU.max)
+                else:
+                    ts(A(out, lo, hi), src, scale, ALU.mult)
+            else:
+                act(A(out, lo, hi), src, AF.Relu if relu else AF.Identity, scale=scale)
+            for k in range(2):
+                mm(pb(banks, lo // 4, hi // 4), A(w), A(out, lo + k, hi, 4), False, k == 1 and hi in (2048, NC), "sum")
+        after(0)
+        after(1)
+
+    def gather16(win, out, banks, mout):
+        for q, lo, hi in CH16:
+            src = IND(win, A("invO", lo // 16, hi // 16))
+            if q == "v":
+                cpy(A(out, lo, hi), src)
+            else:
+                act(A(out, lo, hi), src)
+        for q, lo, hi in CH16:
+            for k in range(4):
+                mm(pb(banks, lo // 4, hi // 4), A("qIb"), A(out, lo + k, hi, 4), False, k == 3 and hi in (2048, NC), "sum")
+        cpy(A(mout, 0, 512), A(banks[0]))
+        act(A(mout, 512, V), A(banks[1], 0, V - 512))
+
+    def base(banks, w, x):
+        for h, (lo, hi) in enumerate(HALF):
+            mm(A(banks[h], 0, hi - lo), A(w), A(x, lo, hi) if x != "one" else A(x, 0, hi - lo), True, False)
+
+    def spread(out, other, off, banks, op, side=None):
+        for h, (lo, hi) in enumerate(HALF):
+            cut = 4 - len(side[0][h]) if side else 4
+            for k in range(cut):
+                tt(A(out, 4 * lo + k, 4 * hi, 4), A(banks[h], 0, hi - lo), A(other, off + 4 * lo + k, off + 4 * hi, 4), op)
+            for k in range(cut, 4):
+                o = A(side[0][h][k - cut], 0, hi - lo)
+                for j, (w, x, wide) in enumerate(side[1]):
+                    src = A(x, wide[0] + 4 * lo + k, wide[0] + 4 * hi, 4) if wide else A(x, lo, hi)
+                    mm(o, A(w), src, j == 0, j == len(side[1]) - 1)
+                act(A(out, 4 * lo + k, 4 * hi, 4), o, side[2], bias=side[3])
+
+    def inverse_lists(bank):
+        extract(A(bank, 256, 280), "EE", "invT", lambda r: DM + NC + r, 24, 16)
+        cpy(A("wbU"), A(bank, 256, 280))
+        extract(A(bank, 0, 248), "EX", "invT", lambda r: DM + r, 248, 16)
+        cpy(A("invO"), A(bank, 0, 248))
+
+    load_cm()
+    act(A("Lq", V, V + E), turn(x0, "Fh"))
+    claim_sweep(A("Lq"), "q1", False)
+    cpy(A(snd()), IND(A("q1", 0, V), A("xbU")))
+    x1 = send(False)
+    act(A("S14", NA, NA + 512), A("P0"))
+    act(A("S14", NA + 512, NA + V), A("P1", 0, V - 512))
+    cpy(A("sigO"), A("sigI", 0, 224))
+    cpy(A("Ff"), A("Fh"))
+    act(A("aIf"), A("Ib"), scale=64.0)
+    act(A("nIf"), A("Ib"), scale=-1.0)
+    act(A("If"), A("Ib"))
+
+    for t in range(RO + 1):
+        close = t == RO
+        r0 = 4 * (3 - t)
+        act(A("q1", V, V + E), turn(x1, "Fh"))
+        if t == 0:
+            inverse_lists("P7")
+            for c in range(0, 248, 62):
+                act(A("cp", DM + 16 * c, DM + 16 * c + 992), IND(A("cm"), A("invO", c, c + 62)))
+        else:
+            extract(A("P7", 0, 224), "EX", "sigT", lambda r: DM + r, 224, 16)
+            cpy(A("sigO"), A("P7", 0, 224))
+        claim_sweep(A("q1"), "q2", t > 0)
+        export(A("q2"), "xbU")
+        x2 = send(False)
+        for h, (lo, hi) in enumerate(HALF):
+            act(A("P%d" % h, 0, hi - lo), A("q2", lo, hi))
+        if close:
+            act(A("val14"), A("valS"), scale=2.0 ** 14)
+            act(A("bIf"), A("Ib"), scale=2.0 ** 27)
+            act(A("mIb"), A("Ib"), scale=-2.0 ** 22)
+            act(A("Bf"), A("Bb"))
+            act(A("pO"), A("Lq", 0, V), bias=512.0, scale=4.0)
+        base(("P2", "P3"), "bIf" if close else "aIf", "LB")
+        if t > 0:
+            act(A("dIb"), A("Ib"), scale=-0.375 * (2.0 ** 27 if close else 64.0))
+            for h, (lo, hi) in enumerate(HALF):
+                mm(A("P%d" % (2 + h), 0, hi - lo), A("dIb"), A("okF", lo, hi), False, False)
+        spread("W", "cp", DM, ("P0", "P1"), ALU.subtract, (SIDE3[min(t, 1)], (("If", "q2", None), ("nIb", "cp", (DM,))), AF.Identity, 0.0))
+        if t > 0:
+            inverse_lists("P6")
+        tt(A("W", NC, NX), turn(x2, "Ff"), A("cp", DM + NC, DM + NX), ALU.subtract)
+        scale = 2.0 ** 27 if close else 64.0
+
+        def shortfall(h):
+            lo, hi = HALF[h]
+            o = A("P%d" % (2 + h), 0, hi - lo)
+            if h == 0:
+                act(A("rw"), A("W", NC, NX), AF.Relu, scale=scale)
+            tt(o, o, A("R", 4 * lo + 2, 4 * hi, 4), ALU.subtract)
+            tt(A("Db", lo, hi), o, A("R", 4 * lo + 3, 4 * hi, 4), ALU.is_gt)
+            if h == 0 and close:
+                tt(A("vw"), IND(A("val14"), A("wbU")), A("rw"), ALU.min)
+
+        gather32(A("W"), "sigO", "R", scale, True, ("P2", "P3"), "nIf", shortfall)
+        if close:
+            tt(A(snd()), IND(A("Db"), A("wbU")), A("vw"), ALU.mult)
+        else:
+            tt(A(snd()), IND(A("Db"), A("wbU")), A("rw"), ALU.min)
+        x3 = send(True)
+        for h, (lo, hi) in enumerate(HALF):
+            mm(A("P%d" % h, 0, hi - lo), A("Ib"), A("Db", lo, hi), True, True)
+
+        if close:
+            for h, (lo, hi) in enumerate(HALF):
+                o = A("P%d" % h, 0, hi - lo)
+                tt(o, o, A("val14", lo, hi), ALU.mult)
+            base(("P4", "P5"), "If", "valS")
+            spread("Cf", "R", 0, ("P0", "P1"), ALU.min)
+            act(A("nM"), A("Cf", 3, NC, 4), AF.Relu, bias=1.0, scale=-1.0)
+            act(A("Cf", NC, NX), turn(x3, "Bf"))
+            win = "Cf"
+            banks = ("P4", "P5")
+            for sw in range(3):
+                def rest(h):
+                    lo, hi = HALF[h]
+                    o = A(banks[h], 0, hi - lo)
+                    tt(o, o, A("Zf", 4 * lo + 2, 4 * hi, 4), ALU.add)
+                    if sw < 2:
+                        tt(A("mf", lo, hi), o, A("Zf", 4 * lo + 3, 4 * hi, 4), ALU.add)
+                    else:
+                        tt(o, o, A("Zf", 4 * lo + 3, 4 * hi, 4), ALU.add)
+                        tt(A("mf", lo, hi), o, A("Db", lo, hi), ALU.mult)
+                        dma("y" if h == 0 else "s", ("out", "mu", lo, hi), A("mf", lo, hi))
+
+                gather32(A(win), "invO", "Zf", 2.0 ** -16 if sw == 0 else 0.25, False, banks, "If", rest)
+                if sw == 2:
+                    break
+                act(A(banks[0]), A("mf", 0, 512))
+                export(A("mf"), "wbU")
+                xm = send(True)
+                act(A(banks[1], 0, V - 512), A("mf", 512, V))
+                nxt = ("P0", "P1") if sw == 0 else ("P4", "P5")
+                base(nxt, "If", "valS")
+                spread("W", "Cf", 0, banks, ALU.min, ((("P6",), ("P7",)), (("If", "mf", None), ("mIb", "nM", None)), AF.Relu, 0.0))
+                for h, (lo, hi) in enumerate(HALF):
+                    o = A("P%d" % (2 + h), 0, hi - lo)
+                    if sw == 0:
+                        tt(o, o, A("R", 4 * lo + 3, 4 * hi, 4), ALU.subtract)
+                        act(o, o, AF.Relu, scale=2.0 ** -27)
+                    else:
+                        tt(A("pO", lo, hi), A("pO", lo, hi), o, ALU.subtract)
+                if sw == 1:
+                    dma("y", ("out", "pay", 0, V), A("pO"))
+                tt(A("W", NC, NX), turn(xm, "Bf"), A("Cf", NC, NX), ALU.min)
+                win = "W"
+                banks = nxt
+            break
+
+        if t == 0:
+            act(A("one"), A("cm", 0, 512), scale=0.0, bias=1.0)
+            act(A("qIb"), A("Ib"), scale=0.25)
+            act(A("E4", 15, 143, 16), A("blk", 0, 128, 16), scale=4.0)
+            ts(A("tc"), A("ioA"), 144, ALU.add)
+            ts(A("pJ", 0, 1), A("pI"), 2, ALU.arith_shift_right, 3, ALU.bitwise_and)
+            ts(A("pJ", 1, 2), A("pI"), 3, ALU.bitwise_and)
+            ts(A("tc"), A("tc"), 127, ALU.bitwise_and)
+            cpy(A("col", 13, 15), A("pJ"))
+            ts(A("Bb"), A("tc"), 0, ALU.is_equal)
+            ts(A("thr"), A("thI"), 1.0 / 64, ALU.mult, 15.0, ALU.add)
+        base(("P4", "P5"), "Ib", "one")
+        for k in range(4):
+            act(A("MA", NA * k, NA * k + NA), A("R", r0 + k, NC, 16), AF.Sign)
+        if t == 0:
+            act(A("i9", 0, 112), A("i9", 0, 112), bias=col(13))
+            act(A("i9", 112, 126), A("i9", 112, 126), bias=col(0))
+            act(A("iB"), A("i9", 112, 126))
+            act(col(15), col(14), bias=float(DM))
+            act(A("sIb"), A("Ib"), scale=16.0)
+            act(A("cp", 0, DM), A("cm", 0, DM), scale=0.0)
+            act(A("sigT", 0, DM), A("cm", 0, DM), scale=0.0)
+            act(A("sigT", DM + NC, DM + NX), A("cm", 0, E), scale=0.0)
+            act(A("S14", 0, NA), A("cm", 0, NA), scale=0.0)
+            act(A("S14", NA + V, NA + V + E), A("cm", 0, E), scale=0.0)
+            act(A("actW", 0, 16), A("cm", 0, 16), scale=0.0)
+            act(A("actW", NA, 240), A("cm", 0, 16), scale=0.0)
+            act(A("c01"), A("ioC", 0, 16))
+            act(A("okF"), A("cm", 0, V), scale=0.0)
+            act(A("cIb"), A("Ib"), scale=0.375 / 4)
+        act(A("vF", 0, 14), A("i9", 112, 126), bias=float(3 - t), scale=4.0)
+        act(A("vF", 14, 28), A("i9", 112, 126), bias=float(DM + r0), scale=16.0)
+        act(A("kk"), A("i9"), bias=float(1 - 256 * r0), scale=0.0)
+        act(A("nM"), A("R", 3, NC, 4), AF.Relu, bias=1.0, scale=-1.0)
+        spread("C0b", "R", 0, ("P0", "P1"), ALU.min, ((("P2",), ("P3",)), (("Ib", "Db", None), ("nIb", "nM", None)), AF.Relu, 0.0))
+        act(A("C0b", NC, NX), turn(x3, "Bb"))
+        port0 = lambda r: DM + 16 * r + r0
+        port4 = lambda r: DM + 16 * (r >> 2) + r0
+        ports = lambda r: DM + 16 * (r >> 2) + r0 + (r & 3)
+        extract(A("P6", 0, 56), "EW", "invT", port4, 56, 64)
+        extract(A("P6", 56, 70), "EE", "invT", port0, 14, 256)
+        gather16(A("C0b"), "Zb1", ("P4", "P5"), "mb1")
+        ts(A("g4U"), A("P6", 0, 56), col(15), ALU.add)
+        tt(A("ne"), A("P6", 56, 70), A("vF", 0, 14), ALU.not_equal)
+        ts(A("wU"), A("P6", 56, 70), NA, ALU.add)
+        ts(A("xw"), A("P6", 56, 70), NA, ALU.add)
+        cpy(A("vdU"), A("ne"))
+        export(A("mb1"), "wbU")
+        x4 = send(True)
+        base(("P0", "P1"), "Ib", "one")
+        extract(A("P3", 0, 56), "E4", "MA", lambda r: r, 56, 16)
+        extract(A("P3", 56, 70), "EW", "invT", port0, 14, 256)
+        extract(A("P3", 80, 136), "EE", "invT", ports, 56, 64)
+        act(A("gw"), IND(A("sigT"), A("g4U")))
+        act(A("vdR"), IND(A("c01"), A("vdU")))
+        for l in range(4):
+            act(A("mk", l, V, 4), A("Zb1", r0 + l, NC, 16))
+        spread("C1b", "C0b", 0, ("P4", "P5"), ALU.mult, ((("P2",), ("P7",)), (("Ib", "mb1", None), ("sIb", "C0b", (0,))), AF.Relu, -16.0))
+        tt(A("C1b", NC, NX), turn(x4, "Bb"), A("C0b", NC, NX), ALU.mult)
+        mm(A("P6", 0, 126), A("If"), A("kk"), True, False)
+        extract(A("P6", 0, 56), "KS", "sigT", ports, 56, 64, False, False)
+        gather16(A("C1b"), "Zb2", ("P0", "P1"), "mb2")
+        tt(A("kI"), A("P3", 0, 56), A("kc"), ALU.add)
+        tt(A("kI", 0, 28), A("kI", 0, 28), A("kI", 28, 56), ALU.min)
+        tt(A("kI", 0, 14), A("kI", 0, 14), A("kI", 14, 28), ALU.min)
+        ts(A("kI", 0, 14), A("kI", 0, 14), 3, ALU.bitwise_and)
+        export(A("mb2", 0, V), "wbU")
+        x5 = send(True)
+        ts(A("ne"), A("kI", 0, 14), DM, ALU.add)
+        tt(A("rF", 0, 14), A("kI", 0, 14), A("vF", 14, 28), ALU.add)
+        tt(A("rF", 14, 28), A("P3", 56, 70), A("ne"), ALU.add)
+        cpy(A("aU"), A("P3", 80, 136))
+        cpy(A("rU"), A("rF"))
+        act(A("vS"), IND(A("sigT"), A("rU")))
+        extract(A("P6", 56, 112), "KS", "gw", lambda r: r, 56, 16, False, False)
+        extract(A("P6", 112, 126), "KI", "invT", port0, 14, 256, False)
+        extract(A("P3", 0, 28), "EX", "vS", lambda r: r, 28, 16)
+        extract(A("P3", 28, 56), "EE", "vS", lambda r: r, 28, 16)
+        tt(A("n1"), A("P6", 0, 126), A("i9"), ALU.is_le)
+        tt(A("n2"), A("P6", 0, 126), A("n1"), ALU.mult)
+        cpy(A("cU"), A("n2"))
+        ts(A("sU"), A("P3", 0, 28), DM, ALU.add)
+        cpy(A("lU"), A("P3", 28, 56))
+        ts(A("xx", 28, 42), A("P3", 14, 28), DM, ALU.add)
+        ts(A("xx", 42, 56), A("P3", 0, 14), DM, ALU.add)
+        act(A("vC"), IND(A("cp"), A("sU")))
+        act(A("vL"), IND(A("Lq"), A("lU")), scale=0.25)
+        mm(A("P3", 0, DM), A("qIb"), A("vC"), True, True)
+        mm(A("P2", 0, NA), A("sIb"), A("Db", 3 - t, V, 4), True, False)
+        mm(A("P4", 0, NA), A("sIb"), A("vdR"), True, False)
+        mm(A("P4", 0, NA), A("NE"), A("invT", DM + r0, DM + NC, 16), False, False)
+        mm(A("P6", 0, 14), A("Ib"), A("iB"), True, False)
+        tt(A("yn", 0, NA), A("P3", 0, NA), A("vL", NA, DM), ALU.max)
+        tt(A("yn", NA, DM), A("P3", NA, DM), A("vL", 0, NA), ALU.max)
+        tt(A("P3", 0, DM), A("P3", 0, DM), A("vL"), ALU.max)
+        tt(A("yn"), A("yn"), A("P3", 0, DM), ALU.subtract)
+        act(A("dv"), A("yn", 0, NA), bias=12.0 / 128, scale=1.0 / 128)
+        tt(A("nw"), IND(A("S14"), A("wU")), A("yn", NA, DM), ALU.add)
+        cpy(A("mb2", V, V + E), turn(x5, "Bb"))
+        for lo, hi in ((0, 640), (640, V)):
+            tt(A("z3", lo, hi), IND(A("mb2"), A("aU", lo // 16, hi // 16)), A("mk", lo, hi), ALU.mult)
+            for l in range(4):
+                mm(A("P2", lo // 4, hi // 4), A("qIb"), A("z3", lo + l, hi, 4), False, l == 3 and hi == V)
+        ts(A("vote"), A("P2", 0, NA), A("thr"), ALU.is_ge)
+        mm(A("P4", 0, NA), A("blk"), A("vote"), False, True)
+        ts(A("actW", 1, NA + 1), A("P4", 0, NA), 24.5, ALU.is_ge)
+        mm(A("P5", 0, NA), A("sIb"), A("actW", 1, NA + 1), True, False)
+        act(A("cg", 2 * V, 9 * NA), IND(A("actW"), A("cU", 112, 126)))
+        mm(A("P5", 0, NA), A("nIb"), A("cg", 2 * V, 2 * V + NA), False, False)
+        for q, lo, hi in (("v", 0, 640), ("s", V, V + 512), ("v", 640, V), ("s", V + 512, V + 768), ("v", V + 768, 2 * V)):
+            (cpy if q == "v" else act)(A("cg", lo, hi), IND(A("actW"), A("cU", lo // 16, hi // 16)))
+            for j in range(4):
+                mm(A("P5", (lo % V) // 4, ((hi - 1) % V + 1) // 4), A("nIb"), A("cg", lo + j, hi, 4), False, hi == 2 * V and j == 3)
+        okv = A("okF", 3 - t, V, 4)
+        ts(okv, A("P5", 0, NA), 15.5, ALU.is_ge, 128.0, ALU.mult)
+        extract(A("P6", 0, 14), "E4", "okF", lambda r: 4 * r + 3 - t, 14, 64, False)
+        mm(A("P2", 0, NA), A("Ib"), okv, True, True)
+        tt(A("o1"), A("P6", 0, 14), A("xw"), ALU.min)
+        cpy(A("owU"), A("o1"))
+        tt(A("P2", 0, NA), A("P2", 0, NA), A("dv"), ALU.mult)
+        cpy(IND(A("S14"), A("owU")), A("nw"))
+        sv = A("S14", NA + 3 - t, NA + V, 4)
+        tt(sv, A("P2", 0, NA), sv, ALU.add)
+        tt(A(snd()), IND(A("S14", NA, NA + V), A("xbU")), A("snd0"), ALU.min)
+        x1 = send(False)
+        act(A("xx", 0, 14), A("rF", 14, 28))
+        act(A("xx", 14, 28), A("rF", 0, 14))
+        for j in range(4):
+            act(A("o4", 14 * j, 14 * j + 14), A("P6", 0, 14), bias=float(NA * (j & 1)))
+        act(A("vN"), IND(A("invT"), A("sU")))
+        for h, (lo, hi) in enumerate(HALF):
+            act(A("P%d" % h, 0, hi - lo), A("Lq", lo, hi))
+        tt(A("o4"), A("o4"), A("xx"), ALU.min)
+        cpy(A("oU"), A("o4"))
+        cpy(IND(A("sigT"), A("oU", 0, 28)), A("vS"))
+        load_cm()
+        extract(A("P7", 0, 224), "EE", "sigT", lambda r: DM + r, 224, 16)
+        for h, (lo, hi) in enumerate(HALF):
+            tt(A("q1", lo, hi), A("P%d" % h, 0, hi - lo), A("S14", NA + lo, NA + hi), ALU.min)
+        cpy(IND(A("cp"), A("oU", 28, 56)), A("vC"))
+        cpy(A("atO"), A("P7", 0, 224))
+        cpy(IND(A("invT"), A("oU", 28, 56)), A("vN"))
+    return ops
+
+
+def order(ops):
+    seen = {}
+    deps = []
+    for n, (q, kind, args, rd, wr) in enumerate(ops):
+        need = set()
+        dma = kind in ("dma", "send")
+        for acc, is_w in ((rd, False), (wr, True)):
+            for name, lo, hi, step in acc:
+                psum = SCRATCH[name][0] == "psum"
+                for m, mlo, mhi, mstep, m_w in seen.get(name, ()):
+                    same = ops[m][0] == q and not dma and ops[m][1] not in ("dma", "send", "arrive")
+                    hit = mlo < hi and lo < mhi and (lo - mlo) % math.gcd(step, mstep) == 0 and (m_w or is_w)
+                    if same and kind == "mm":
+                        hit = hit and args[3]
+                    if hit or (psum and not same):
+                        need.add(m)
+        for acc, is_w in ((rd, False), (wr, True)):
+            for name, lo, hi, step in acc:
+                seen.setdefault(name, []).append((n, lo, hi, step, is_w))
+        deps.append(need)
+    return deps
+
+
+def cost(op, c):
+    q, kind, a = op[:3]
+
+    def wide(x):
+        return 4 if SCRATCH[x[1]][2] in (F32, I32) else 2
+
+    def count(x):
+        return 16 * (x[2][3] - x[2][2]) if x[0] == "ind" else len(range(x[2], x[3], x[4]))
+
+    def psum(x):
+        return SCRATCH[x[1]][0] == "psum"
+
+    if kind == "arrive":
+        return 0.0, 0.0
+    if kind == "send":
+        return 500.0, c["flight"]
+    if kind == "dma":
+        x = a[0] if a[0][0] == "ap" else a[1]
+        return 60.0, 2000.0 + 0.21 * count(x) * wide(x)
+    if kind == "mm":
+        t = max(64, count(a[2])) * (4 if wide(a[2]) == 4 else 1) * c["pe"] + 5
+        return t, t
+    k = count(a[0])
+    if a[0][0] == "ind":
+        t = k * c["scatter"]
+    elif kind in ("iota", "sel"):
+        t = 130 + 2 * k
+    elif kind == "fill":
+        t = k * wide(a[0]) / 4
+    elif a[1][0] == "ind":
+        t = k * max(c["gather"], c.get("fused", 0) if kind == "tt" else 0)
+    elif kind == "tt":
+        t = k * (1 if psum(a[1]) or psum(a[2]) else 2)
+    elif kind == "act":
+        t = k
+    else:
+        t = k * (0.5 if wide(a[0]) == 2 and wide(a[1]) == 2 else 1)
+    t = max(t, 64) + c["call"]
+    return t, t
+
+
+def links(ops, deps):
+    out = []
+    last = {}
+    for n, op in enumerate(ops):
+        keys = []
+        if op[1] == "mm":
+            keys = [("bank", op[4][0][0])] + ([op[2][5]] if op[2][5] else [])
+        elif op[1] == "send":
+            keys = [("x", op[2][0]), "xs"]
+        more = set(last[k] for k in keys if k in last)
+        if op[1] == "arrive":
+            more.add(last[("x", op[2][0])])
+        for k in keys:
+            last[k] = n
+        out.append(set(m for m in deps[n] if ops[m][1] != "send") | more)
+    return out
+
+
+def plan():
+    ops = build()
+    deps = order(ops)
+    pre = links(ops, deps)
+    tm = [cost(op, COST) for op in ops]
+    size = len(ops)
+    gap = [{m: tm[m][1] + COST["hop"] if m in deps[n] or ops[n][1] == "arrive" else tm[m][0] + 0.001 for m in pre[n]} for n in range(size)]
+    post = [{} for n in range(size)]
+    for n in range(size):
+        for m, d in gap[n].items():
+            post[m][n] = d
+
+    def place(turn, before, back):
+        busy = {}
+        at = [0.0] * size
+        for n in turn:
+            need = max(tm[n][0], 0.001)
+            t = tm[n][1] - need if back else 0.0
+            for m, d in before[n].items():
+                t = max(t, at[m] + max(tm[m][0], 0.001) + d - need if back else at[m] + d)
+            line = busy.setdefault(ops[n][0], [])
+            j = len(line)
+            while j > 0 and line[j - 1][1] > t:
+                j -= 1
+            while j < len(line) and t + need > line[j][0]:
+                t = max(t, line[j][1])
+                j += 1
+            line.insert(j, (t, t + need))
+            at[n] = t
+        if back:
+            return [-(at[n] + max(tm[n][0], 0.001)) for n in range(size)]
+        return at
+
+    way = [t[1] for t in tm]
+    for n in range(size - 1, -1, -1):
+        for m, d in gap[n].items():
+            way[m] = max(way[m], d + way[n])
+    start = place(sorted(range(size), key=lambda k: (-way[k], k)), gap, False)
+    best = max(start[n] + tm[n][1] for n in range(size))
+    now = start
+    for rep in range(ROUNDS):
+        late = place(sorted(range(size), key=lambda k: (-now[k], -k)), post, True)
+        now = place(sorted(range(size), key=lambda k: (late[k], k)), gap, False)
+        end = max(now[n] + tm[n][1] for n in range(size))
+        if end < best:
+            best, start = end, now
+    seed = 12345
+    for rep in range(TRIES):
+        seed = (seed * 1103515245 + 12345) % 2147483648
+        mid = best * (seed >> 8) / 8388608.0
+        shift = {}
+        key = []
+        for n in range(size):
+            name = (ops[n][0], ops[n][4][0][0] if ops[n][4] else "")
+            if name not in shift:
+                seed = (seed * 1103515245 + 12345) % 2147483648
+                u = (seed >> 8) / 8388608.0
+                shift[name] = (u - 0.15) * -40000.0 if u < 0.15 else (0.85 - u) * 40000.0 if u > 0.85 else 0.0
+            key.append(start[n] + (shift[name] if abs(start[n] - mid) < 7000 else 0.0))
+        for n in range(size):
+            for m in gap[n]:
+                key[n] = max(key[n], key[m] + 0.0001)
+        now = place(sorted(range(size), key=lambda k: (key[k], k)), gap, False)
+        end = max(now[n] + tm[n][1] for n in range(size))
+        if end <= best:
+            best, start = end, now
+    seq = sorted(range(size), key=lambda k: (start[k], k))
+    new = {m: j for j, m in enumerate(seq)}
+    return [ops[m] for m in seq], [set(new[k] for k in deps[m]) for m in seq]
+
+
+_PLAN = []
+
+
+def rank_program(g, core, T, topo):
+    rank = T.rank_of(core)
+    if rank is None:
+        return
+    n_r = len(T.cores)
+    if not _PLAN:
+        _PLAN.extend(plan())
+    ops, deps = _PLAN
+    queue = {"v": g.vector, "s": g.scalar, "p": g.tensor, "g": g, "y": g.sync}
+    own = {"v": "sv", "s": "ss", "p": "sp", "g": "sg"}
+    known = {k: {} for k in queue}
+    cover = {}
+    waits = []
+    for n, need in enumerate(deps):
+        q = ops[n][0]
+        keep = []
+        for m in sorted(need, reverse=True):
+            if ops[m][1] == "send":
+                continue
+            key = ops[m][0] if ops[m][1] not in ("dma", "arrive") else m
+            if known[q].get(key, -1) >= m:
+                continue
+            keep.append(m)
+            for k, c in cover[m].items():
+                known[q][k] = max(known[q].get(k, -1), c)
+        waits.append(keep)
+        cover[n] = dict(known[q])
+        cover[n][q if ops[n][1] not in ("dma", "arrive") else n] = n
+    wanted = set(m for keep in waits for m in keep)
+
+    def ap(x):
+        if not isinstance(x, tuple):
+            return x
+        if x[0] == "ap":
+            return T[x[1]][:, x[2]:x[3]:x[4]] if x[4] != 1 else T[x[1]][:, x[2]:x[3]]
+        if x[0] == "ind":
+            return ap(x[1]).indirect(ap(x[2]))
+        if x[0] == "in":
+            return T[x[1]][:]
+        return T[x[1]][:, x[2]:x[3]]
+
+    count = {k: 0 for k in own}
+    mark = {}
+    waited = {k: {} for k in queue}
+    total = {}
+    for n, (q, kind, args, rd, wr) in enumerate(ops):
+        e = queue[q]
+        need = {}
+        for m in waits[n]:
+            s, c = mark[m]
+            need[s] = max(need.get(s, 0), c)
+        for s, c in need.items():
+            if waited[q].get(s, 0) < c:
+                e.wait_ge(T.sem[s], c)
+                waited[q][s] = c
+        if kind == "arrive":
+            mark[n] = ("arr%d" % args[0], total["arr%d" % args[0]])
+            continue
+        if kind == "send":
+            x, back = args
+            tr = []
+            for d in range(1, n_r):
+                dst = T.cores[(rank - d if back else rank + d) % n_r]
+                eng = topo.engines(core, dst)
+                k = len(eng) // 4
+                part = eng[k * (d - 1):k * d] if d < n_r - 1 else eng[k * (d - 1):]
+                mask = 0
+                for b in part:
+                    mask |= 1 << b
+                rid, pid, _ = topo.addr(dst)
+                tr.append(RemoteDMATransfer(dst_ids=[DstId(rid=rid, pnc=pid)], dma_engine_mask=mask, remote_sem=T.sem["arr%d" % x],
+                                            src=ap(A("snd%d" % x, X * (d - 1), X * d)), dst=ap(A("lnd%d" % x, X * (d - 1), X * d))))
+                total["arr%d" % x] = total.get("arr%d" % x, 0) + len(part)
+                total["sent"] = total.get("sent", 0) + len(part)
+            g.remote_dma_fused(tr, local_sem=T.sem["sent"])
+            continue
+        if kind == "dma":
+            e.dma_start(ap(args[0]), ap(args[1])).then_inc(T.sem[args[2]], 16)
+            mark[n] = (args[2], 16)
+            total[args[2]] = 16
+            continue
+        a = [ap(x) for x in args]
+        if kind == "copy":
+            ins = e.tensor_copy(a[0], a[1])
+        elif kind == "ts":
+            if a[5] is None:
+                ins = e.tensor_scalar(a[0], a[1], a[2], None, a[4])
+            else:
+                ins = e.tensor_scalar(a[0], a[1], a[2], a[3], a[4], a[5])
+        elif kind == "tt":
+            ins = e.tensor_tensor(a[0], a[1], a[2], a[3])
+        elif kind == "act":
+            ins = e.activation(a[0], a[1], a[2], bias=a[3], scale=a[4])
+        elif kind == "mm":
+            ins = e.matmul(a[0], a[1], a[2], a[3], a[4])
+        elif kind == "fill":
+            ins = e.memset(a[0], a[1])
+        elif kind == "sel":
+            ins = e.affine_select(a[0], a[0], a[1], a[2], a[3], a[4], a[5])
+        elif SCRATCH[args[0][1]][2] == I32:
+            ins = e.iota(a[0], a[1], a[2], a[3])
+        else:
+            ins = e.iota(a[0], a[1], a[2], a[3], allow_small_or_imprecise_dtypes=True)
+        if n in wanted:
+            ins.then_inc(T.sem[own[q]], 1)
+            count[q] += 1
+            mark[n] = (own[q], count[q])
+    for q in own:
+        total[own[q]] = count[q]
+    for s, c in total.items():
+        if c and max(w.get(s, 0) for w in waited.values()) < c:
+            g.wait_ge(T.sem[s], c)

@@ -4,34 +4,37 @@ from concourse.mybir import AluOpType as ALU, ActivationFunctionType as AF
 
 V, X, E, NC, NX, NA = 896, 128, 384, 3584, 3968, 224
 RO = 2
+VH = 512
+NV = 4 * VH
+NS = NC - NV
 DM = 448
 F32, BF, F16, I32, U16 = "float32", "bfloat16", "float16", "int32", "uint16"
 XDT = [F16] + [F16, F32, BF, BF, BF] * RO + [F16, F32, F32, F32, F32]
 
 _SB = {
-    "sigI": (248, I32), "lstU": (248, U16), "sigO": (224, U16), "atO": (224, U16), "xbU": (24, U16),
-    "invO": (248, U16), "wbU": (24, U16), "ta": (256, I32), "tb": (224, I32),
-    "debtI": (V, I32), "cashI": (V, I32), "thI": (1, I32), "thr": (1, F32), "colS": (NC, BF), "valS": (V, F32),
-    "Lq": (V + E, F32), "e16": (V, F16), "LB": (V, F32), "cm": (NX, BF),
+    "sigI": (248, I32), "lstU": (248, U16), "sigL": (224, U16), "atO": (224, U16), "xbU": (24, U16),
+    "invL": (248, U16), "wbU": (24, U16), "ta": (256, I32), "tb": (224, F32),
+    "debtI": (V, I32), "cashI": (V, I32), "thI": (1, I32), "thr": (1, F32), "colS": (NX, BF), "valS": (V, F32),
+    "Lq": (V + E, F32), "e16": (V, F16), "LB": (V, F16), "cm": (NC, BF),
     "S14": (NA + V + E, F32), "q1": (V + E, F32), "q2": (V, F32), "y16": (NC, F16), "W": (NX, F32), "R": (NC, F32),
-    "rw": (E, F32), "Db": (V, BF), "C0b": (NX, BF), "Zb1": (NC, BF),
-    "mb1": (V, BF), "mb2": (V + E, BF), "Cf": (NX, F32), "Zf": (NC, F32),
+    "rw": (E, F32), "Db": (V, BF), "C0b": (NX, BF), "Z": (NC, BF), "mb1": (V, BF), "mb2": (V + E, BF), "Cf": (NX, F32), "Rs": (NS, F32),
     "vinit": (NX, BF), "invT": (DM + NX, BF), "sigT": (DM + NX, BF), "cp": (DM + NX, BF),
-    "ioA": (128, I32), "ioC": (256, F32), "tf": (256, F32), "tc": (128, I32), "pI": (1, I32), "pJ": (2, I32), "OH": (16, F32),
-    "col": (24, F32), "Ib": (128, BF), "nIb": (128, BF), "qIb": (128, BF), "sIb": (128, BF), "qIh": (128, F16), "nIh": (128, F16),
-    "If": (128, F32), "nIf": (128, F32), "aIf": (128, F32), "bIf": (128, F32), "Fh": (128, F16), "Ff": (128, F32),
-    "Bb": (128, BF), "Bf": (128, F32), "mats": (6 * 144 + 256, BF), "one": (512, BF), "c01": (16, BF), "blkT": (256, BF),
-    "mIb": (128, BF), "cIb": (128, BF), "dIb": (128, BF), "i9": (126, F32), "iB": (14, BF), "kc": (56, F32), "kk": (126, F32),
+    "zb": (128, BF), "zf": (128, F32), "ioC": (256, F32), "tf": (256, F32), "pI": (1, I32), "pJ": (2, I32), "OH": (16, F32),
+    "col": (24, F32), "colB": (4, BF), "Ib": (128, BF), "nIb": (128, BF), "qIb": (128, BF), "sIb": (128, BF), "one": (VH, BF),
+    "qIh": (128, F16), "Ih": (128, F16), "If": (128, F32), "nIf": (128, F32), "Fh": (128, F16), "Ff": (128, F32),
+    "c15": (128, F32), "c2": (128, F32), "uIb": (128, BF), "mIb": (128, BF),
+    "aIb": (128, BF), "Bb": (128, BF), "Bf": (128, F32), "mats": (6 * 144 + 256, BF), "c01": (16, BF), "blkT": (256, BF),
+    "dIb": (128, BF), "i9": (126, F32), "iB": (14, BF), "kc": (56, F32), "kk": (126, F32),
     "MA": (V, BF), "mk": (V, BF), "z3": (V, BF), "aU": (56, U16), "vF": (28, F32), "ne": (14, F32),
     "kI": (56, I32), "n1": (126, F32), "n2": (126, F32), "cU": (126, U16), "wU": (14, U16), "vdU": (14, U16),
-    "g4U": (56, U16), "rF": (28, F32), "rU": (28, U16), "sU": (28, U16), "lU": (28, U16),
-    "vS": (DM, BF), "vN": (DM, BF), "vC": (DM, BF),
+    "g4U": (56, U16), "rF": (28, F32), "rU": (28, U16), "sU": (56, U16),
+    "vS": (DM, BF), "vN": (DM, BF), "vC": (DM, BF), "rIh": (128, F16),
     "vdR": (NA, BF), "vote": (NA, BF), "actW": (240, BF), "okF": (V, BF),
     "xw": (14, F32), "xx": (56, F32), "o1": (14, F32), "o4": (56, F32), "owU": (14, U16), "oU": (56, U16),
 }
-ALIAS = {"C1b": ("vinit", 0, NX), "Zb2": ("colS", 0, NC), "cg": ("colS", 0, 9 * NA), "gw": ("z3", 0, V), "mf": ("q2", 0, V),
-         "vL": ("Zf", 0, DM), "yn": ("Zf", DM, DM), "dv": ("Zf", 2 * DM, NA), "nw": ("Zf", 2 * DM + NA, NA),
-         "val14": ("S14", NA, V), "Lf": ("Cf", 0, V), "pO": ("q1", 0, V), "vw": ("q1", V, E), "nM": ("mb2", 0, V),
+ALIAS = {"C1b": ("vinit", 0, NX), "Z2": ("colS", 0, NC), "cg": ("colS", 0, 9 * NA), "gw": ("z3", 0, V), "mf": ("Lq", 0, V),
+         "vL": ("y16", 0, DM), "yn": ("y16", DM, DM), "yo": ("y16", 2 * DM, DM), "dv": ("Rs", 0, NA), "dw": ("Rs", NA, NA), "nw": ("Rs", DM, NA),
+         "pO": ("q2", 0, V), "u0": ("q1", 0, V), "vw": ("q1", V, E), "b1": ("S14", 0, VH), "nM": ("Z", 0, NC),
          "EX": ("mats", 0, 144), "EE": ("mats", 144, 144), "EW": ("mats", 288, 144), "KI": ("mats", 432, 144), "KS": ("mats", 576, 144),
          "E4": ("mats", 720, 144), "NE": ("mats", 864, 128), "blk": ("mats", 992, 128)}
 for _d, _s in ((F16, "h"), (F32, "f"), (BF, "b")):
@@ -47,15 +50,27 @@ for _i in range(8):
 _DMAS = ["d%d" % i for i in range(10)]
 SEMAPHORES = ["sv", "ss", "sp", "sg", "sent"] + ["arr%d" % i for i in range(len(XDT))] + _DMAS
 
-HALF = ((0, 512), (512, V))
-CH32 = (("v", 0, 256), ("s", 256, 512), ("v", 512, 1024), ("s", 1024, 1536), ("v", 1536, 2048), ("s", 2048, 2560), ("v", 2560, 2816),
-        ("s", 2816, 3328), ("s", 3328, NC))
-CH16 = (("v", 0, 1024), ("s", 1024, 2048), ("v", 2048, 2560), ("s", 2560, 3072), ("v", 3072, 3328), ("s", 3328, NC))
-SIDE3 = ((("P4",), ("P5",)), (("P4", "P5"), ("P6",)))
-PIECE = 32
-COST = dict(gather=1.56, scatter=3.8, pe=0.5, flight=3500.0, hop=80.0, call=60.0)
+HALF = ((0, VH), (VH, V))
+CH16 = (("v", 0, 768), ("s", 768, 1536), ("v", 1536, 2048), ("s", 2048, 2816), ("v", 2816, 3328), ("s", 3328, NC))
+CH3 = (("v", 0, 256), ("s", 256, 512), ("v", 512, 1024), ("s", 1024, 1536), ("v", 1536, 2048), ("s", 2048, 2560), ("s", 2560, 3072),
+       ("s", 3072, NC))
+SIDEW = ((("P4",), ("P5",)), (("P4", "P5"), ("P6",)))
+SIDE0 = (("P2",), ("P3",))
+SIDE1 = (("P2", "P3"), ("P2", "P3"))
+CH1 = (("v", 0, 512), ("o", 1024, 1536), ("v", 512, 1024), ("o", 1536, 2048), ("t", 2048, 2560), ("o", 2560, 3072), ("o", 3072, NC))
+CH2 = ((("v", 0, 512), ("o", 1024, 1536), ("v", 512, 1024), ("t", 1536, 2048), ("t", 2048, 2560), ("t", 2560, 3072), ("t", 3072, NC)),
+       (("t", 0, 512), ("v", 512, 1024), ("t", 1024, 1536), ("t", 1536, 2048), ("t", 2048, 2560), ("t", 2560, 3072), ("v", 3072, NC)))
+ADD3 = (1, 2)
+GWV = 0
+CPV = (1, 3, 5)
+SF, SW = 2, 1
+CH32 = ((0, 0, 192), (0, 192, 384), (1, 0, 384), (2, 0, 384), (3, 0, 256), (3, 256, 384))
+PIECE = 16
+COST = dict(gather=1.56, fused=1.75, scatter=3.8, pe=0.56, flight=4000.0, hop=90.0, call=60.0)
 ROUNDS = 6
-TRIES = 500
+TRIES = 20000
+LUMP = 650.0
+EARLY = 0.05
 
 
 def A(name, a=0, b=None, step=1):
@@ -111,8 +126,19 @@ def build():
     def iota(out, pat, base, cm):
         put("g", "iota", out, [], (out, pat, base, cm))
 
-    def select(out, pat, op, c, base, cm):
-        put("g", "sel", out, [out], (out, pat, op, c, base, cm))
+    def zero(out):
+        iota(out, [[0, out[3] - out[2]]], 0, 0)
+
+    def select(out, pat, op, c, base, cm, x=None):
+        put("g", "sel", out, [x or out], (out, pat, op, c, base, cm, x or out))
+
+    def hand(out, x):
+        select(out, [[0, len(range(*out[2:]))]], ALU.is_equal, 0.0, 0, 0, x)
+
+    def diag(w, c, shift=0):
+        select(A(w), [[-1, 128]], ALU.not_equal, c, shift, 1, A("zf" if SCRATCH[A(w)[1]][2] == F32 else "zb"))
+        if shift:
+            select(A(w), [[-1, 128]], ALU.not_equal, c, shift - 128 if shift > 0 else shift + 128, 1)
 
     nd = [0]
 
@@ -130,12 +156,15 @@ def build():
         nx[0] += 1
         return nx[0] - 1
 
-    def export(win, lst):
-        cpy(A(snd(), 0, 192), IND(win, A(lst, 0, 12)))
-        act(A(snd(), 192, E), IND(win, A(lst, 12, 24)))
+    def export(win, lst, scale=1.0):
+        ts(A(snd(), 0, 192), IND(win, A(lst, 0, 12)), scale, ALU.mult)
+        act(A(snd(), 192, E), IND(win, A(lst, 12, 24)), scale=scale)
+
+    def arrive(n):
+        ops.append(("a", "arrive", (n,), [], span(A("lnd%d" % n))))
 
     def turn(n, w):
-        ops.append(("p", "arrive", (n,), [], span(A("lnd%d" % n))))
+        arrive(n)
         mm(A("P7", 0, E), A(w), A("lnd%d" % n), True, True)
         return A("P7", 0, E)
 
@@ -144,9 +173,17 @@ def build():
             f = first(r)
             mm(out, A(w, 15 - r, 143 - r), A(tab, f, f + step * (n - 1) + 1, step), start and r == 0, stop and r == 15)
 
+    def shares(bank, tab):
+        for k in range(4):
+            extract(A(bank, 56 * k, 56 * k + 56), "EX", tab, lambda r: DM + 4 * r + k, 56, 64)
+        return A(bank, 0, NA)
+
+    def part(lst, k, lo, hi):
+        return A(lst, 56 * k + lo // 16, 56 * k + hi // 16)
+
     def pb(banks, lo, hi):
-        h = 0 if lo < 512 else 1
-        return A(banks[h], lo - 512 * h, hi - 512 * h)
+        h = 0 if lo < VH else 1
+        return A(banks[h], lo - VH * h, hi - VH * h)
 
     def col(j):
         return A("col", j, j + 1)
@@ -157,15 +194,21 @@ def build():
     dma("y", A("sigI", 224, 248), ("in", "xpt"))
     dma("s", A("debtI"), ("in", "debt"))
     dma("y", A("sigI", 0, 224), ("in", "sig"))
-    dma("s", A("colS"), ("in", "coll"))
+    dma("s", A("colS", 0, NC), ("in", "coll"))
     dma("y", A("cashI"), ("in", "cash"))
     dma("y", A("thI"), ("in", "th"))
     dma("y", A("valS"), ("in", "val"))
     iota(A("pI"), [[0, 1]], 0, 1)
     iota(A("ioC"), [[1, 256]], 0, 0)
-    iota(A("ioA"), [[1, 128]], 0, -1)
-    fill(A("mats", 0, 992), 0.0)
-    fill(A("invT", 0, DM), 0.0)
+    zero(A("zb"))
+    zero(A("zf"))
+    diag("Ib", 1.0)
+    diag("Ff", 1.0, 16)
+    diag("nIf", -1.0)
+    zero(A("mats", 0, 496))
+    zero(A("mats", 496, 992))
+    zero(A("invT", 0, DM))
+    zero(A("colS", NC, NX))
     ts(A("pJ", 0, 1), A("pI"), 15, ALU.bitwise_and)
     cpy(col(0), A("pJ", 0, 1))
     ts(A("OH"), A("ioC", 0, 16), col(0), ALU.is_equal)
@@ -178,12 +221,10 @@ def build():
     act(col(2), oh(7), bias=col(1), scale=0.25)
     act(col(7), col(4), scale=8.0)
     act(col(3), col(2), bias=-0.5, scale=0.5)
-    ts(A("tc"), A("ioA"), 112, ALU.add)
-    ts(A("Ib"), A("ioA"), 0, ALU.is_equal)
-    ts(A("tc"), A("tc"), 127, ALU.bitwise_and)
-    ts(A("qIh"), A("ioA"), 0, ALU.is_equal, 0.25, ALU.mult)
-    ts(A("Fh"), A("tc"), 0, ALU.is_equal)
-    ts(A("nIh"), A("ioA"), 0, ALU.is_equal, -1.0, ALU.mult)
+    cpy(A("colB"), A("col", 4, 8))
+    act(A("qIh"), A("Ib"), scale=0.25)
+    act(A("Fh"), A("Ff"))
+    act(A("Ih"), A("Ib"))
     ts(A("ta", 0, 24), A("sigI", 224, 248), 2, ALU.arith_shift_right)
     cpy(A("xbU"), A("ta", 0, 24))
     ts(A(snd()), IND(A("debtI"), A("xbU")), 0.25, ALU.mult, -128.0, ALU.add)
@@ -191,25 +232,25 @@ def build():
     ts(A("tf"), A("ioC"), col(2), ALU.mult, col(3), ALU.add)
     cpy(A("lstU"), A("sigI"))
     cpy(A("ta"), A("tf"))
-    ts(A("Lq", 0, V), A("debtI"), 0.25, ALU.mult, -128.0, ALU.add)
+    act(A("Lq", 0, V), A("debtI"), bias=-128.0, scale=0.25)
     cpy(A("vinit", 0, 256), A("ta"))
-    ts(A("tb"), A("sigI", 0, 224), -3 * V, ALU.add)
-    act(A("vinit", 256, 512), A("vinit", 0, 256), bias=col(4))
-    ts(A("ta", 0, 224), A("sigI", 0, 224), 2, ALU.arith_shift_right)
-    act(A("vinit", 512, 1024), A("vinit", 0, 512), bias=col(5))
-    tt(A("ta", 0, 224), A("ta", 0, 224), A("tb"), ALU.max)
+    act(A("tb"), A("sigI", 0, 224), bias=-0.375, scale=0.25)
+    act(A("P6", 0, 224), A("sigI", 0, 224), bias=-3.0 * V)
+    ts(A("vinit", 256, 512), A("vinit", 0, 256), A("colB", 0, 1), ALU.add)
+    ts(A("vinit", 512, 1024), A("vinit", 0, 512), A("colB", 1, 2), ALU.add)
+    tt(A("tb"), A("tb"), A("P6", 0, 224), ALU.max)
     act(A("cm", 1024, NC), A("colS", 1024, NC), bias=-128.0)
-    cpy(A("atO"), A("ta", 0, 224))
-    cpy(A("e16"), A("cashI"))
+    cpy(A("atO"), A("tb"))
+    act(A("e16"), A("cashI"))
     act(A("cm", 0, 1024), A("colS", 0, 1024), bias=-128.0)
-    act(A("vinit", 1024, 2048), A("vinit", 0, 1024), bias=col(6))
+    ts(A("vinit", 1024, 2048), A("vinit", 0, 1024), A("colB", 2, 3), ALU.add)
     act(col(8), oh(7), bias=col(2), scale=0.75)
     act(col(9), col(8), bias=-0.5, scale=0.5)
     act(col(10), col(4), bias=oh(6), scale=14.0)
     act(col(12), oh(4), bias=col(10), scale=4.0)
     act(col(11), oh(0), bias=col(12))
     act(A("tf"), A("ioC"), bias=col(9), scale=col(8))
-    act(A("vinit", 2048, NC), A("vinit", 0, NC - 2048), bias=col(7))
+    ts(A("vinit", 2048, NC), A("vinit", 0, NC - 2048), A("colB", 3, 4), ALU.add)
     cpy(A("ta"), A("tf"))
     cpy(A("blkT"), A("ta"))
     act(A("vinit", NC, NC + 256), A("blkT"), bias=col(10))
@@ -218,15 +259,15 @@ def build():
         cpy(IND(A("invT", DM, DM + NX), A("lstU", c, min(c + PIECE, 248))), A("vinit", 16 * c, 16 * min(c + PIECE, 248)))
     for c in range(0, 224, 56):
         act(A("sigT", DM + 16 * c, DM + 16 * c + V), IND(A("vinit"), A("lstU", c, c + 56)))
-    act(A("Lf"), A("Lq", 0, V), bias=512.0, scale=4.0)
-    act(A("nIb"), A("Ib"), scale=-1.0)
-    act(A("cm", NC, NX), A("cm", 0, E), scale=0.0)
+    diag("nIb", -1.0)
+    diag("qIb", 0.25)
     for h, (lo, hi) in enumerate(HALF):
-        o = A("P%d" % (2 + h), 0, hi - lo)
-        mm(o, A("nIh"), A("e16", lo, hi), True, False)
+        o = A("P%d" % h, 0, hi - lo)
+        mm(o, A("qIh"), A("e16", lo, hi), True, False)
         for k in range(4):
-            mm(o, A("nIb"), A("colS", 4 * lo + k, 4 * hi, 4), False, k == 3)
-        tt(A("LB", lo, hi), o, A("Lf", lo, hi), ALU.add)
+            mm(o, A("qIb"), A("colS", 4 * lo + k, 4 * hi, 4), False, False)
+        mm(o, A("nIf"), A("Lq", lo, hi), False, True)
+        act(A("LB", lo, hi), o, scale=-4.0, bias=512.0)
     fill(A("mats", 992, 1120), 1.0)
     for w, rows in (("EX", ((0, 256), (1, 1))), ("EE", ((4, 64), (7, 1))), ("EW", ((0, 256), (5, 4))),
                     ("KI", ((0, 16), (2, 1), (3, -4096), (5, 1024))), ("KS", ((0, 16), (1, 256), (2, 1), (3, -4096)))):
@@ -239,71 +280,66 @@ def build():
     iota(A("i9", 112, 126), [[16, 14]], 0, 0)
     iota(A("kc"), [[1, 4], [0, 14]], 0, 0)
 
-    def load_cm():
-        for c in range(5):
-            mm(A("P%d" % (2 + c)), A("Ib"), A("cm", 1024 + 512 * c, 1536 + 512 * c), True, True)
-
-    def claim_sweep(win, out, acted):
-        def total(c):
-            o = pb(("P0", "P1"), 128 * c, 128 * c + 128)
-            mm(o, A("qIh"), A("e16", 128 * c, 128 * c + 128), True, False)
-            if acted:
-                mm(o, A("cIb"), A("okF", 128 * c, 128 * c + 128), False, False)
-            for k in range(4):
-                mm(o, A("qIh"), A("y16", 512 * c + k, 512 * c + 512, 4), False, k == 3)
-
-        def top(c):
-            tt(A("y16", 512 * c, 512 * c + 512), A("Zf", 512 * c, 512 * c + 512), A("P%d" % c), ALU.max)
-            total(c)
-
-        tt(A("y16", 0, 1024), IND(win, A("atO", 0, 64)), A("cm", 0, 1024), ALU.max)
-        for c in range(2, 7):
-            act(A("Zf", 512 * c, 512 * c + 512), IND(win, A("atO", 32 * c, 32 * c + 32)))
-        total(0)
-        total(1)
-        top(2)
-        top(3)
-        top(4)
-        tt(A(out, 0, 512), A("P0"), A("Lq", 0, 512), ALU.min)
-        top(5)
-        top(6)
-        tt(A(out, 512, V), A("P1", 0, V - 512), A("Lq", 512, V), ALU.min)
-
-    def gather32(win, lst, out, scale, relu, banks, w, after):
-        for q, lo, hi in CH32:
-            src = IND(win, A(lst, lo // 16, hi // 16))
-            if q == "v":
-                if relu:
-                    ts(A(out, lo, hi), src, scale, ALU.mult, 0.0, ALU.max)
+    def claim_sweep(win, out, pieces, wide):
+        for h, (lo, hi) in enumerate(HALF):
+            mm(A("P%d" % h, 0, hi - lo), A("qIh"), A("e16", lo, hi), True, False)
+        bank = 2
+        for j, (how, lo, hi) in enumerate(pieces):
+            y, x, c = A("y16", lo, hi), IND(win, A("atO", lo // 16, hi // 16)), A("cm", lo, hi)
+            o = pb(("P0", "P1"), lo // 4, hi // 4)
+            w, val = "qIh", "y16"
+            if how == "v":
+                tt(y, x, c, ALU.max)
+            else:
+                p = A("P%d" % bank, 0, hi - lo)
+                bank += 1
+                act(y, x)
+                if how == "t":
+                    mm(p, A("Ib"), c, True, True)
+                    tt(y, y, p, ALU.max)
                 else:
-                    ts(A(out, lo, hi), src, scale, ALU.mult)
-            else:
-                act(A(out, lo, hi), src, AF.Relu if relu else AF.Identity, scale=scale)
-            for k in range(2):
-                mm(pb(banks, lo // 4, hi // 4), A(w), A(out, lo + k, hi, 4), False, k == 1 and hi in (2048, NC), "sum")
-        after(0)
-        after(1)
-
-    def gather16(win, out, banks, mout):
-        for q, lo, hi in CH16:
-            src = IND(win, A("invO", lo // 16, hi // 16))
-            if q == "v":
-                cpy(A(out, lo, hi), src)
-            else:
-                act(A(out, lo, hi), src)
-        for q, lo, hi in CH16:
+                    for k in range(4):
+                        mm(o, A("qIb"), A("cm", lo + k, hi, 4), False, False)
+                    mm(p, A("nIb"), c, True, False)
+                    mm(p, A("Ih"), y, False, True)
+                    if wide:
+                        w, val = "c2", "R"
+                    act(A(val, lo, hi), p, AF.Relu)
+            last = all((lo < NV) != (a < NV) for _, a, b in pieces[j + 1:])
             for k in range(4):
-                mm(pb(banks, lo // 4, hi // 4), A("qIb"), A(out, lo + k, hi, 4), False, k == 3 and hi in (2048, NC), "sum")
-        cpy(A(mout, 0, 512), A(banks[0]))
-        act(A(mout, 512, V), A(banks[1], 0, V - 512))
+                mm(o, A(w), A(val, lo + k, hi, 4), False, last and k == 3)
+            if last:
+                a, b = HALF[lo >= NV]
+                tt(A(out, a, b), A("P%d" % (lo >= NV), 0, b - a), A("Lq", a, b), ALU.min)
+
+    def sum32(win, lst, first, out, bank, w):
+        for k in range(4):
+            for lo, hi in ((0, VH // 2), (VH // 2, VH)):
+                tt(A(out, lo, hi), IND(win, part(lst, k, lo, hi)), A(out if k else first, lo, hi), ALU.add)
+        for k, lo, hi in CH32:
+            r = A("Rs", (V - VH) * k + lo, (V - VH) * k + hi)
+            act(r, IND(win, part(lst, k, VH + lo, VH + hi)))
+            mm(A(bank, lo, hi), A(w), r, False, (k, lo, hi) == CH32[-1])
 
     def base(banks, w, x):
         for h, (lo, hi) in enumerate(HALF):
             mm(A(banks[h], 0, hi - lo), A(w), A(x, lo, hi) if x != "one" else A(x, 0, hi - lo), True, False)
 
-    def spread(out, other, off, banks, op, side=None):
+    def gather(win, lst, pieces, out, scale, banks, w, planes):
+        for j, (q, lo, hi) in enumerate(pieces):
+            x = IND(win, A(lst, lo // 16, hi // 16))
+            if q == "v":
+                ts(A(out, lo, hi), x, scale, ALU.mult, 0.0, ALU.max)
+            else:
+                act(A(out, lo, hi), x, AF.Relu, scale=scale)
+            last = all((lo < NV) != (a < NV) for _, a, b in pieces[j + 1:])
+            n = planes[lo >= NV]
+            for k in range(n):
+                mm(pb(banks, lo // 4, hi // 4), A(w), A(out, lo + k, hi, 4), False, last and k == n - 1)
+
+    def spread(out, other, off, banks, op, side):
         for h, (lo, hi) in enumerate(HALF):
-            cut = 4 - len(side[0][h]) if side else 4
+            cut = 4 - len(side[0][h])
             for k in range(cut):
                 tt(A(out, 4 * lo + k, 4 * hi, 4), A(banks[h], 0, hi - lo), A(other, off + 4 * lo + k, off + 4 * hi, 4), op)
             for k in range(cut, 4):
@@ -313,265 +349,273 @@ def build():
                     mm(o, A(w), src, j == 0, j == len(side[1]) - 1)
                 act(A(out, 4 * lo + k, 4 * hi, 4), o, side[2], bias=side[3])
 
-    def inverse_lists(bank):
-        extract(A(bank, 256, 280), "EE", "invT", lambda r: DM + NC + r, 24, 16)
-        cpy(A("wbU"), A(bank, 256, 280))
-        extract(A(bank, 0, 248), "EX", "invT", lambda r: DM + r, 248, 16)
-        cpy(A("invO"), A(bank, 0, 248))
+    def threats(win, out, banks, mout):
+        gather(A(win), "invL", CH16, out, 1.0, banks, "qIb", (4, 4))
+        cpy(A(mout, 0, VH), A(banks[0]))
+        act(A(mout, VH, V), A(banks[1], 0, V - VH))
+        export(A(mout, 0, V), "wbU")
+        return send(True)
 
-    load_cm()
     act(A("Lq", V, V + E), turn(x0, "Fh"))
-    claim_sweep(A("Lq"), "q1", False)
-    cpy(A(snd()), IND(A("q1", 0, V), A("xbU")))
+    claim_sweep(A("Lq"), "q1", CH1, False)
+    act(A(snd()), IND(A("q1", 0, V), A("xbU")))
     x1 = send(False)
-    act(A("S14", NA, NA + 512), A("P0"))
-    act(A("S14", NA + 512, NA + V), A("P1", 0, V - 512))
-    cpy(A("sigO"), A("sigI", 0, 224))
-    cpy(A("Ff"), A("Fh"))
-    act(A("aIf"), A("Ib"), scale=64.0)
-    act(A("nIf"), A("Ib"), scale=-1.0)
-    act(A("If"), A("Ib"))
+    act(A("S14", NA, NA + VH), A("P0"))
+    act(A("S14", NA + VH, NA + V), A("P1", 0, V - VH))
+    cpy(A("sigL"), A("sigI", 0, NA))
+    iota(A("one"), [[0, VH]], 1, 0)
+    zero(A("c01"))
+    select(A("c01"), [[-1, 16]], ALU.is_ge, 1.0, 0, 0)
+    for w, c, shift in (("If", 1.0, 0), ("aIb", 2.0 ** 27, 0), ("Bb", 1.0, -16), ("sIb", 16.0, 0),
+                        ("dIb", 0.375, 0), ("Bf", 1.0, -16), ("c15", 2.0 ** -15, 0),
+                        ("c2", 0.25, 0), ("uIb", 2.0 ** 11, 0), ("mIb", -2.0 ** 19, 0)):
+        diag(w, c, shift)
+    for w, lo, hi in (("cp", 0, DM), ("sigT", 0, DM), ("sigT", DM + NC, DM + NX), ("S14", 0, NA), ("S14", NA + V, NA + V + E),
+                      ("actW", 0, 16), ("actW", NA, 240), ("okF", 0, DM), ("okF", DM, V)):
+        zero(A(w, lo, hi))
+    act(A("E4", 15, 143, 16), A("blk", 0, 128, 16), scale=4.0)
+    ts(A("pJ", 0, 1), A("pI"), 2, ALU.arith_shift_right, 3, ALU.bitwise_and)
+    ts(A("pJ", 1, 2), A("pI"), 3, ALU.bitwise_and)
+    cpy(A("col", 13, 15), A("pJ"))
+    ts(A("thr"), A("thI"), 1.0 / 64, ALU.mult, 15.0, ALU.add)
 
     for t in range(RO + 1):
         close = t == RO
         r0 = 4 * (3 - t)
-        act(A("q1", V, V + E), turn(x1, "Fh"))
         if t == 0:
-            inverse_lists("P7")
-            for c in range(0, 248, 62):
-                act(A("cp", DM + 16 * c, DM + 16 * c + 992), IND(A("cm"), A("invO", c, c + 62)))
+            act(A("q1", V, V + E), turn(x1, "Fh"))
         else:
-            extract(A("P7", 0, 224), "EX", "sigT", lambda r: DM + r, 224, 16)
-            cpy(A("sigO"), A("P7", 0, 224))
-        claim_sweep(A("q1"), "q2", t > 0)
+            tt(A("q1", V, V + E), turn(x1, "Fh"), A("Lq", V, V + E), ALU.min)
+        if t == 0:
+            for lo, hi in ((0, 128), (128, 248)):
+                extract(A("P7", lo, hi), "EX", "invT", lambda r: DM + 16 * lo + r, hi - lo, 16)
+                cpy(A("invL", lo, hi), A("P7", lo, hi))
+            for j, c in enumerate(range(0, 248, 32)):
+                end = min(c + 32, 248)
+                o, x = A("cp", DM + 16 * c, DM + 16 * end), IND(A("colS"), A("invL", c, end))
+                if j in CPV:
+                    ts(o, x, -128.0, ALU.add)
+                else:
+                    act(o, x, bias=-128.0)
+        else:
+            extract(A("P7", 0, NA), "EX", "sigT", lambda r: DM + r, NA, 16)
+            cpy(A("sigL"), A("P7", 0, NA))
+        claim_sweep(A("q1"), "q2", CH2[min(t, 1)], True)
         export(A("q2"), "xbU")
         x2 = send(False)
         for h, (lo, hi) in enumerate(HALF):
             act(A("P%d" % h, 0, hi - lo), A("q2", lo, hi))
+        base(("P2", "P3"), "aIb", "LB")
+        spread("W", "cp", DM, ("P0", "P1"), ALU.subtract, (SIDEW[min(t, 1)], (("If", "q2", None), ("nIb", "cp", (DM,))), AF.Identity, 0.0))
+        extract(A("P6", 256, 280), "EE", "invT", lambda r: DM + NC + r, 24, 16)
+        cpy(A("wbU"), A("P6", 256, 280))
         if close:
-            act(A("val14"), A("valS"), scale=2.0 ** 14)
-            act(A("bIf"), A("Ib"), scale=2.0 ** 27)
-            act(A("mIb"), A("Ib"), scale=-2.0 ** 22)
-            act(A("Bf"), A("Bb"))
-            act(A("pO"), A("Lq", 0, V), bias=512.0, scale=4.0)
-        base(("P2", "P3"), "bIf" if close else "aIf", "LB")
-        if t > 0:
-            act(A("dIb"), A("Ib"), scale=-0.375 * (2.0 ** 27 if close else 64.0))
-            for h, (lo, hi) in enumerate(HALF):
-                mm(A("P%d" % (2 + h), 0, hi - lo), A("dIb"), A("okF", lo, hi), False, False)
-        spread("W", "cp", DM, ("P0", "P1"), ALU.subtract, (SIDE3[min(t, 1)], (("If", "q2", None), ("nIb", "cp", (DM,))), AF.Identity, 0.0))
-        if t > 0:
-            inverse_lists("P6")
+            cpy(A("invL", 0, NA), shares("P6", "invT"))
+            act(A("b1"), A("valS", 0, VH), scale=2.0 ** 13)
+        elif t > 0:
+            extract(A("P6", 0, NA), "EX", "invT", lambda r: DM + r, NA, 16)
+            cpy(A("invL", 0, NA), A("P6", 0, NA))
         tt(A("W", NC, NX), turn(x2, "Ff"), A("cp", DM + NC, DM + NX), ALU.subtract)
-        scale = 2.0 ** 27 if close else 64.0
-
-        def shortfall(h):
-            lo, hi = HALF[h]
-            o = A("P%d" % (2 + h), 0, hi - lo)
-            if h == 0:
-                act(A("rw"), A("W", NC, NX), AF.Relu, scale=scale)
-            tt(o, o, A("R", 4 * lo + 2, 4 * hi, 4), ALU.subtract)
-            tt(A("Db", lo, hi), o, A("R", 4 * lo + 3, 4 * hi, 4), ALU.is_gt)
-            if h == 0 and close:
-                tt(A("vw"), IND(A("val14"), A("wbU")), A("rw"), ALU.min)
-
-        gather32(A("W"), "sigO", "R", scale, True, ("P2", "P3"), "nIf", shortfall)
+        gather(A("W"), "sigL", CH3, "R", 2.0 ** 27, ("P2", "P3"), "nIf", ADD3)
+        act(A("rw"), A("W", NC, NX), AF.Relu, scale=2.0 ** 27)
         if close:
-            tt(A(snd()), IND(A("Db"), A("wbU")), A("vw"), ALU.mult)
-        else:
-            tt(A(snd()), IND(A("Db"), A("wbU")), A("rw"), ALU.min)
+            tt(A("vw"), IND(A("valS"), A("wbU")), A("rw"), ALU.min)
+        for h, (lo, hi) in enumerate(HALF):
+            o = A("P%d" % (2 + h), 0, hi - lo)
+            for k in range(ADD3[h], 3):
+                tt(o, o, A("R", 4 * lo + k, 4 * hi, 4), ALU.subtract)
+            tt(A("Db", lo, hi), o, A("R", 4 * lo + 3, 4 * hi, 4), ALU.is_gt)
+        tt(A(snd()), IND(A("Db"), A("wbU")), A("vw" if close else "rw"), ALU.mult if close else ALU.min)
         x3 = send(True)
         for h, (lo, hi) in enumerate(HALF):
-            mm(A("P%d" % h, 0, hi - lo), A("Ib"), A("Db", lo, hi), True, True)
+            mm(A("P%d" % h, 0, hi - lo), A("uIb" if close else "Ib"), A("Db", lo, hi), True, True)
 
         if close:
-            for h, (lo, hi) in enumerate(HALF):
-                o = A("P%d" % h, 0, hi - lo)
-                tt(o, o, A("val14", lo, hi), ALU.mult)
-            base(("P4", "P5"), "If", "valS")
-            spread("Cf", "R", 0, ("P0", "P1"), ALU.min)
-            act(A("nM"), A("Cf", 3, NC, 4), AF.Relu, bias=1.0, scale=-1.0)
-            act(A("Cf", NC, NX), turn(x3, "Bf"))
+            rest = A("P1", 0, V - VH)
+            tt(rest, rest, A("valS", VH, V), ALU.mult)
+            tt(A("P0"), A("P0"), A("valS", 0, VH), ALU.mult)
+            if SF:
+                act(A("u0", VH, V), rest)
+            for k in range(4):
+                tt(A("Cf", k, NV, 4), A("P0"), A("R", k, NV, 4), ALU.min)
+                if k < SF:
+                    act(A("nM", k, NS, 4), A("R", NV + k, NC, 4), AF.Relu, bias=1.0, scale=-1.0)
+                    o = A("P%d" % (4 + 2 * (k & 1)), 0, V - VH)
+                    mm(o, A("mIb"), A("nM", k, NS, 4), True, False)
+                    mm(o, A("If"), A("u0", VH, V), False, True)
+                    act(A("Cf", NV + k, NC, 4), o, AF.Relu)
+                else:
+                    tt(A("Cf", NV + k, NC, 4), rest, A("R", NV + k, NC, 4), ALU.min)
+            act(A("Cf", NC, NX), turn(x3, "Bf"), scale=2.0 ** 11)
             win = "Cf"
-            banks = ("P4", "P5")
-            for sw in range(3):
-                def rest(h):
-                    lo, hi = HALF[h]
-                    o = A(banks[h], 0, hi - lo)
-                    tt(o, o, A("Zf", 4 * lo + 2, 4 * hi, 4), ALU.add)
-                    if sw < 2:
-                        tt(A("mf", lo, hi), o, A("Zf", 4 * lo + 3, 4 * hi, 4), ALU.add)
-                    else:
-                        tt(o, o, A("Zf", 4 * lo + 3, 4 * hi, 4), ALU.add)
-                        tt(A("mf", lo, hi), o, A("Db", lo, hi), ALU.mult)
-                        dma("y" if h == 0 else "s", ("out", "mu", lo, hi), A("mf", lo, hi))
-
-                gather32(A(win), "invO", "Zf", 2.0 ** -16 if sw == 0 else 0.25, False, banks, "If", rest)
+            for sw, (bank, w, c, wa, first) in enumerate((("P5", "c15", 2.0 ** -15, "c2", "b1"), ("P1", "c2", 0.25, "c2", "valS"),
+                                                          ("P5", "If", 1.0, "If", "valS"))):
+                rest = A(bank, 0, V - VH)
+                mm(rest, A(wa), A("valS", VH, V), True, False)
                 if sw == 2:
+                    mm(A("P6"), A("Ib"), A("Db", 0, VH), True, True)
+                sum32(A(win), "invL", first, "mf", bank, w)
+                if sw == 2:
+                    tt(A("mf", VH, V), rest, A("Db", VH, V), ALU.mult)
+                    dma("s", ("out", "mu", VH, V), A("mf", VH, V))
+                    tt(A("mf", 0, VH), A("P6"), A("mf", 0, VH), ALU.mult)
+                    dma("y", ("out", "mu", 0, VH), A("mf", 0, VH))
                     break
-                act(A(banks[0]), A("mf", 0, 512))
-                export(A("mf"), "wbU")
+                act(A("mf", VH, V), rest, scale=1.0 / c)
+                export(A("mf"), "wbU", c)
                 xm = send(True)
-                act(A(banks[1], 0, V - 512), A("mf", 512, V))
-                nxt = ("P0", "P1") if sw == 0 else ("P4", "P5")
-                base(nxt, "If", "valS")
-                spread("W", "Cf", 0, banks, ALU.min, ((("P6",), ("P7",)), (("If", "mf", None), ("mIb", "nM", None)), AF.Relu, 0.0))
+                act(A("P0"), A("mf", 0, VH), scale=c)
+                if sw == 0:
+                    for k in range(SW):
+                        act(A("nM", k, NS, 4), A("Cf", NV + k, NC, 4), AF.Relu, bias=1.0, scale=-1.0)
+                for k in range(4):
+                    tt(A("W", k, NV, 4), A("P0"), A("Cf", k, NV, 4), ALU.min)
+                for k in range(SW, 4):
+                    tt(A("W", NV + k, NC, 4), rest, A("Cf", NV + k, NC, 4), ALU.min)
+                for k in range(SW):
+                    o = A("P%d" % (4 + 2 * (k & 1)), 0, V - VH)
+                    mm(o, A("mIb"), A("nM", k, NS, 4), True, False)
+                    mm(o, A(w), A("mf", VH, V), False, True)
+                    act(A("W", NV + k, NC, 4), o, AF.Relu)
                 for h, (lo, hi) in enumerate(HALF):
                     o = A("P%d" % (2 + h), 0, hi - lo)
                     if sw == 0:
                         tt(o, o, A("R", 4 * lo + 3, 4 * hi, 4), ALU.subtract)
                         act(o, o, AF.Relu, scale=2.0 ** -27)
                     else:
-                        tt(A("pO", lo, hi), A("pO", lo, hi), o, ALU.subtract)
+                        tt(A("pO", lo, hi), A("debtI", lo, hi), o, ALU.subtract)
                 if sw == 1:
                     dma("y", ("out", "pay", 0, V), A("pO"))
                 tt(A("W", NC, NX), turn(xm, "Bf"), A("Cf", NC, NX), ALU.min)
                 win = "W"
-                banks = nxt
             break
 
-        if t == 0:
-            act(A("one"), A("cm", 0, 512), scale=0.0, bias=1.0)
-            act(A("qIb"), A("Ib"), scale=0.25)
-            act(A("E4", 15, 143, 16), A("blk", 0, 128, 16), scale=4.0)
-            ts(A("tc"), A("ioA"), 144, ALU.add)
-            ts(A("pJ", 0, 1), A("pI"), 2, ALU.arith_shift_right, 3, ALU.bitwise_and)
-            ts(A("pJ", 1, 2), A("pI"), 3, ALU.bitwise_and)
-            ts(A("tc"), A("tc"), 127, ALU.bitwise_and)
-            cpy(A("col", 13, 15), A("pJ"))
-            ts(A("Bb"), A("tc"), 0, ALU.is_equal)
-            ts(A("thr"), A("thI"), 1.0 / 64, ALU.mult, 15.0, ALU.add)
         base(("P4", "P5"), "Ib", "one")
-        for k in range(4):
-            act(A("MA", NA * k, NA * k + NA), A("R", r0 + k, NC, 16), AF.Sign)
+        for h, (lo, hi) in enumerate(HALF):
+            for k in range(4 - len(SIDE0[h]), 4):
+                act(A("nM", 4 * lo + k, 4 * hi, 4), A("R", 4 * lo + k, 4 * hi, 4), AF.Relu, bias=1.0, scale=-1.0)
+        spread("C0b", "R", 0, ("P0", "P1"), ALU.min, (SIDE0, (("Ib", "Db", None), ("nIb", "nM", (0,))), AF.Relu, 0.0))
         if t == 0:
             act(A("i9", 0, 112), A("i9", 0, 112), bias=col(13))
             act(A("i9", 112, 126), A("i9", 112, 126), bias=col(0))
             act(A("iB"), A("i9", 112, 126))
             act(col(15), col(14), bias=float(DM))
-            act(A("sIb"), A("Ib"), scale=16.0)
-            act(A("cp", 0, DM), A("cm", 0, DM), scale=0.0)
-            act(A("sigT", 0, DM), A("cm", 0, DM), scale=0.0)
-            act(A("sigT", DM + NC, DM + NX), A("cm", 0, E), scale=0.0)
-            act(A("S14", 0, NA), A("cm", 0, NA), scale=0.0)
-            act(A("S14", NA + V, NA + V + E), A("cm", 0, E), scale=0.0)
-            act(A("actW", 0, 16), A("cm", 0, 16), scale=0.0)
-            act(A("actW", NA, 240), A("cm", 0, 16), scale=0.0)
-            act(A("c01"), A("ioC", 0, 16))
-            act(A("okF"), A("cm", 0, V), scale=0.0)
-            act(A("cIb"), A("Ib"), scale=0.375 / 4)
+            act(A("rIh"), A("Ib"), scale=-0.25)
         act(A("vF", 0, 14), A("i9", 112, 126), bias=float(3 - t), scale=4.0)
-        act(A("vF", 14, 28), A("i9", 112, 126), bias=float(DM + r0), scale=16.0)
+        act(A("vF", 14, 28), A("i9", 112, 126), bias=float(r0), scale=16.0)
         act(A("kk"), A("i9"), bias=float(1 - 256 * r0), scale=0.0)
-        act(A("nM"), A("R", 3, NC, 4), AF.Relu, bias=1.0, scale=-1.0)
-        spread("C0b", "R", 0, ("P0", "P1"), ALU.min, ((("P2",), ("P3",)), (("Ib", "Db", None), ("nIb", "nM", None)), AF.Relu, 0.0))
-        act(A("C0b", NC, NX), turn(x3, "Bb"))
         port0 = lambda r: DM + 16 * r + r0
         port4 = lambda r: DM + 16 * (r >> 2) + r0
         ports = lambda r: DM + 16 * (r >> 2) + r0 + (r & 3)
+        for k in range(4):
+            act(A("MA", NA * k, NA * k + NA), A("R", r0 + k, NC, 16), AF.Sign)
+        act(A("C0b", NC, NX), turn(x3, "Bb"))
         extract(A("P6", 0, 56), "EW", "invT", port4, 56, 64)
         extract(A("P6", 56, 70), "EE", "invT", port0, 14, 256)
-        gather16(A("C0b"), "Zb1", ("P4", "P5"), "mb1")
+        x4 = threats("C0b", "Z", ("P4", "P5"), "mb1")
         ts(A("g4U"), A("P6", 0, 56), col(15), ALU.add)
-        tt(A("ne"), A("P6", 56, 70), A("vF", 0, 14), ALU.not_equal)
+        tt(A("vdU"), A("P6", 56, 70), A("vF", 0, 14), ALU.not_equal)
         ts(A("wU"), A("P6", 56, 70), NA, ALU.add)
-        ts(A("xw"), A("P6", 56, 70), NA, ALU.add)
-        cpy(A("vdU"), A("ne"))
-        export(A("mb1"), "wbU")
-        x4 = send(True)
-        base(("P0", "P1"), "Ib", "one")
-        extract(A("P3", 0, 56), "E4", "MA", lambda r: r, 56, 16)
-        extract(A("P3", 56, 70), "EW", "invT", port0, 14, 256)
-        extract(A("P3", 80, 136), "EE", "invT", ports, 56, 64)
-        act(A("gw"), IND(A("sigT"), A("g4U")))
+        act(A("xw"), A("P6", 56, 70), bias=float(NA))
+        extract(A("P0", 0, 56), "E4", "MA", lambda r: r, 56, 16)
+        extract(A("P0", 56, 70), "EW", "invT", port0, 14, 256)
+        extract(A("P0", 80, 136), "EE", "invT", ports, 56, 64)
+        for c in (0, 28):
+            (cpy if c < 28 * GWV else act)(A("gw", 16 * c, 16 * c + DM), IND(A("sigT"), A("g4U", c, c + 28)))
         act(A("vdR"), IND(A("c01"), A("vdU")))
         for l in range(4):
-            act(A("mk", l, V, 4), A("Zb1", r0 + l, NC, 16))
-        spread("C1b", "C0b", 0, ("P4", "P5"), ALU.mult, ((("P2",), ("P7",)), (("Ib", "mb1", None), ("sIb", "C0b", (0,))), AF.Relu, -16.0))
-        tt(A("C1b", NC, NX), turn(x4, "Bb"), A("C0b", NC, NX), ALU.mult)
+            hand(A("mk", l, V, 4), A("Z", r0 + l, NC, 16))
         mm(A("P6", 0, 126), A("If"), A("kk"), True, False)
         extract(A("P6", 0, 56), "KS", "sigT", ports, 56, 64, False, False)
-        gather16(A("C1b"), "Zb2", ("P0", "P1"), "mb2")
-        tt(A("kI"), A("P3", 0, 56), A("kc"), ALU.add)
+        tt(A("kI"), A("P0", 0, 56), A("kc"), ALU.add)
         tt(A("kI", 0, 28), A("kI", 0, 28), A("kI", 28, 56), ALU.min)
         tt(A("kI", 0, 14), A("kI", 0, 14), A("kI", 14, 28), ALU.min)
         ts(A("kI", 0, 14), A("kI", 0, 14), 3, ALU.bitwise_and)
-        export(A("mb2", 0, V), "wbU")
-        x5 = send(True)
-        ts(A("ne"), A("kI", 0, 14), DM, ALU.add)
         tt(A("rF", 0, 14), A("kI", 0, 14), A("vF", 14, 28), ALU.add)
-        tt(A("rF", 14, 28), A("P3", 56, 70), A("ne"), ALU.add)
-        cpy(A("aU"), A("P3", 80, 136))
+        tt(A("rF", 14, 28), A("P0", 56, 70), A("kI", 0, 14), ALU.add)
+        cpy(A("aU"), A("P0", 80, 136))
         cpy(A("rU"), A("rF"))
-        act(A("vS"), IND(A("sigT"), A("rU")))
+        act(A("vS"), IND(A("sigT", DM, DM + NX), A("rU")))
+        spread("C1b", "C0b", 0, ("P4", "P5"), ALU.mult, (SIDE1, (("Ib", "mb1", None), ("sIb", "C0b", (0,))), AF.Relu, -16.0))
+        tt(A("C1b", NC, NX), turn(x4, "Bb"), A("C0b", NC, NX), ALU.mult)
+        base(("P0", "P1"), "Ib", "one")
+        x5 = threats("C1b", "Z2", ("P0", "P1"), "mb2")
         extract(A("P6", 56, 112), "KS", "gw", lambda r: r, 56, 16, False, False)
         extract(A("P6", 112, 126), "KI", "invT", port0, 14, 256, False)
-        extract(A("P3", 0, 28), "EX", "vS", lambda r: r, 28, 16)
-        extract(A("P3", 28, 56), "EE", "vS", lambda r: r, 28, 16)
+        extract(A("P4", 0, 28), "EX", "vS", lambda r: r, 28, 16)
+        extract(A("P4", 28, 56), "EE", "vS", lambda r: r, 28, 16)
         tt(A("n1"), A("P6", 0, 126), A("i9"), ALU.is_le)
         tt(A("n2"), A("P6", 0, 126), A("n1"), ALU.mult)
         cpy(A("cU"), A("n2"))
-        ts(A("sU"), A("P3", 0, 28), DM, ALU.add)
-        cpy(A("lU"), A("P3", 28, 56))
-        ts(A("xx", 28, 42), A("P3", 14, 28), DM, ALU.add)
-        ts(A("xx", 42, 56), A("P3", 0, 14), DM, ALU.add)
-        act(A("vC"), IND(A("cp"), A("sU")))
-        act(A("vL"), IND(A("Lq"), A("lU")), scale=0.25)
-        mm(A("P3", 0, DM), A("qIb"), A("vC"), True, True)
-        mm(A("P2", 0, NA), A("sIb"), A("Db", 3 - t, V, 4), True, False)
-        mm(A("P4", 0, NA), A("sIb"), A("vdR"), True, False)
-        mm(A("P4", 0, NA), A("NE"), A("invT", DM + r0, DM + NC, 16), False, False)
+        cpy(A("sU"), A("P4", 0, 56))
+        act(A("xx", 28, 42), A("P4", 14, 28), bias=float(DM))
+        act(A("xx", 42, 56), A("P4", 0, 14), bias=float(DM))
+        act(A("vC"), IND(A("cp", DM, DM + NX), A("sU", 0, 28)))
+        act(A("vL"), IND(A("Lq"), A("sU", 28, 56)))
+        mm(A("P5", 0, NA), A("sIb"), A("Db", 3 - t, V, 4), True, False)
         mm(A("P6", 0, 14), A("Ib"), A("iB"), True, False)
-        tt(A("yn", 0, NA), A("P3", 0, NA), A("vL", NA, DM), ALU.max)
-        tt(A("yn", NA, DM), A("P3", NA, DM), A("vL", 0, NA), ALU.max)
-        tt(A("P3", 0, DM), A("P3", 0, DM), A("vL"), ALU.max)
-        tt(A("yn"), A("yn"), A("P3", 0, DM), ALU.subtract)
-        act(A("dv"), A("yn", 0, NA), bias=12.0 / 128, scale=1.0 / 128)
-        tt(A("nw"), IND(A("S14"), A("wU")), A("yn", NA, DM), ALU.add)
+        mm(A("P4", 0, DM), A("nIb"), A("vC"), True, False)
+        mm(A("P4", 0, NA), A("Ih"), A("vL", NA, DM), False, False)
+        mm(A("P4", NA, DM), A("Ih"), A("vL", 0, NA), False, True)
+        act(A("yn"), A("P4", 0, DM), AF.Relu)
+        mm(A("P7", 0, DM), A("nIb"), A("vC"), True, False)
+        mm(A("P7", 0, DM), A("Ih"), A("vL"), False, True)
+        act(A("yo"), A("P7", 0, DM), AF.Relu, scale=1.0)
+        mm(A("P4", 0, DM), A("qIh"), A("yn"), True, False)
+        mm(A("P4", 0, DM), A("rIh"), A("yo"), False, True)
+        act(A("dv"), A("P4", 0, NA), bias=12.0 / 128, scale=1.0 / 128)
+        act(A("dw"), A("P4", NA, DM))
+        tt(A("nw"), IND(A("S14"), A("wU")), A("dw"), ALU.add)
+        mm(A("P3", 0, NA), A("sIb"), A("vdR"), True, False)
+        mm(A("P3", 0, NA), A("NE"), A("invT", DM + r0, DM + NC, 16), False, False)
         cpy(A("mb2", V, V + E), turn(x5, "Bb"))
         for lo, hi in ((0, 640), (640, V)):
             tt(A("z3", lo, hi), IND(A("mb2"), A("aU", lo // 16, hi // 16)), A("mk", lo, hi), ALU.mult)
             for l in range(4):
-                mm(A("P2", lo // 4, hi // 4), A("qIb"), A("z3", lo + l, hi, 4), False, l == 3 and hi == V)
-        ts(A("vote"), A("P2", 0, NA), A("thr"), ALU.is_ge)
-        mm(A("P4", 0, NA), A("blk"), A("vote"), False, True)
-        ts(A("actW", 1, NA + 1), A("P4", 0, NA), 24.5, ALU.is_ge)
-        mm(A("P5", 0, NA), A("sIb"), A("actW", 1, NA + 1), True, False)
+                mm(A("P5", lo // 4, hi // 4), A("qIb"), A("z3", lo + l, hi, 4), False, l == 3 and hi == V)
+        ts(A("vote"), A("P5", 0, NA), A("thr"), ALU.is_ge)
+        mm(A("P3", 0, NA), A("blk"), A("vote"), False, True)
+        ts(A("actW", 1, NA + 1), A("P3", 0, NA), 24.5, ALU.is_ge)
+        mm(A("P2", 0, NA), A("sIb"), A("actW", 1, NA + 1), True, False)
         act(A("cg", 2 * V, 9 * NA), IND(A("actW"), A("cU", 112, 126)))
-        mm(A("P5", 0, NA), A("nIb"), A("cg", 2 * V, 2 * V + NA), False, False)
-        for q, lo, hi in (("v", 0, 640), ("s", V, V + 512), ("v", 640, V), ("s", V + 512, V + 768), ("v", V + 768, 2 * V)):
+        mm(A("P2", 0, NA), A("nIb"), A("cg", 2 * V, 2 * V + NA), False, False)
+        for q, lo, hi in (("v", 0, 512), ("s", V, V + 512), ("v", 512, V), ("s", V + 512, V + 768), ("v", V + 768, 2 * V)):
             (cpy if q == "v" else act)(A("cg", lo, hi), IND(A("actW"), A("cU", lo // 16, hi // 16)))
             for j in range(4):
-                mm(A("P5", (lo % V) // 4, ((hi - 1) % V + 1) // 4), A("nIb"), A("cg", lo + j, hi, 4), False, hi == 2 * V and j == 3)
+                mm(A("P2", (lo % V) // 4, ((hi - 1) % V + 1) // 4), A("nIb"), A("cg", lo + j, hi, 4), False, hi == 2 * V and j == 3)
         okv = A("okF", 3 - t, V, 4)
-        ts(okv, A("P5", 0, NA), 15.5, ALU.is_ge, 128.0, ALU.mult)
+        ts(okv, A("P2", 0, NA), 15.5, ALU.is_ge, 128.0, ALU.mult)
         extract(A("P6", 0, 14), "E4", "okF", lambda r: 4 * r + 3 - t, 14, 64, False)
-        mm(A("P2", 0, NA), A("Ib"), okv, True, True)
-        tt(A("o1"), A("P6", 0, 14), A("xw"), ALU.min)
-        cpy(A("owU"), A("o1"))
-        tt(A("P2", 0, NA), A("P2", 0, NA), A("dv"), ALU.mult)
-        cpy(IND(A("S14"), A("owU")), A("nw"))
+        mm(A("P5", 0, NA), A("Ib"), okv, True, True)
+        tt(A("P5", 0, NA), A("P5", 0, NA), A("dv"), ALU.mult)
         sv = A("S14", NA + 3 - t, NA + V, 4)
-        tt(sv, A("P2", 0, NA), sv, ALU.add)
-        tt(A(snd()), IND(A("S14", NA, NA + V), A("xbU")), A("snd0"), ALU.min)
+        tt(sv, A("P5", 0, NA), sv, ALU.add)
+        tt(A("owU"), A("P6", 0, 14), A("xw"), ALU.min)
+        cpy(IND(A("S14"), A("owU")), A("nw"))
+        export(A("S14", NA, NA + V), "xbU")
         x1 = send(False)
-        act(A("xx", 0, 14), A("rF", 14, 28))
-        act(A("xx", 14, 28), A("rF", 0, 14))
+        act(A("xx", 0, 14), A("rF", 14, 28), bias=float(DM))
+        act(A("xx", 14, 28), A("rF", 0, 14), bias=float(DM))
         for j in range(4):
             act(A("o4", 14 * j, 14 * j + 14), A("P6", 0, 14), bias=float(NA * (j & 1)))
-        act(A("vN"), IND(A("invT"), A("sU")))
+        act(A("vN"), IND(A("invT", DM, DM + NX), A("sU", 0, 28)))
         for h, (lo, hi) in enumerate(HALF):
             act(A("P%d" % h, 0, hi - lo), A("Lq", lo, hi))
-        tt(A("o4"), A("o4"), A("xx"), ALU.min)
-        cpy(A("oU"), A("o4"))
+        tt(A("oU"), A("o4"), A("xx"), ALU.min)
         cpy(IND(A("sigT"), A("oU", 0, 28)), A("vS"))
-        load_cm()
-        extract(A("P7", 0, 224), "EE", "sigT", lambda r: DM + r, 224, 16)
+        for b, w, x, c in (("P7", "Ih", "e16", 1.0), ("P4", "nIb", "LB", -1.0)):
+            mm(A(b, 0, NA), A("dIb"), okv, True, False)
+            mm(A(b, 0, NA), A(w), A(x, 3 - t, V, 4), False, True)
+            act(A(x, 3 - t, V, 4), A(b, 0, NA), scale=c)
+        for b, lo, hi in (("P5", 0, 96), ("P6", 96, NA)):
+            extract(A(b, lo, hi), "EE", "sigT", lambda r: DM + 16 * lo + r, hi - lo, 16)
+            cpy(A("atO", lo, hi), A(b, lo, hi))
         for h, (lo, hi) in enumerate(HALF):
             tt(A("q1", lo, hi), A("P%d" % h, 0, hi - lo), A("S14", NA + lo, NA + hi), ALU.min)
-        cpy(IND(A("cp"), A("oU", 28, 56)), A("vC"))
-        cpy(A("atO"), A("P7", 0, 224))
-        cpy(IND(A("invT"), A("oU", 28, 56)), A("vN"))
+        for c in (0, 14):
+            cpy(IND(A("cp"), A("oU", 28 + c, 42 + c)), A("vC", 16 * c, 16 * c + NA))
+        for c in (0, 14):
+            cpy(IND(A("invT"), A("oU", 28 + c, 42 + c)), A("vN", 16 * c, 16 * c + NA))
     return ops
 
 
@@ -661,69 +705,138 @@ def plan():
     ops = build()
     deps = order(ops)
     pre = links(ops, deps)
-    tm = [cost(op, COST) for op in ops]
-    size = len(ops)
-    gap = [{m: tm[m][1] + COST["hop"] if m in deps[n] or ops[n][1] == "arrive" else tm[m][0] + 0.001 for m in pre[n]} for n in range(size)]
+    one = [cost(op, COST) for op in ops]
+    unit, members, tm = [], [], []
+    for n, op in enumerate(ops):
+        m = n - 1
+        if (op[1] == "mm" and ops[m][1] == "mm" and op[2][0][1] == ops[m][2][0][1] and op[2][2][1] == ops[m][2][2][1]
+                and tm[-1][0] + one[n][0] <= LUMP and not op[2][3] and deps[n] <= deps[members[-1][0]]):
+            members[-1].append(n)
+            tm[-1] = (tm[-1][0] + one[n][0],) * 2
+        else:
+            members.append([n])
+            tm.append((max(one[n][0], 0.001), one[n][1]))
+        unit.append(len(members) - 1)
+    size = len(members)
+    line_of = [ops[ms[0]][0] for ms in members]
+    gap = []
+    above = []
+    for u, ms in enumerate(members):
+        d = {}
+        for n in ms:
+            for m in pre[n]:
+                if unit[m] != u:
+                    w = tm[unit[m]][1] + COST["hop"] if m in deps[n] or ops[n][1] == "arrive" else tm[unit[m]][0] + 0.001
+                    d[unit[m]] = max(d.get(unit[m], 0.0), w)
+        far = 0
+        for m in d:
+            far |= above[m]
+        gap.append({m: w for m, w in d.items() if not far >> m & 1 or ops[members[m][0]][1] == "send"})
+        for m in d:
+            far |= 1 << m
+        above.append(far)
     post = [{} for n in range(size)]
     for n in range(size):
         for m, d in gap[n].items():
             post[m][n] = d
+    sends = [u for u in range(size) if ops[members[u][0]][1] == "send"]
 
     def place(turn, before, back):
-        busy = {}
+        busy = {q: ([], []) for q in set(line_of)}
         at = [0.0] * size
         for n in turn:
-            need = max(tm[n][0], 0.001)
-            t = tm[n][1] - need if back else 0.0
-            for m, d in before[n].items():
-                t = max(t, at[m] + max(tm[m][0], 0.001) + d - need if back else at[m] + d)
-            line = busy.setdefault(ops[n][0], [])
-            j = len(line)
-            while j > 0 and line[j - 1][1] > t:
+            need = tm[n][0]
+            if back:
+                t = tm[n][1] - need
+                for m, d in before[n].items():
+                    if at[m] + tm[m][0] + d - need > t:
+                        t = at[m] + tm[m][0] + d - need
+            else:
+                t = 0.0
+                for m, d in before[n].items():
+                    if at[m] + d > t:
+                        t = at[m] + d
+            first, end = busy[line_of[n]]
+            j = len(end)
+            while j > 0 and end[j - 1] > t:
                 j -= 1
-            while j < len(line) and t + need > line[j][0]:
-                t = max(t, line[j][1])
+            while j < len(end) and t + need > first[j]:
+                if end[j] > t:
+                    t = end[j]
                 j += 1
-            line.insert(j, (t, t + need))
+            first.insert(j, t)
+            end.insert(j, t + need)
             at[n] = t
         if back:
-            return [-(at[n] + max(tm[n][0], 0.001)) for n in range(size)]
+            return [-(at[n] + tm[n][0]) for n in range(size)]
         return at
+
+    def worth(at):
+        return max(at[n] + tm[n][1] for n in range(size)) + EARLY * sum(at[n] for n in sends)
 
     way = [t[1] for t in tm]
     for n in range(size - 1, -1, -1):
         for m, d in gap[n].items():
             way[m] = max(way[m], d + way[n])
     start = place(sorted(range(size), key=lambda k: (-way[k], k)), gap, False)
-    best = max(start[n] + tm[n][1] for n in range(size))
+    best = worth(start)
     now = start
     for rep in range(ROUNDS):
         late = place(sorted(range(size), key=lambda k: (-now[k], -k)), post, True)
         now = place(sorted(range(size), key=lambda k: (late[k], k)), gap, False)
-        end = max(now[n] + tm[n][1] for n in range(size))
-        if end < best:
-            best, start = end, now
-    seed = 12345
+        if worth(now) < best:
+            best, start = worth(now), now
+    seed = [12345]
+
+    def draw(k):
+        seed[0] = (seed[0] * 1103515245 + 12345) % 2147483648
+        return (seed[0] >> 8) * k >> 23
+
+    def held(at):
+        before = {}
+        last = {}
+        for n in sorted(range(size), key=lambda k: at[k]):
+            before[n] = last.get(line_of[n])
+            last[line_of[n]] = n
+        out = []
+        seen = set()
+        for n in sends + [max(range(size), key=lambda k: at[k] + tm[k][1])]:
+            while n is not None and n not in seen:
+                seen.add(n)
+                ready, by = 0.0, None
+                for m, d in gap[n].items():
+                    if at[m] + d > ready:
+                        ready, by = at[m] + d, m
+                if at[n] > ready + 0.01:
+                    by = m = before[n]
+                    while m is not None and at[m] + tm[m][0] > ready:
+                        out.append((n, m))
+                        m = before[m]
+                n = by
+        return out
+
+    pairs = held(start)
     for rep in range(TRIES):
-        seed = (seed * 1103515245 + 12345) % 2147483648
-        mid = best * (seed >> 8) / 8388608.0
-        shift = {}
-        key = []
-        for n in range(size):
-            name = (ops[n][0], ops[n][4][0][0] if ops[n][4] else "")
-            if name not in shift:
-                seed = (seed * 1103515245 + 12345) % 2147483648
-                u = (seed >> 8) / 8388608.0
-                shift[name] = (u - 0.15) * -40000.0 if u < 0.15 else (0.85 - u) * 40000.0 if u > 0.85 else 0.0
-            key.append(start[n] + (shift[name] if abs(start[n] - mid) < 7000 else 0.0))
-        for n in range(size):
-            for m in gap[n]:
-                key[n] = max(key[n], key[m] + 0.0001)
+        key = list(start)
+        for more in range(1 + draw(2)):
+            n, m = pairs[draw(len(pairs))]
+            if draw(3):
+                key[m] = key[n] + 0.5 + (tm[n][0] + 3000.0 * draw(3)) * draw(2)
+            else:
+                key[n] = key[m] - 0.5
+                for k in range(n, -1, -1):
+                    for j in post[k]:
+                        if key[j] <= key[k]:
+                            key[k] = key[j] - 0.0001
+        for k in range(size):
+            for j in gap[k]:
+                if key[j] >= key[k]:
+                    key[k] = key[j] + 0.0001
         now = place(sorted(range(size), key=lambda k: (key[k], k)), gap, False)
-        end = max(now[n] + tm[n][1] for n in range(size))
-        if end <= best:
-            best, start = end, now
-    seq = sorted(range(size), key=lambda k: (start[k], k))
+        if worth(now) <= best:
+            best, start = worth(now), now
+            pairs = held(start)
+    seq = [n for u in sorted(range(size), key=lambda k: (start[k], k)) for n in members[u]]
     new = {m: j for j, m in enumerate(seq)}
     return [ops[m] for m in seq], [set(new[k] for k in deps[m]) for m in seq]
 
@@ -746,6 +859,10 @@ def rank_program(g, core, T, topo):
     waits = []
     for n, need in enumerate(deps):
         q = ops[n][0]
+        if ops[n][1] == "arrive":
+            waits.append([])
+            cover[n] = {n: n}
+            continue
         keep = []
         for m in sorted(need, reverse=True):
             if ops[m][1] == "send":
@@ -758,7 +875,7 @@ def rank_program(g, core, T, topo):
                 known[q][k] = max(known[q].get(k, -1), c)
         waits.append(keep)
         cover[n] = dict(known[q])
-        cover[n][q if ops[n][1] not in ("dma", "arrive") else n] = n
+        cover[n][q if ops[n][1] != "dma" else n] = n
     wanted = set(m for keep in waits for m in keep)
 
     def ap(x):
@@ -777,6 +894,9 @@ def rank_program(g, core, T, topo):
     waited = {k: {} for k in queue}
     total = {}
     for n, (q, kind, args, rd, wr) in enumerate(ops):
+        if kind == "arrive":
+            mark[n] = ("arr%d" % args[0], total["arr%d" % args[0]])
+            continue
         e = queue[q]
         need = {}
         for m in waits[n]:
@@ -786,9 +906,6 @@ def rank_program(g, core, T, topo):
             if waited[q].get(s, 0) < c:
                 e.wait_ge(T.sem[s], c)
                 waited[q][s] = c
-        if kind == "arrive":
-            mark[n] = ("arr%d" % args[0], total["arr%d" % args[0]])
-            continue
         if kind == "send":
             x, back = args
             tr = []
@@ -829,7 +946,7 @@ def rank_program(g, core, T, topo):
         elif kind == "fill":
             ins = e.memset(a[0], a[1])
         elif kind == "sel":
-            ins = e.affine_select(a[0], a[0], a[1], a[2], a[3], a[4], a[5])
+            ins = e.affine_select(a[0], a[6], a[1], a[2], a[3], a[4], a[5])
         elif SCRATCH[args[0][1]][2] == I32:
             ins = e.iota(a[0], a[1], a[2], a[3])
         else:

@@ -5,6 +5,7 @@ from concourse.mybir import AluOpType as ALU, ActivationFunctionType as AF
 V, X, E, NC, NX, NA = 896, 128, 384, 3584, 3968, 224
 RO = 2
 VH = 512
+VC = 512
 NV = 4 * VH
 NS = NC - NV
 DM = 448
@@ -12,65 +13,82 @@ F32, BF, F16, I32, U16 = "float32", "bfloat16", "float16", "int32", "uint16"
 XDT = [F16] + [F16, F32, BF, BF, BF] * RO + [F16, F32, F32, F32, F32]
 
 _SB = {
-    "sigI": (248, I32), "lstU": (248, U16), "sigL": (224, U16), "atO": (224, U16), "xbU": (24, U16),
-    "invL": (248, U16), "wbU": (24, U16), "ta": (256, I32), "tb": (224, F32),
+    "sc": (NA + 248, I32), "lstU": (248, U16), "sigL": (224, U16), "atO": (224, U16), "xbU": (24, U16),
+    "invL": (248, U16), "wbU": (24, U16), "w4U": (96, U16), "invW": (96, U16), "zW": (4 * E, BF), "gT": (4 * E, BF),
+    "cw": (E, BF), "mw": (E, BF), "qBb": (128, BF), "ta": (256, I32),
     "debtI": (V, I32), "cashI": (V, I32), "thI": (1, I32), "thr": (1, F32), "colS": (NX, BF), "valS": (V, F32),
     "Lq": (V + E, F32), "e16": (V, F16), "LB": (V, F16), "cm": (NC, BF),
-    "S14": (NA + V + E, F32), "q1": (V + E, F32), "q2": (V, F32), "y16": (NC, F16), "W": (NX, F32), "R": (NC, F32),
-    "rw": (E, F32), "Db": (V, BF), "C0b": (NX, BF), "Z": (NC, BF), "mb1": (V, BF), "mb2": (V + E, BF), "Cf": (NX, F32), "Rs": (NS, F32),
+    "S14": (NA + V + E, F32), "q1w": (NA + V + E, F32), "q2": (V, F32), "y16": (NC, F16), "W": (NX, F32), "R": (NC, F32),
+    "rw": (E, F32), "Db": (V, BF), "C0b": (NX, BF), "Z": (NC, BF), "mb1": (V, BF), "mb2": (V + 16, BF), "w5": (16 + E, BF), "C1b": (NX, BF), "aW": (56, U16), "Cf": (NX, F32), "Rs": (1792, F32),
     "vinit": (NX, BF), "invT": (DM + NX, BF), "sigT": (DM + NX, BF), "cp": (DM + NX, BF),
-    "zb": (128, BF), "zf": (128, F32), "ioC": (256, F32), "tf": (256, F32), "pI": (1, I32), "pJ": (2, I32), "OH": (16, F32),
+    "zb": (128, BF), "zf": (128, F32), "ioC": (256, F32), "pI": (1, I32), "pJ": (2, I32), "OH": (16, F32),
     "col": (24, F32), "colB": (4, BF), "Ib": (128, BF), "nIb": (128, BF), "qIb": (128, BF), "sIb": (128, BF), "one": (VH, BF),
     "qIh": (128, F16), "Ih": (128, F16), "If": (128, F32), "nIf": (128, F32), "Fh": (128, F16), "Ff": (128, F32),
-    "c15": (128, F32), "c2": (128, F32), "uIb": (128, BF), "mIb": (128, BF),
-    "aIb": (128, BF), "Bb": (128, BF), "Bf": (128, F32), "mats": (6 * 144 + 256, BF), "c01": (16, BF), "blkT": (256, BF),
+    "c15": (128, F32), "c2": (128, F32), "uIb": (128, BF), "mIb": (128, BF), "pIb": (128, BF), "pBb": (128, BF),
+    "aIb": (128, BF), "Bb": (128, BF), "Bf": (128, F32), "mats": (9 * 144 + 256, BF), "c01": (16, BF), "blkT": (256, BF),
     "dIb": (128, BF), "i9": (126, F32), "iB": (14, BF), "kc": (56, F32), "kk": (126, F32),
-    "MA": (V, BF), "mk": (V, BF), "z3": (V, BF), "aU": (56, U16), "vF": (28, F32), "ne": (14, F32),
+    "MA": (V, BF), "mk": (V, BF), "z3": (V, BF), "aU": (56, U16), "vF": (28, F32),
     "kI": (56, I32), "n1": (126, F32), "n2": (126, F32), "cU": (126, U16), "wU": (14, U16), "vdU": (14, U16),
     "g4U": (56, U16), "rF": (28, F32), "rU": (28, U16), "sU": (56, U16),
     "vS": (DM, BF), "vN": (DM, BF), "vC": (DM, BF), "rIh": (128, F16),
     "vdR": (NA, BF), "vote": (NA, BF), "actW": (240, BF), "okF": (V, BF),
-    "xw": (14, F32), "xx": (56, F32), "o1": (14, F32), "o4": (56, F32), "owU": (14, U16), "oU": (56, U16),
+    "xw": (14, F32), "xx": (56, F32), "o4": (56, F32), "owU": (14, U16), "oU": (56, U16),
 }
-ALIAS = {"C1b": ("vinit", 0, NX), "Z2": ("colS", 0, NC), "cg": ("colS", 0, 9 * NA), "gw": ("z3", 0, V), "mf": ("Lq", 0, V),
+ALIAS = {"tb": ("Rs", 0, NA), "tf": ("Rs", NA, 256), "Z2": ("colS", 0, NC), "cg": ("colS", 0, 9 * NA), "u0": ("q1w", NA, V), "q1": ("q1w", NA, V + E), "nq": ("Rs", DM + NA, NA), "gw": ("z3", 0, V), "mf": ("Lq", 0, V),
          "vL": ("y16", 0, DM), "yn": ("y16", DM, DM), "yo": ("y16", 2 * DM, DM), "dv": ("Rs", 0, NA), "dw": ("Rs", NA, NA), "nw": ("Rs", DM, NA),
-         "pO": ("q2", 0, V), "u0": ("q1", 0, V), "vw": ("q1", V, E), "b1": ("S14", 0, VH), "nM": ("Z", 0, NC),
+         "pO": ("q2", 0, V), "vw": ("q1w", NA + V, E), "Lh": ("y16", NC - V, V), "b1": ("S14", 0, VH), "nM": ("Z", 0, NC),
          "EX": ("mats", 0, 144), "EE": ("mats", 144, 144), "EW": ("mats", 288, 144), "KI": ("mats", 432, 144), "KS": ("mats", 576, 144),
-         "E4": ("mats", 720, 144), "NE": ("mats", 864, 128), "blk": ("mats", 992, 128)}
+         "E4": ("mats", 720, 144), "NE": ("mats", 864, 128), "blk": ("mats", 992, 128),
+         "XS": ("mats", 1120, 144), "ES": ("mats", 1264, 144), "EP": ("mats", 1408, 144), "se": ("mk", 0, V),
+         "sigI": ("sc", NA, 248), "sd": ("cashI", 0, DM)}
 for _d, _s in ((F16, "h"), (F32, "f"), (BF, "b")):
     _k = [i for i, d in enumerate(XDT) if d == _d]
     _SB["snd" + _s] = (E * len(_k), _d)
-    _SB["lnd" + _s] = (E * len(_k), _d)
+    if _d != BF:
+        _SB["lnd" + _s] = (E * len(_k), _d)
     for _j, _i in enumerate(_k):
         ALIAS["snd%d" % _i] = ("snd" + _s, E * _j, E)
-        ALIAS["lnd%d" % _i] = ("lnd" + _s, E * _j, E)
+        ALIAS["lnd%d" % _i] = ("lnd" + _s, E * _j, E) if _d != BF else (("C0b", NC, E), ("C1b", NC, E), ("w5", 16, E))[_j % 3]
+ALIAS.update({"lnd13": ("Cf", NC, E), "lnd14": ("S14", VH + E, E), "snd13": ("Lq", V, E)})
+_SB["sndf"] = (E * 5, F32)
+_SB["lndf"] = (E * 4, F32)
+ALIAS.update({"snd14": ("sndf", 3 * E, E), "snd15": ("sndf", 4 * E, E), "lnd15": ("lndf", 3 * E, E)})
 SCRATCH = {k: ("sbuf", [128, n], d) for k, (n, d) in _SB.items()}
 for _i in range(8):
     SCRATCH["P%d" % _i] = ("psum", [128, 512], F32)
-_DMAS = ["d%d" % i for i in range(10)]
+_DMAS = ["d%d" % i for i in range(16)]
+SHIFTED = ((0, 1024), (1024, 2048), (2048, 2816), (2816, NC))
 SEMAPHORES = ["sv", "ss", "sp", "sg", "sent"] + ["arr%d" % i for i in range(len(XDT))] + _DMAS
 
 HALF = ((0, VH), (VH, V))
-CH16 = (("v", 0, 768), ("s", 768, 1536), ("v", 1536, 2048), ("s", 2048, 2816), ("v", 2816, 3328), ("s", 3328, NC))
+CH16 = (("v", 0, 512), ("s", 512, 1280), ("v", 1280, 2048), ("s", 2048, 2816), ("v", 2816, 3072), ("s", 3072, NC))
+CHW = (("v", 0, 512), ("s", 512, 1024), ("v", 1024, 1280), ("s", 1280, 4 * E))
+FIRST = ((1, 1), (1, 1))
 CH3 = (("v", 0, 256), ("s", 256, 512), ("v", 512, 1024), ("s", 1024, 1536), ("v", 1536, 2048), ("s", 2048, 2560), ("s", 2560, 3072),
-       ("s", 3072, NC))
+       ("s", 3072, 3328), ("v", 3328, NC))
 SIDEW = ((("P4",), ("P5",)), (("P4", "P5"), ("P6",)))
-SIDE0 = (("P2",), ("P3",))
-SIDE1 = (("P2", "P3"), ("P2", "P3"))
+SIDE0 = ((), ())
+SIDE1 = ((), ())
 CH1 = (("v", 0, 512), ("o", 1024, 1536), ("v", 512, 1024), ("o", 1536, 2048), ("t", 2048, 2560), ("o", 2560, 3072), ("o", 3072, NC))
 CH2 = ((("v", 0, 512), ("o", 1024, 1536), ("v", 512, 1024), ("t", 1536, 2048), ("t", 2048, 2560), ("t", 2560, 3072), ("t", 3072, NC)),
-       (("t", 0, 512), ("v", 512, 1024), ("t", 1024, 1536), ("t", 1536, 2048), ("t", 2048, 2560), ("t", 2560, 3072), ("v", 3072, NC)))
+       (("t", 0, 512), ("v", 512, 1024), ("t", 1024, 1536), ("t", 1536, 2048), ("t", 2048, 2560), ("t", 2560, 2880), ("v", 2880, NC)))
 ADD3 = (1, 2)
 GWV = 0
 CPV = (1, 3, 5)
+CHG = (("v", 0, 256), ("s", V, V + 384), ("v", 256, 640), ("v", 640, V), ("s", V + 384, V + 768), ("v", V + 768, 2 * V))
+EVAC = 1
+READY = ((), (), ())
+CMV = 1024
 SF, SW = 2, 1
-CH32 = ((0, 0, 192), (0, 192, 384), (1, 0, 384), (2, 0, 384), (3, 0, 256), (3, 256, 384))
-PIECE = 16
-COST = dict(gather=1.56, fused=1.75, scatter=3.8, pe=0.56, flight=4000.0, hop=90.0, call=60.0)
+PIECE = 24
+COST = dict(gather=1.75, fused=1.85, scatter=4.2, pe=0.56, flight=3600.0, hop=90.0, call=60.0)
+COST2 = dict(gather=1.4, fused=1.6, scatter=3.5, pe=0.6, flight=4500.0, hop=100.0)
+SECOND = 1.0
 ROUNDS = 6
-TRIES = 20000
+TRIES, RUNS = 24000, 6
 LUMP = 650.0
-EARLY = 0.05
+SLACK = 5.0
+EARLY = 0.01
 
 
 def A(name, a=0, b=None, step=1):
@@ -152,7 +170,7 @@ def build():
         return "snd%d" % nx[0]
 
     def send(back):
-        put("g", "send", None, [A(snd())], (nx[0], back))
+        put("g", "send", A("lnd%d" % (nx[0] + 1)) if nx[0] + 1 < len(XDT) else None, [A(snd())], (nx[0], back))
         nx[0] += 1
         return nx[0] - 1
 
@@ -160,13 +178,21 @@ def build():
         ts(A(snd(), 0, 192), IND(win, A(lst, 0, 12)), scale, ALU.mult)
         act(A(snd(), 192, E), IND(win, A(lst, 12, 24)), scale=scale)
 
-    def arrive(n):
-        ops.append(("a", "arrive", (n,), [], span(A("lnd%d" % n))))
+    def arrive(n, *ready):
+        ops.append(("a", "arrive", (n,), [y for x in ready for y in span(A(x))], span(A("lnd%d" % n))))
 
     def turn(n, w):
         arrive(n)
         mm(A("P7", 0, E), A(w), A("lnd%d" % n), True, True)
         return A("P7", 0, E)
+
+    def halves(n, w, bank, *ready):
+        arrive(n, *ready)
+        out = []
+        for b, lo in (("P7", 0), (bank, E // 2)):
+            mm(A(b, 0, E // 2), A(w), A("lnd%d" % n, lo, lo + E // 2), True, True)
+            out.append((A(b, 0, E // 2), NC + lo, NC + lo + E // 2))
+        return out
 
     def extract(out, w, tab, first, n, step, start=True, stop=True):
         for r in range(16):
@@ -196,6 +222,7 @@ def build():
     dma("y", A("sigI", 0, 224), ("in", "sig"))
     dma("s", A("colS", 0, NC), ("in", "coll"))
     dma("y", A("cashI"), ("in", "cash"))
+    dma("y", A("sigT", DM, DM + NC), ("in", "coll"))
     dma("y", A("thI"), ("in", "th"))
     dma("y", A("valS"), ("in", "val"))
     iota(A("pI"), [[0, 1]], 0, 1)
@@ -207,6 +234,7 @@ def build():
     diag("nIf", -1.0)
     zero(A("mats", 0, 496))
     zero(A("mats", 496, 992))
+    zero(A("mats", 1120, 1552))
     zero(A("invT", 0, DM))
     zero(A("colS", NC, NX))
     ts(A("pJ", 0, 1), A("pI"), 15, ALU.bitwise_and)
@@ -227,7 +255,7 @@ def build():
     act(A("Ih"), A("Ib"))
     ts(A("ta", 0, 24), A("sigI", 224, 248), 2, ALU.arith_shift_right)
     cpy(A("xbU"), A("ta", 0, 24))
-    ts(A(snd()), IND(A("debtI"), A("xbU")), 0.25, ALU.mult, -128.0, ALU.add)
+    act(A(snd()), IND(A("debtI"), A("xbU")), bias=-128.0, scale=0.25)
     x0 = send(False)
     ts(A("tf"), A("ioC"), col(2), ALU.mult, col(3), ALU.add)
     cpy(A("lstU"), A("sigI"))
@@ -239,38 +267,49 @@ def build():
     ts(A("vinit", 256, 512), A("vinit", 0, 256), A("colB", 0, 1), ALU.add)
     ts(A("vinit", 512, 1024), A("vinit", 0, 512), A("colB", 1, 2), ALU.add)
     tt(A("tb"), A("tb"), A("P6", 0, 224), ALU.max)
-    act(A("cm", 1024, NC), A("colS", 1024, NC), bias=-128.0)
     cpy(A("atO"), A("tb"))
     act(A("e16"), A("cashI"))
-    act(A("cm", 0, 1024), A("colS", 0, 1024), bias=-128.0)
-    ts(A("vinit", 1024, 2048), A("vinit", 0, 1024), A("colB", 2, 3), ALU.add)
+    for lo, hi in SHIFTED:
+        if lo >= CMV:
+            ts(A("cm", lo, hi), A("colS", lo, hi), -128.0, ALU.add)
+        else:
+            act(A("cm", lo, hi), A("colS", lo, hi), bias=-128.0)
+    act(A("vinit", 1024, 2048), A("vinit", 0, 1024), bias=col(6))
     act(col(8), oh(7), bias=col(2), scale=0.75)
     act(col(9), col(8), bias=-0.5, scale=0.5)
     act(col(10), col(4), bias=oh(6), scale=14.0)
     act(col(12), oh(4), bias=col(10), scale=4.0)
     act(col(11), oh(0), bias=col(12))
     act(A("tf"), A("ioC"), bias=col(9), scale=col(8))
-    ts(A("vinit", 2048, NC), A("vinit", 0, NC - 2048), A("colB", 3, 4), ALU.add)
+    for lo in (2048, 2816):
+        act(A("vinit", lo, lo + 768), A("vinit", lo - 2048, lo - 1280), bias=col(7))
     cpy(A("ta"), A("tf"))
     cpy(A("blkT"), A("ta"))
     act(A("vinit", NC, NC + 256), A("blkT"), bias=col(10))
     act(A("vinit", NC + 256, NX), A("blkT", 0, 128), bias=col(11))
     for c in range(0, 248, PIECE):
         cpy(IND(A("invT", DM, DM + NX), A("lstU", c, min(c + PIECE, 248))), A("vinit", 16 * c, 16 * min(c + PIECE, 248)))
-    for c in range(0, 224, 56):
-        act(A("sigT", DM + 16 * c, DM + 16 * c + V), IND(A("vinit"), A("lstU", c, c + 56)))
+    cpy(A("sc", 0, NA), A("atO"))
+    for j, (op, c) in enumerate(((ALU.arith_shift_right, 4), (ALU.bitwise_and, 15))):
+        ts(A("sd"), A("sc", 0, DM), c, op)
+        act(A("se", DM * j, DM * j + DM), A("sd"))
+    for row, j in ((2, 0), (0, 1), (3, 2), (1, 3)):
+        dma("y", A("sigT", DM, DM + NC) + (row,), A("se", NA * j, NA * j + NA))
     diag("nIb", -1.0)
     diag("qIb", 0.25)
+    act(A("Lh"), A("Lq", 0, V))
+    iota(A("one"), [[0, VH]], 1, 0)
     for h, (lo, hi) in enumerate(HALF):
         o = A("P%d" % h, 0, hi - lo)
         mm(o, A("qIh"), A("e16", lo, hi), True, False)
         for k in range(4):
             mm(o, A("qIb"), A("colS", 4 * lo + k, 4 * hi, 4), False, False)
-        mm(o, A("nIf"), A("Lq", lo, hi), False, True)
+        mm(o, A("nIb"), A("Lh", lo, hi), False, True)
         act(A("LB", lo, hi), o, scale=-4.0, bias=512.0)
     fill(A("mats", 992, 1120), 1.0)
     for w, rows in (("EX", ((0, 256), (1, 1))), ("EE", ((4, 64), (7, 1))), ("EW", ((0, 256), (5, 4))),
-                    ("KI", ((0, 16), (2, 1), (3, -4096), (5, 1024))), ("KS", ((0, 16), (1, 256), (2, 1), (3, -4096)))):
+                    ("KI", ((0, 16), (2, 1), (3, -4096), (5, 1024))), ("KS", ((0, 1), (1, 256))),
+                    ("XS", ((0, 16), (1, 1))), ("ES", ((2, 16), (3, 1))), ("EP", ((0, 16), (2, 1), (3, -3584), (5, 896)))):
         for r, c in rows:
             select(A(w, 15, 143, 16), [[-16, 8]], ALU.not_equal, float(c), -r, 1)
     select(A("NE"), [[-16, 8], [0, 16]], ALU.not_equal, -64.0, -6, 1)
@@ -314,12 +353,13 @@ def build():
 
     def sum32(win, lst, first, out, bank, w):
         for k in range(4):
-            for lo, hi in ((0, VH // 2), (VH // 2, VH)):
+            for lo, hi in ((0, 256), (256, VC)):
                 tt(A(out, lo, hi), IND(win, part(lst, k, lo, hi)), A(out if k else first, lo, hi), ALU.add)
-        for k, lo, hi in CH32:
-            r = A("Rs", (V - VH) * k + lo, (V - VH) * k + hi)
-            act(r, IND(win, part(lst, k, VH + lo, VH + hi)))
-            mm(A(bank, lo, hi), A(w), r, False, (k, lo, hi) == CH32[-1])
+        n = V - VC
+        for k, lo, hi in ((0, 0, 192), (0, 192, n), (1, 0, n), (2, 0, n), (3, 0, 256), (3, 256, n)):
+            r = A("Rs", n * k + lo, n * k + hi)
+            act(r, IND(win, part(lst, k, VC + lo, VC + hi)))
+            mm(A(bank, lo, hi), A(w), r, False, k == 3 and hi == n)
 
     def base(banks, w, x):
         for h, (lo, hi) in enumerate(HALF):
@@ -349,12 +389,28 @@ def build():
                     mm(o, A(w), src, j == 0, j == len(side[1]) - 1)
                 act(A(out, 4 * lo + k, 4 * hi, 4), o, side[2], bias=side[3])
 
-    def threats(win, out, banks, mout):
-        gather(A(win), "invL", CH16, out, 1.0, banks, "qIb", (4, 4))
-        cpy(A(mout, 0, VH), A(banks[0]))
-        act(A(mout, VH, V), A(banks[1], 0, V - VH))
-        export(A(mout, 0, V), "wbU")
+    def masked_out(x, mask, w, bias):
+        mm(A("P7", 0, E), A(w), A(mask), True, False)
+        cpy(A("cw", 0, 192), IND(x, A("wbU", 0, 12)))
+        act(A("cw", 192, E), IND(x, A("wbU", 12, 24)))
+        mm(A("P7", 0, E), A("Bb"), A("cw"), False, True)
+        act(A(snd()), A("P7", 0, E), AF.Relu, bias=bias)
         return send(True)
+
+    def threats(win, out, banks, mout, mask, first):
+        if first:
+            mm(A("P7", 0, E), A("sIb"), A(mask), True, False)
+            for q, lo, hi in CHW:
+                (cpy if q == "v" else act)(A("zW", lo, hi), IND(A(win), A("invW", lo // 16, hi // 16)))
+                for l in range(4):
+                    mm(A("P7", lo // 4, hi // 4), A("qBb"), A("zW", lo + l, hi, 4), False, hi == 4 * E and l == 3)
+            act(A(snd()), A("P7", 0, E), AF.Relu, bias=-15.0)
+            x = send(True)
+        gather(A(win), "invL", CH16, out, 1.0, banks, "qIb", (4, 4))
+        for h, (lo, hi) in enumerate(HALF):
+            if mout == "mb2" or not first or SIDE1[h]:
+                (act if h or EVAC else cpy)(A(mout, lo, hi), A(banks[h], 0, hi - lo))
+        return x if first else masked_out(A(mout, 0, V), mask, "sIb", -16.0)
 
     act(A("Lq", V, V + E), turn(x0, "Fh"))
     claim_sweep(A("Lq"), "q1", CH1, False)
@@ -362,30 +418,26 @@ def build():
     x1 = send(False)
     act(A("S14", NA, NA + VH), A("P0"))
     act(A("S14", NA + VH, NA + V), A("P1", 0, V - VH))
-    cpy(A("sigL"), A("sigI", 0, NA))
-    iota(A("one"), [[0, VH]], 1, 0)
     zero(A("c01"))
     select(A("c01"), [[-1, 16]], ALU.is_ge, 1.0, 0, 0)
-    for w, c, shift in (("If", 1.0, 0), ("aIb", 2.0 ** 27, 0), ("Bb", 1.0, -16), ("sIb", 16.0, 0),
+    for w, c, shift in (("If", 1.0, 0), ("aIb", 2.0 ** 27, 0), ("Bb", 1.0, -16), ("sIb", 16.0, 0), ("qBb", 0.25, -16),
                         ("dIb", 0.375, 0), ("Bf", 1.0, -16), ("c15", 2.0 ** -15, 0),
-                        ("c2", 0.25, 0), ("uIb", 2.0 ** 11, 0), ("mIb", -2.0 ** 19, 0)):
+                        ("c2", 0.25, 0), ("uIb", 2.0 ** 11, 0), ("mIb", -2.0 ** 19, 0), ("pIb", 2.0 ** 19, 0),
+                        ("pBb", 2.0 ** 19, -16)):
         diag(w, c, shift)
-    for w, lo, hi in (("cp", 0, DM), ("sigT", 0, DM), ("sigT", DM + NC, DM + NX), ("S14", 0, NA), ("S14", NA + V, NA + V + E),
-                      ("actW", 0, 16), ("actW", NA, 240), ("okF", 0, DM), ("okF", DM, V)):
+    for w, lo, hi in (("cp", 0, DM), ("sigT", 0, DM), ("sigT", DM + NC, DM + NX), ("S14", 0, NA), ("q1w", 0, NA), ("S14", NA + V, NA + V + E),
+                      ("actW", 0, 16), ("actW", NA, 240), ("mb2", V, V + 16), ("w5", 0, 16), ("okF", 0, DM), ("okF", DM, V)):
         zero(A(w, lo, hi))
     act(A("E4", 15, 143, 16), A("blk", 0, 128, 16), scale=4.0)
     ts(A("pJ", 0, 1), A("pI"), 2, ALU.arith_shift_right, 3, ALU.bitwise_and)
     ts(A("pJ", 1, 2), A("pI"), 3, ALU.bitwise_and)
     cpy(A("col", 13, 15), A("pJ"))
-    ts(A("thr"), A("thI"), 1.0 / 64, ALU.mult, 15.0, ALU.add)
+    act(A("thr"), A("thI"), bias=15.0, scale=1.0 / 64)
 
     for t in range(RO + 1):
         close = t == RO
         r0 = 4 * (3 - t)
-        if t == 0:
-            act(A("q1", V, V + E), turn(x1, "Fh"))
-        else:
-            tt(A("q1", V, V + E), turn(x1, "Fh"), A("Lq", V, V + E), ALU.min)
+        act(A("q1", V, V + E), turn(x1, "Fh"))
         if t == 0:
             for lo, hi in ((0, 128), (128, 248)):
                 extract(A("P7", lo, hi), "EX", "invT", lambda r: DM + 16 * lo + r, hi - lo, 16)
@@ -398,7 +450,7 @@ def build():
                 else:
                     act(o, x, bias=-128.0)
         else:
-            extract(A("P7", 0, NA), "EX", "sigT", lambda r: DM + r, NA, 16)
+            extract(A("P7", 0, NA), "XS", "sigT", lambda r: DM + NA * r, NA, 1)
             cpy(A("sigL"), A("P7", 0, NA))
         claim_sweep(A("q1"), "q2", CH2[min(t, 1)], True)
         export(A("q2"), "xbU")
@@ -409,24 +461,42 @@ def build():
         spread("W", "cp", DM, ("P0", "P1"), ALU.subtract, (SIDEW[min(t, 1)], (("If", "q2", None), ("nIb", "cp", (DM,))), AF.Identity, 0.0))
         extract(A("P6", 256, 280), "EE", "invT", lambda r: DM + NC + r, 24, 16)
         cpy(A("wbU"), A("P6", 256, 280))
+        if not close and max(FIRST[t]):
+            extract(A("P6", 288, 384), "EW", "invT", lambda r: DM + NC + (r >> 2), 96, 4)
+            ts(A("w4U"), A("P6", 288, 384), col(14), ALU.add)
+            for c in range(0, 96, 32):
+                act(A("gT", 16 * c, 16 * c + 512), IND(A("invT", DM, DM + NX), A("w4U", c, c + 32)))
         if close:
             cpy(A("invL", 0, NA), shares("P6", "invT"))
-            act(A("b1"), A("valS", 0, VH), scale=2.0 ** 13)
+            act(A("b1", 0, VC), A("valS", 0, VC), scale=2.0 ** 13)
         elif t > 0:
             extract(A("P6", 0, NA), "EX", "invT", lambda r: DM + r, NA, 16)
             cpy(A("invL", 0, NA), A("P6", 0, NA))
-        tt(A("W", NC, NX), turn(x2, "Ff"), A("cp", DM + NC, DM + NX), ALU.subtract)
-        gather(A("W"), "sigL", CH3, "R", 2.0 ** 27, ("P2", "P3"), "nIf", ADD3)
-        act(A("rw"), A("W", NC, NX), AF.Relu, scale=2.0 ** 27)
+        for x, lo, hi in halves(x2, "Ff", "P0", *READY[0]):
+            tt(A("W", lo, hi), x, A("cp", DM + lo, DM + hi), ALU.subtract)
+        gather(A("W"), "sigL" if t else "lstU", CH3, "R", 2.0 ** 27, ("P2", "P3"), "nIf", ADD3)
         if close:
+            act(A("rw"), A("W", NC, NX), AF.Relu, scale=2.0 ** 27)
             tt(A("vw"), IND(A("valS"), A("wbU")), A("rw"), ALU.min)
+            mm(A("P7", 0, E), A("Bf"), A("vw"), True, False)
+        else:
+            act(A("mw"), A("W", NC, NX), AF.Sign)
+            if max(FIRST[t]):
+                extract(A("P6", 0, 96), "EX", "gT", lambda r: r, 96, 16)
+                cpy(A("invW"), A("P6", 0, 96))
         for h, (lo, hi) in enumerate(HALF):
             o = A("P%d" % (2 + h), 0, hi - lo)
             for k in range(ADD3[h], 3):
                 tt(o, o, A("R", 4 * lo + k, 4 * hi, 4), ALU.subtract)
             tt(A("Db", lo, hi), o, A("R", 4 * lo + 3, 4 * hi, 4), ALU.is_gt)
-        tt(A(snd()), IND(A("Db"), A("wbU")), A("vw" if close else "rw"), ALU.mult if close else ALU.min)
-        x3 = send(True)
+        if close:
+            ts(A("cw", 0, 192), IND(A("Db"), A("wbU", 0, 12)), -1.0, ALU.add)
+            act(A("cw", 192, E), IND(A("Db"), A("wbU", 12, 24)), bias=-1.0)
+            mm(A("P7", 0, E), A("pBb"), A("cw"), False, True)
+            act(A(snd()), A("P7", 0, E), AF.Relu, scale=2.0 ** 11)
+            x3 = send(True)
+        else:
+            x3 = masked_out(A("Db"), "mw", "Bb", -1.0)
         for h, (lo, hi) in enumerate(HALF):
             mm(A("P%d" % h, 0, hi - lo), A("uIb" if close else "Ib"), A("Db", lo, hi), True, True)
 
@@ -434,8 +504,7 @@ def build():
             rest = A("P1", 0, V - VH)
             tt(rest, rest, A("valS", VH, V), ALU.mult)
             tt(A("P0"), A("P0"), A("valS", 0, VH), ALU.mult)
-            if SF:
-                act(A("u0", VH, V), rest)
+            act(A("u0", VH, V), rest)
             for k in range(4):
                 tt(A("Cf", k, NV, 4), A("P0"), A("R", k, NV, 4), ALU.min)
                 if k < SF:
@@ -446,37 +515,40 @@ def build():
                     act(A("Cf", NV + k, NC, 4), o, AF.Relu)
                 else:
                     tt(A("Cf", NV + k, NC, 4), rest, A("R", NV + k, NC, 4), ALU.min)
-            act(A("Cf", NC, NX), turn(x3, "Bf"), scale=2.0 ** 11)
+            arrive(x3)
             win = "Cf"
             for sw, (bank, w, c, wa, first) in enumerate((("P5", "c15", 2.0 ** -15, "c2", "b1"), ("P1", "c2", 0.25, "c2", "valS"),
                                                           ("P5", "If", 1.0, "If", "valS"))):
-                rest = A(bank, 0, V - VH)
-                mm(rest, A(wa), A("valS", VH, V), True, False)
+                rest, mine = A(bank, 0, V - VC), A("P0", 0, VC)
                 if sw == 2:
-                    mm(A("P6"), A("Ib"), A("Db", 0, VH), True, True)
+                    mm(mine, A("Ib"), A("Db", 0, VC), True, True)
+                    mm(rest, A("pIb"), A("Db", VC, V), True, False)
+                    mm(rest, A("mIb"), A("one", 0, V - VC), False, False)
+                mm(rest, A(wa), A("valS", VC, V), sw < 2, False)
                 sum32(A(win), "invL", first, "mf", bank, w)
                 if sw == 2:
-                    tt(A("mf", VH, V), rest, A("Db", VH, V), ALU.mult)
-                    dma("s", ("out", "mu", VH, V), A("mf", VH, V))
-                    tt(A("mf", 0, VH), A("P6"), A("mf", 0, VH), ALU.mult)
-                    dma("y", ("out", "mu", 0, VH), A("mf", 0, VH))
+                    act(A("mf", VC, V), rest, AF.Relu)
+                    dma("y", ("out", "mu", VC, V), A("mf", VC, V))
+                    for q, lo, hi in (("y", 0, 256), ("s", 256, VC)):
+                        tt(A("mf", lo, hi), A("P0", lo, hi), A("mf", lo, hi), ALU.mult)
+                        dma(q, ("out", "mu", lo, hi), A("mf", lo, hi))
                     break
-                act(A("mf", VH, V), rest, scale=1.0 / c)
+                act(A("mf", VC, V), rest, scale=1.0 / c)
                 export(A("mf"), "wbU", c)
                 xm = send(True)
-                act(A("P0"), A("mf", 0, VH), scale=c)
+                act(mine, A("mf", 0, VC), scale=c)
                 if sw == 0:
                     for k in range(SW):
-                        act(A("nM", k, NS, 4), A("Cf", NV + k, NC, 4), AF.Relu, bias=1.0, scale=-1.0)
+                        act(A("nM", 4 * VC + k, NC, 4), A("Cf", 4 * VC + k, NC, 4), AF.Relu, bias=1.0, scale=-1.0)
                 for k in range(4):
-                    tt(A("W", k, NV, 4), A("P0"), A("Cf", k, NV, 4), ALU.min)
+                    tt(A("W", k, 4 * VC, 4), mine, A("Cf", k, 4 * VC, 4), ALU.min)
                 for k in range(SW, 4):
-                    tt(A("W", NV + k, NC, 4), rest, A("Cf", NV + k, NC, 4), ALU.min)
+                    tt(A("W", 4 * VC + k, NC, 4), rest, A("Cf", 4 * VC + k, NC, 4), ALU.min)
                 for k in range(SW):
-                    o = A("P%d" % (4 + 2 * (k & 1)), 0, V - VH)
-                    mm(o, A("mIb"), A("nM", k, NS, 4), True, False)
-                    mm(o, A(w), A("mf", VH, V), False, True)
-                    act(A("W", NV + k, NC, 4), o, AF.Relu)
+                    o = A("P%d" % (4 + 2 * (k & 1)), 0, V - VC)
+                    mm(o, A("mIb"), A("nM", 4 * VC + k, NC, 4), True, False)
+                    mm(o, A(w), A("mf", VC, V), False, True)
+                    act(A("W", 4 * VC + k, NC, 4), o, AF.Relu)
                 for h, (lo, hi) in enumerate(HALF):
                     o = A("P%d" % (2 + h), 0, hi - lo)
                     if sw == 0:
@@ -486,7 +558,8 @@ def build():
                         tt(A("pO", lo, hi), A("debtI", lo, hi), o, ALU.subtract)
                 if sw == 1:
                     dma("y", ("out", "pay", 0, V), A("pO"))
-                tt(A("W", NC, NX), turn(xm, "Bf"), A("Cf", NC, NX), ALU.min)
+                for x, lo, hi in halves(xm, "Bf", "P6"):
+                    tt(A("W", lo, hi), x, A("Cf", lo, hi), ALU.min)
                 win = "W"
             break
 
@@ -499,87 +572,94 @@ def build():
             act(A("i9", 0, 112), A("i9", 0, 112), bias=col(13))
             act(A("i9", 112, 126), A("i9", 112, 126), bias=col(0))
             act(A("iB"), A("i9", 112, 126))
-            act(col(15), col(14), bias=float(DM))
+            act(col(15), col(14), bias=float(DM), scale=float(NA))
             act(A("rIh"), A("Ib"), scale=-0.25)
         act(A("vF", 0, 14), A("i9", 112, 126), bias=float(3 - t), scale=4.0)
-        act(A("vF", 14, 28), A("i9", 112, 126), bias=float(r0), scale=16.0)
+        act(A("vF", 14, 28), A("i9", 112, 126), bias=float(NA * r0))
         act(A("kk"), A("i9"), bias=float(1 - 256 * r0), scale=0.0)
         port0 = lambda r: DM + 16 * r + r0
         port4 = lambda r: DM + 16 * (r >> 2) + r0
         ports = lambda r: DM + 16 * (r >> 2) + r0 + (r & 3)
         for k in range(4):
             act(A("MA", NA * k, NA * k + NA), A("R", r0 + k, NC, 16), AF.Sign)
-        act(A("C0b", NC, NX), turn(x3, "Bb"))
-        extract(A("P6", 0, 56), "EW", "invT", port4, 56, 64)
+        arrive(x3)
+        extract(A("P6", 0, 56), "EP", "invT", port4, 56, 64)
         extract(A("P6", 56, 70), "EE", "invT", port0, 14, 256)
-        x4 = threats("C0b", "Z", ("P4", "P5"), "mb1")
+        x4 = threats("C0b", "Z", ("P4", "P5"), "mb1", "snd%d" % x3, FIRST[t][0])
         ts(A("g4U"), A("P6", 0, 56), col(15), ALU.add)
         tt(A("vdU"), A("P6", 56, 70), A("vF", 0, 14), ALU.not_equal)
-        ts(A("wU"), A("P6", 56, 70), NA, ALU.add)
+        cpy(A("wU"), A("P6", 56, 70))
         act(A("xw"), A("P6", 56, 70), bias=float(NA))
+        extract(A("P0", 56, 70), "EP", "invT", port0, 14, 256)
         extract(A("P0", 0, 56), "E4", "MA", lambda r: r, 56, 16)
-        extract(A("P0", 56, 70), "EW", "invT", port0, 14, 256)
-        extract(A("P0", 80, 136), "EE", "invT", ports, 56, 64)
+        extract(A("P1", 0, 56), "EE", "invT", ports, 56, 64)
+        ts(A("aU"), A("P1", 0, 56), V, ALU.min)
+        ts(A("aW"), A("P1", 0, 56), 16 - V, ALU.add, 0, ALU.max)
         for c in (0, 28):
             (cpy if c < 28 * GWV else act)(A("gw", 16 * c, 16 * c + DM), IND(A("sigT"), A("g4U", c, c + 28)))
         act(A("vdR"), IND(A("c01"), A("vdU")))
         for l in range(4):
             hand(A("mk", l, V, 4), A("Z", r0 + l, NC, 16))
         mm(A("P6", 0, 126), A("If"), A("kk"), True, False)
-        extract(A("P6", 0, 56), "KS", "sigT", ports, 56, 64, False, False)
+        extract(A("P6", 0, 56), "KS", "sigT", lambda r: DM + NA * (r0 + (r & 3)) + (r >> 2), 56, 4, False, False)
         tt(A("kI"), A("P0", 0, 56), A("kc"), ALU.add)
         tt(A("kI", 0, 28), A("kI", 0, 28), A("kI", 28, 56), ALU.min)
         tt(A("kI", 0, 14), A("kI", 0, 14), A("kI", 14, 28), ALU.min)
-        ts(A("kI", 0, 14), A("kI", 0, 14), 3, ALU.bitwise_and)
+        ts(A("kI", 14, 28), A("kI", 0, 14), 3, ALU.bitwise_and)
+        ts(A("kI", 0, 14), A("kI", 14, 28), NA, ALU.mult)
         tt(A("rF", 0, 14), A("kI", 0, 14), A("vF", 14, 28), ALU.add)
         tt(A("rF", 14, 28), A("P0", 56, 70), A("kI", 0, 14), ALU.add)
-        cpy(A("aU"), A("P0", 80, 136))
         cpy(A("rU"), A("rF"))
         act(A("vS"), IND(A("sigT", DM, DM + NX), A("rU")))
-        spread("C1b", "C0b", 0, ("P4", "P5"), ALU.mult, (SIDE1, (("Ib", "mb1", None), ("sIb", "C0b", (0,))), AF.Relu, -16.0))
-        tt(A("C1b", NC, NX), turn(x4, "Bb"), A("C0b", NC, NX), ALU.mult)
-        base(("P0", "P1"), "Ib", "one")
-        x5 = threats("C1b", "Z2", ("P0", "P1"), "mb2")
-        extract(A("P6", 56, 112), "KS", "gw", lambda r: r, 56, 16, False, False)
-        extract(A("P6", 112, 126), "KI", "invT", port0, 14, 256, False)
-        extract(A("P4", 0, 28), "EX", "vS", lambda r: r, 28, 16)
-        extract(A("P4", 28, 56), "EE", "vS", lambda r: r, 28, 16)
+        extract(A("P6", 112, 126), "KI", "invT", port0, 14, 256, False, False)
+        extract(A("P6", 56, 112), "KS", "gw", lambda r: r, 56, 16, False)
+        extract(A("P1", 28, 56), "ES", "vS", lambda r: r, 28, 16)
+        extract(A("P1", 0, 28), "XS", "vS", lambda r: r, 28, 16)
         tt(A("n1"), A("P6", 0, 126), A("i9"), ALU.is_le)
         tt(A("n2"), A("P6", 0, 126), A("n1"), ALU.mult)
         cpy(A("cU"), A("n2"))
-        cpy(A("sU"), A("P4", 0, 56))
-        act(A("xx", 28, 42), A("P4", 14, 28), bias=float(DM))
-        act(A("xx", 42, 56), A("P4", 0, 14), bias=float(DM))
+        cpy(A("sU"), A("P1", 0, 56))
+        act(A("xx", 28, 42), A("P1", 14, 28), bias=float(DM))
+        act(A("xx", 42, 56), A("P1", 0, 14), bias=float(DM))
         act(A("vC"), IND(A("cp", DM, DM + NX), A("sU", 0, 28)))
         act(A("vL"), IND(A("Lq"), A("sU", 28, 56)))
-        mm(A("P5", 0, NA), A("sIb"), A("Db", 3 - t, V, 4), True, False)
         mm(A("P6", 0, 14), A("Ib"), A("iB"), True, False)
-        mm(A("P4", 0, DM), A("nIb"), A("vC"), True, False)
-        mm(A("P4", 0, NA), A("Ih"), A("vL", NA, DM), False, False)
-        mm(A("P4", NA, DM), A("Ih"), A("vL", 0, NA), False, True)
-        act(A("yn"), A("P4", 0, DM), AF.Relu)
-        mm(A("P7", 0, DM), A("nIb"), A("vC"), True, False)
-        mm(A("P7", 0, DM), A("Ih"), A("vL"), False, True)
-        act(A("yo"), A("P7", 0, DM), AF.Relu, scale=1.0)
-        mm(A("P4", 0, DM), A("qIh"), A("yn"), True, False)
-        mm(A("P4", 0, DM), A("rIh"), A("yo"), False, True)
-        act(A("dv"), A("P4", 0, NA), bias=12.0 / 128, scale=1.0 / 128)
-        act(A("dw"), A("P4", NA, DM))
-        tt(A("nw"), IND(A("S14"), A("wU")), A("dw"), ALU.add)
-        mm(A("P3", 0, NA), A("sIb"), A("vdR"), True, False)
-        mm(A("P3", 0, NA), A("NE"), A("invT", DM + r0, DM + NC, 16), False, False)
-        cpy(A("mb2", V, V + E), turn(x5, "Bb"))
-        for lo, hi in ((0, 640), (640, V)):
+        mm(A("P0", 0, DM), A("nIb"), A("vC"), True, False)
+        mm(A("P0", 0, NA), A("Ih"), A("vL", NA, DM), False, False)
+        mm(A("P0", NA, DM), A("Ih"), A("vL", 0, NA), False, True)
+        act(A("yn"), A("P0", 0, DM), AF.Relu)
+        mm(A("P1", 0, DM), A("nIb"), A("vC"), True, False)
+        mm(A("P1", 0, DM), A("Ih"), A("vL"), False, True)
+        act(A("yo"), A("P1", 0, DM), AF.Relu, scale=1.0)
+        mm(A("P0", 0, DM), A("qIh"), A("yn"), True, False)
+        mm(A("P0", 0, DM), A("rIh"), A("yo"), False, True)
+        act(A("dv"), A("P0", 0, NA), bias=12.0 / 128, scale=1.0 / 128)
+        act(A("dw"), A("P0", NA, DM))
+        tt(A("nw"), IND(A("S14", NA, NA + V + E), A("wU")), A("dw"), ALU.add)
+        tt(A("nq"), IND(A("Lq"), A("wU")), A("nw"), ALU.min)
+        spread("C1b", "C0b", 0, ("P4", "P5"), ALU.mult, (SIDE1, (("Ib", "mb1", None), ("sIb", "C0b", (0,))), AF.Relu, -16.0))
+        arrive(x4, *READY[1])
+        base(("P2", "P3"), "Ib", "one")
+        x5 = threats("C1b", "Z2", ("P2", "P3"), "mb2", "snd%d" % x3, FIRST[t][1])
+        mm(A("P5", 0, NA), A("sIb"), A("Db", 3 - t, V, 4), True, False)
+        mm(A("P4", 0, NA), A("sIb"), A("vdR"), True, False)
+        mm(A("P4", 0, NA), A("NE"), A("invT", DM + r0, DM + NC, 16), False, False)
+        for lo, hi in ((0, DM), (DM, V)):
             tt(A("z3", lo, hi), IND(A("mb2"), A("aU", lo // 16, hi // 16)), A("mk", lo, hi), ALU.mult)
+        for l in range(4):
+            mm(A("P5", 0, NA), A("qIb"), A("z3", l, V, 4), False, False)
+        arrive(x5, *READY[2])
+        for q, lo, hi in (("v", 0, DM), ("s", DM, V)):
+            (cpy if q == "v" else act)(A("MA", lo, hi), IND(A("w5"), A("aW", lo // 16, hi // 16)))
             for l in range(4):
-                mm(A("P5", lo // 4, hi // 4), A("qIb"), A("z3", lo + l, hi, 4), False, l == 3 and hi == V)
+                mm(A("P5", lo // 4, hi // 4), A("qIb"), A("MA", lo + l, hi, 4), False, l == 3 and hi == V)
         ts(A("vote"), A("P5", 0, NA), A("thr"), ALU.is_ge)
-        mm(A("P3", 0, NA), A("blk"), A("vote"), False, True)
-        ts(A("actW", 1, NA + 1), A("P3", 0, NA), 24.5, ALU.is_ge)
+        mm(A("P4", 0, NA), A("blk"), A("vote"), False, True)
+        ts(A("actW", 1, NA + 1), A("P4", 0, NA), 24.5, ALU.is_ge)
         mm(A("P2", 0, NA), A("sIb"), A("actW", 1, NA + 1), True, False)
         act(A("cg", 2 * V, 9 * NA), IND(A("actW"), A("cU", 112, 126)))
         mm(A("P2", 0, NA), A("nIb"), A("cg", 2 * V, 2 * V + NA), False, False)
-        for q, lo, hi in (("v", 0, 512), ("s", V, V + 512), ("v", 512, V), ("s", V + 512, V + 768), ("v", V + 768, 2 * V)):
+        for q, lo, hi in CHG:
             (cpy if q == "v" else act)(A("cg", lo, hi), IND(A("actW"), A("cU", lo // 16, hi // 16)))
             for j in range(4):
                 mm(A("P2", (lo % V) // 4, ((hi - 1) % V + 1) // 4), A("nIb"), A("cg", lo + j, hi, 4), False, hi == 2 * V and j == 3)
@@ -589,18 +669,20 @@ def build():
         mm(A("P5", 0, NA), A("Ib"), okv, True, True)
         tt(A("P5", 0, NA), A("P5", 0, NA), A("dv"), ALU.mult)
         sv = A("S14", NA + 3 - t, NA + V, 4)
-        tt(sv, A("P5", 0, NA), sv, ALU.add)
+        tt(A("P5", 0, NA), A("P5", 0, NA), sv, ALU.add)
+        tt(A("q1", 3 - t, V, 4), A("P5", 0, NA), A("Lq", 3 - t, V, 4), ALU.min)
         tt(A("owU"), A("P6", 0, 14), A("xw"), ALU.min)
-        cpy(IND(A("S14"), A("owU")), A("nw"))
-        export(A("S14", NA, NA + V), "xbU")
+        cpy(IND(A("q1w"), A("owU")), A("nq"))
+        export(A("q1", 0, V), "xbU")
         x1 = send(False)
+        if t + 1 < RO:
+            act(sv, A("P5", 0, NA))
+            cpy(IND(A("S14"), A("owU")), A("nw"))
         act(A("xx", 0, 14), A("rF", 14, 28), bias=float(DM))
         act(A("xx", 14, 28), A("rF", 0, 14), bias=float(DM))
         for j in range(4):
             act(A("o4", 14 * j, 14 * j + 14), A("P6", 0, 14), bias=float(NA * (j & 1)))
         act(A("vN"), IND(A("invT", DM, DM + NX), A("sU", 0, 28)))
-        for h, (lo, hi) in enumerate(HALF):
-            act(A("P%d" % h, 0, hi - lo), A("Lq", lo, hi))
         tt(A("oU"), A("o4"), A("xx"), ALU.min)
         cpy(IND(A("sigT"), A("oU", 0, 28)), A("vS"))
         for b, w, x, c in (("P7", "Ih", "e16", 1.0), ("P4", "nIb", "LB", -1.0)):
@@ -608,14 +690,11 @@ def build():
             mm(A(b, 0, NA), A(w), A(x, 3 - t, V, 4), False, True)
             act(A(x, 3 - t, V, 4), A(b, 0, NA), scale=c)
         for b, lo, hi in (("P5", 0, 96), ("P6", 96, NA)):
-            extract(A(b, lo, hi), "EE", "sigT", lambda r: DM + 16 * lo + r, hi - lo, 16)
+            extract(A(b, lo, hi), "ES", "sigT", lambda r: DM + NA * r + lo, hi - lo, 1)
             cpy(A("atO", lo, hi), A(b, lo, hi))
-        for h, (lo, hi) in enumerate(HALF):
-            tt(A("q1", lo, hi), A("P%d" % h, 0, hi - lo), A("S14", NA + lo, NA + hi), ALU.min)
-        for c in (0, 14):
-            cpy(IND(A("cp"), A("oU", 28 + c, 42 + c)), A("vC", 16 * c, 16 * c + NA))
-        for c in (0, 14):
-            cpy(IND(A("invT"), A("oU", 28 + c, 42 + c)), A("vN", 16 * c, 16 * c + NA))
+        for w, x in (("cp", "vC"), ("invT", "vN")):
+            for c in (0, 14):
+                cpy(IND(A(w), A("oU", 28 + c, 42 + c)), A(x, 16 * c, 16 * c + NA))
     return ops
 
 
@@ -679,7 +758,7 @@ def cost(op, c):
         t = k
     else:
         t = k * (0.5 if wide(a[0]) == 2 and wide(a[1]) == 2 else 1)
-    t = max(t, 64) + c["call"]
+    t = max(t, 64) + c["call"] * (1.3 if q == "s" else 1.0)
     return t, t
 
 
@@ -771,8 +850,26 @@ def plan():
             return [-(at[n] + tm[n][0]) for n in range(size)]
         return at
 
+    other = dict(COST)
+    other.update(COST2)
+    tm2 = []
+    for ms in members:
+        c = [cost(ops[n], other) for n in ms]
+        tm2.append((max(sum(x[0] for x in c), 0.001), c[0][1] if len(ms) == 1 else sum(x[0] for x in c)))
+    gap2 = [[(m, tm2[m][1] + other["hop"] if d > tm[m][0] + 0.01 else tm2[m][0]) for m, d in gap[n].items()] for n in range(size)]
+
     def worth(at):
-        return max(at[n] + tm[n][1] for n in range(size)) + EARLY * sum(at[n] for n in sends)
+        free = {q: 0.0 for q in set(line_of)}
+        at2 = [0.0] * size
+        for n in sorted(range(size), key=lambda k: at[k]):
+            t = free[line_of[n]]
+            for m, d in gap2[n]:
+                if at2[m] + d > t:
+                    t = at2[m] + d
+            at2[n] = t
+            free[line_of[n]] = t + tm2[n][0]
+        return sum(w * (max(a[n] + c[n][1] for n in range(size)) + EARLY * sum(a[n] for n in sends))
+                   for a, c, w in ((at, tm, 1.0), (at2, tm2, SECOND)))
 
     way = [t[1] for t in tm]
     for n in range(size - 1, -1, -1):
@@ -815,13 +912,29 @@ def plan():
                 n = by
         return out
 
-    pairs = held(start)
+    first, mark = start, best
     for rep in range(TRIES):
-        key = list(start)
+        if rep % (TRIES // RUNS) == 0:
+            here, level = (first, mark) if rep + TRIES // RUNS < TRIES else (start, best)
+            pairs = held(here)
+        key = list(here)
         for more in range(1 + draw(2)):
             n, m = pairs[draw(len(pairs))]
-            if draw(3):
+            how = draw(8)
+            if how < 4:
                 key[m] = key[n] + 0.5 + (tm[n][0] + 3000.0 * draw(3)) * draw(2)
+            elif how < 6:
+                n = (n, m)[draw(2)]
+                last = max([k for k in sends if here[k] < here[n]] + [0])
+                mine = (above[n] | 1 << n) & ~above[last]
+                step = 1000.0 * (1 + draw(8))
+                for k in range(n + 1):
+                    if mine >> k & 1:
+                        key[k] -= step
+                for k in range(n, -1, -1):
+                    for j in post[k]:
+                        if key[j] <= key[k]:
+                            key[k] = key[j] - 0.0001
             else:
                 key[n] = key[m] - 0.5
                 for k in range(n, -1, -1):
@@ -833,9 +946,12 @@ def plan():
                 if key[j] >= key[k]:
                     key[k] = key[j] + 0.0001
         now = place(sorted(range(size), key=lambda k: (key[k], k)), gap, False)
-        if worth(now) <= best:
-            best, start = worth(now), now
-            pairs = held(start)
+        good = worth(now)
+        if good <= level + SLACK:
+            here, level = now, good
+            pairs = held(here)
+            if good < best:
+                best, start = good, now
     seq = [n for u in sorted(range(size), key=lambda k: (start[k], k)) for n in members[u]]
     new = {m: j for j, m in enumerate(seq)}
     return [ops[m] for m in seq], [set(new[k] for k in deps[m]) for m in seq]
@@ -881,11 +997,13 @@ def rank_program(g, core, T, topo):
     def ap(x):
         if not isinstance(x, tuple):
             return x
+        if x[0] == "ap" and len(x) == 6:
+            return T[x[1]][x[5]:128:16, x[2]:x[3]]
         if x[0] == "ap":
             return T[x[1]][:, x[2]:x[3]:x[4]] if x[4] != 1 else T[x[1]][:, x[2]:x[3]]
         if x[0] == "ind":
             return ap(x[1]).indirect(ap(x[2]))
-        if x[0] == "in":
+        if len(x) == 2:
             return T[x[1]][:]
         return T[x[1]][:, x[2]:x[3]]
 
@@ -913,7 +1031,7 @@ def rank_program(g, core, T, topo):
                 dst = T.cores[(rank - d if back else rank + d) % n_r]
                 eng = topo.engines(core, dst)
                 k = len(eng) // 4
-                part = eng[k * (d - 1):k * d] if d < n_r - 1 else eng[k * (d - 1):]
+                part = eng[0::2][k * (d - 1):k * d] if d < n_r - 1 else eng[1::2]
                 mask = 0
                 for b in part:
                     mask |= 1 << b

import math
from concourse.bass import DstId, RemoteDMATransfer
from concourse.mybir import AluOpType as ALU, ActivationFunctionType as AF

V, X, E, NC, NX, NA = 896, 128, 384, 3584, 3968, 224
RO = 2
VH = 512
VC = 512
NV = 4 * VH
NS = NC - NV
DM = 448
F32, BF, F16, I32, U16 = "float32", "bfloat16", "float16", "int32", "uint16"
XDT = [F16] + [F16, F32, BF, BF, BF] * RO + [F16, F32, F32, F32, F32]

_SB = {
    "sc": (NA + 248, I32), "lstU": (248, U16), "sigL": (224, U16), "atO": (224, U16), "xbU": (24, U16),
    "invL": (248, U16), "wbU": (24, U16), "w4U": (96, U16), "invW": (96, U16), "zW": (4 * E, BF), "gT": (4 * E, BF),
    "cw": (E, BF), "mw": (E, BF), "qBb": (128, BF), "ta": (256, I32),
    "debtI": (V, I32), "cashI": (V, I32), "thI": (1, I32), "thr": (1, F32), "colS": (NX, BF), "valS": (V, F32),
    "Lq": (V + E, F32), "e16": (V, F16), "LB": (V, F16), "cm": (NC, BF),
    "S14": (NA + V + E, F32), "q1w": (NA + V + E, F32), "q2": (V, F32), "y16": (NC, F16), "W": (NX, F32), "R": (NC, F32),
    "rw": (E, F32), "Db": (V, BF), "C0b": (NX, BF), "Z": (NC, BF), "mb1": (V, BF), "mb2": (V + 16, BF), "w5": (16 + E, BF), "C1b": (NX, BF), "aW": (56, U16), "Cf": (NX, F32), "Rs": (1792, F32),
    "vinit": (NX, BF), "invT": (DM + NX, BF), "sigT": (DM + NX, BF), "cp": (DM + NX, BF),
    "zb": (128, BF), "zf": (128, F32), "ioC": (256, F32), "pI": (1, I32), "pJ": (2, I32), "OH": (16, F32),
    "col": (24, F32), "colB": (4, BF), "Ib": (128, BF), "nIb": (128, BF), "qIb": (128, BF), "sIb": (128, BF), "one": (VH, BF),
    "qIh": (128, F16), "Ih": (128, F16), "If": (128, F32), "nIf": (128, F32), "Fh": (128, F16), "Ff": (128, F32),
    "c15": (128, F32), "c2": (128, F32), "uIb": (128, BF), "mIb": (128, BF), "pIb": (128, BF), "pBb": (128, BF),
    "aIb": (128, BF), "Bb": (128, BF), "Bf": (128, F32), "mats": (9 * 144 + 256, BF), "c01": (16, BF), "blkT": (256, BF),
    "dIb": (128, BF), "i9": (126, F32), "iB": (14, BF), "kc": (56, F32), "kk": (126, F32),
    "MA": (V, BF), "mk": (V, BF), "z3": (V, BF), "aU": (56, U16), "vF": (28, F32),
    "kI": (56, I32), "n1": (126, F32), "n2": (126, F32), "cU": (126, U16), "wU": (14, U16), "vdU": (14, U16),
    "g4U": (56, U16), "rF": (28, F32), "rU": (28, U16), "sU": (56, U16),
    "vS": (DM, BF), "vN": (DM, BF), "vC": (DM, BF), "rIh": (128, F16),
    "vdR": (NA, BF), "vote": (NA, BF), "actW": (240, BF), "okF": (V, BF),
    "xw": (14, F32), "xx": (56, F32), "o4": (56, F32), "owU": (14, U16), "oU": (56, U16),
}
ALIAS = {"tb": ("Rs", 0, NA), "tf": ("Rs", NA, 256), "Z2": ("colS", 0, NC), "cg": ("colS", 0, 9 * NA), "u0": ("q1w", NA, V), "q1": ("q1w", NA, V + E), "nq": ("Rs", DM + NA, NA), "gw": ("z3", 0, V), "mf": ("Lq", 0, V),
         "vL": ("y16", 0, DM), "yn": ("y16", DM, DM), "yo": ("y16", 2 * DM, DM), "dv": ("Rs", 0, NA), "dw": ("Rs", NA, NA), "nw": ("Rs", DM, NA),
         "pO": ("q2", 0, V), "vw": ("q1w", NA + V, E), "Lh": ("y16", NC - V, V), "b1": ("S14", 0, VH), "nM": ("Z", 0, NC),
         "EX": ("mats", 0, 144), "EE": ("mats", 144, 144), "EW": ("mats", 288, 144), "KI": ("mats", 432, 144), "KS": ("mats", 576, 144),
         "E4": ("mats", 720, 144), "NE": ("mats", 864, 128), "blk": ("mats", 992, 128),
         "XS": ("mats", 1120, 144), "ES": ("mats", 1264, 144), "EP": ("mats", 1408, 144), "se": ("mk", 0, V),
         "sigI": ("sc", NA, 248), "sd": ("cashI", 0, DM)}
for _d, _s in ((F16, "h"), (F32, "f"), (BF, "b")):
    _k = [i for i, d in enumerate(XDT) if d == _d]
    _SB["snd" + _s] = (E * len(_k), _d)
    if _d != BF:
        _SB["lnd" + _s] = (E * len(_k), _d)
    for _j, _i in enumerate(_k):
        ALIAS["snd%d" % _i] = ("snd" + _s, E * _j, E)
        ALIAS["lnd%d" % _i] = ("lnd" + _s, E * _j, E) if _d != BF else (("C0b", NC, E), ("C1b", NC, E), ("w5", 16, E))[_j % 3]
ALIAS.update({"lnd13": ("Cf", NC, E), "lnd14": ("S14", VH + E, E), "snd13": ("Lq", V, E)})
_SB["sndf"] = (E * 5, F32)
_SB["lndf"] = (E * 4, F32)
ALIAS.update({"snd14": ("sndf", 3 * E, E), "snd15": ("sndf", 4 * E, E), "lnd15": ("lndf", 3 * E, E)})
SCRATCH = {k: ("sbuf", [128, n], d) for k, (n, d) in _SB.items()}
for _i in range(8):
    SCRATCH["P%d" % _i] = ("psum", [128, 512], F32)
_DMAS = ["d%d" % i for i in range(16)]
SHIFTED = ((0, 1024), (1024, 2048), (2048, 2816), (2816, NC))
SEMAPHORES = ["sv", "ss", "sp", "sg", "sent"] + ["arr%d" % i for i in range(len(XDT))] + _DMAS

HALF = ((0, VH), (VH, V))
CH16 = (("v", 0, 512), ("s", 512, 1280), ("v", 1280, 2048), ("s", 2048, 2816), ("v", 2816, 3072), ("s", 3072, NC))
CHW = (("v", 0, 512), ("s", 512, 1024), ("v", 1024, 1280), ("s", 1280, 4 * E))
FIRST = ((1, 1), (1, 1))
CH3 = (("v", 0, 256), ("s", 256, 512), ("v", 512, 1024), ("s", 1024, 1536), ("v", 1536, 2048), ("s", 2048, 2560), ("s", 2560, 3072),
       ("s", 3072, 3328), ("v", 3328, NC))
SIDEW = ((("P4",), ("P5",)), (("P4", "P5"), ("P6",)))
SIDE0 = ((), ())
SIDE1 = ((), ())
CH1 = (("v", 0, 512), ("o", 1024, 1536), ("v", 512, 1024), ("o", 1536, 2048), ("t", 2048, 2560), ("o", 2560, 3072), ("o", 3072, NC))
CH2 = ((("v", 0, 512), ("o", 1024, 1536), ("v", 512, 1024), ("t", 1536, 2048), ("t", 2048, 2560), ("t", 2560, 3072), ("t", 3072, NC)),
       (("t", 0, 512), ("v", 512, 1024), ("t", 1024, 1536), ("t", 1536, 2048), ("t", 2048, 2560), ("t", 2560, 2880), ("v", 2880, NC)))
ADD3 = (1, 2)
GWV = 0
CPV = (1, 3, 5)
CHG = (("v", 0, 256), ("s", V, V + 384), ("v", 256, 640), ("v", 640, V), ("s", V + 384, V + 768), ("v", V + 768, 2 * V))
EVAC = 1
READY = ((), (), ())
CMV = 1024
SF, SW = 2, 1
PIECE = 24
COST = dict(gather=1.75, fused=1.85, scatter=4.2, pe=0.56, flight=3600.0, hop=90.0, call=60.0)
COST2 = dict(gather=1.4, fused=1.6, scatter=3.5, pe=0.6, flight=4500.0, hop=100.0)
SECOND = 1.0
ROUNDS = 6
TRIES, RUNS = 24000, 6
LUMP = 650.0
SLACK = 5.0
EARLY = 0.01


def A(name, a=0, b=None, step=1):
    off = 0
    if name in ALIAS:
        name, off, n = ALIAS[name]
    else:
        n = SCRATCH[name][1][1]
    return ("ap", name, off + a, off + (n if b is None else b), step)


def IND(win, off):
    return ("ind", win, off)


def build():
    ops = []

    def span(x):
        if isinstance(x, tuple) and x[0] == "ap":
            return [(x[1], x[2], x[3], x[4])]
        if isinstance(x, tuple) and x[0] == "ind":
            return span(x[1])
        return []

    def offs(x):
        return span(x[2]) if isinstance(x, tuple) and x[0] == "ind" else []

    def put(q, kind, out, ins, args):
        rd = offs(out)
        for x in ins:
            rd = rd + span(x) + offs(x)
        ops.append((q, kind, args, rd, span(out)))

    def cpy(out, x):
        put("v", "copy", out, [x], (out, x))

    def ts(out, x, s1, op0, s2=None, op1=None):
        put("v", "ts", out, [x, s1, s2], (out, x, s1, s2, op0, op1))

    def tt(out, x, y, op):
        put("v", "tt", out, [x, y], (out, x, y, op))

    def act(out, x, func=AF.Identity, bias=0.0, scale=1.0):
        put("s", "act", out, [x, bias, scale], (out, x, func, bias, scale))

    def mm(out, w, x, start, stop, line=None):
        put("p", "mm", out, [w, x], (out, w, x, start, stop, line))

    def fill(out, c):
        put("v", "fill", out, [], (out, c))

    def iota(out, pat, base, cm):
        put("g", "iota", out, [], (out, pat, base, cm))

    def zero(out):
        iota(out, [[0, out[3] - out[2]]], 0, 0)

    def select(out, pat, op, c, base, cm, x=None):
        put("g", "sel", out, [x or out], (out, pat, op, c, base, cm, x or out))

    def hand(out, x):
        select(out, [[0, len(range(*out[2:]))]], ALU.is_equal, 0.0, 0, 0, x)

    def diag(w, c, shift=0):
        select(A(w), [[-1, 128]], ALU.not_equal, c, shift, 1, A("zf" if SCRATCH[A(w)[1]][2] == F32 else "zb"))
        if shift:
            select(A(w), [[-1, 128]], ALU.not_equal, c, shift - 128 if shift > 0 else shift + 128, 1)

    nd = [0]

    def dma(q, out, x):
        put(q, "dma", out, [x], (out, x, _DMAS[nd[0]]))
        nd[0] += 1

    nx = [0]

    def snd():
        return "snd%d" % nx[0]

    def send(back):
        put("g", "send", A("lnd%d" % (nx[0] + 1)) if nx[0] + 1 < len(XDT) else None, [A(snd())], (nx[0], back))
        nx[0] += 1
        return nx[0] - 1

    def export(win, lst, scale=1.0):
        ts(A(snd(), 0, 192), IND(win, A(lst, 0, 12)), scale, ALU.mult)
        act(A(snd(), 192, E), IND(win, A(lst, 12, 24)), scale=scale)

    def arrive(n, *ready):
        ops.append(("a", "arrive", (n,), [y for x in ready for y in span(A(x))], span(A("lnd%d" % n))))

    def turn(n, w):
        arrive(n)
        mm(A("P7", 0, E), A(w), A("lnd%d" % n), True, True)
        return A("P7", 0, E)

    def halves(n, w, bank, *ready):
        arrive(n, *ready)
        out = []
        for b, lo in (("P7", 0), (bank, E // 2)):
            mm(A(b, 0, E // 2), A(w), A("lnd%d" % n, lo, lo + E // 2), True, True)
            out.append((A(b, 0, E // 2), NC + lo, NC + lo + E // 2))
        return out

    def extract(out, w, tab, first, n, step, start=True, stop=True):
        for r in range(16):
            f = first(r)
            mm(out, A(w, 15 - r, 143 - r), A(tab, f, f + step * (n - 1) + 1, step), start and r == 0, stop and r == 15)

    def shares(bank, tab):
        for k in range(4):
            extract(A(bank, 56 * k, 56 * k + 56), "EX", tab, lambda r: DM + 4 * r + k, 56, 64)
        return A(bank, 0, NA)

    def part(lst, k, lo, hi):
        return A(lst, 56 * k + lo // 16, 56 * k + hi // 16)

    def pb(banks, lo, hi):
        h = 0 if lo < VH else 1
        return A(banks[h], lo - VH * h, hi - VH * h)

    def col(j):
        return A("col", j, j + 1)

    def oh(j):
        return A("OH", j, j + 1)

    dma("y", A("sigI", 224, 248), ("in", "xpt"))
    dma("s", A("debtI"), ("in", "debt"))
    dma("y", A("sigI", 0, 224), ("in", "sig"))
    dma("s", A("colS", 0, NC), ("in", "coll"))
    dma("y", A("cashI"), ("in", "cash"))
    dma("y", A("sigT", DM, DM + NC), ("in", "coll"))
    dma("y", A("thI"), ("in", "th"))
    dma("y", A("valS"), ("in", "val"))
    iota(A("pI"), [[0, 1]], 0, 1)
    iota(A("ioC"), [[1, 256]], 0, 0)
    zero(A("zb"))
    zero(A("zf"))
    diag("Ib", 1.0)
    diag("Ff", 1.0, 16)
    diag("nIf", -1.0)
    zero(A("mats", 0, 496))
    zero(A("mats", 496, 992))
    zero(A("mats", 1120, 1552))
    zero(A("invT", 0, DM))
    zero(A("colS", NC, NX))
    ts(A("pJ", 0, 1), A("pI"), 15, ALU.bitwise_and)
    cpy(col(0), A("pJ", 0, 1))
    ts(A("OH"), A("ioC", 0, 16), col(0), ALU.is_equal)
    act(col(1), oh(2), bias=oh(1), scale=1.0 / 16)
    act(col(4), oh(0), bias=oh(4))
    act(col(2), oh(3), bias=col(1), scale=1.0 / 16)
    act(col(5), col(4), scale=2.0)
    act(col(1), oh(5), bias=col(2), scale=0.25)
    act(col(6), col(4), scale=4.0)
    act(col(2), oh(7), bias=col(1), scale=0.25)
    act(col(7), col(4), scale=8.0)
    act(col(3), col(2), bias=-0.5, scale=0.5)
    cpy(A("colB"), A("col", 4, 8))
    act(A("qIh"), A("Ib"), scale=0.25)
    act(A("Fh"), A("Ff"))
    act(A("Ih"), A("Ib"))
    ts(A("ta", 0, 24), A("sigI", 224, 248), 2, ALU.arith_shift_right)
    cpy(A("xbU"), A("ta", 0, 24))
    act(A(snd()), IND(A("debtI"), A("xbU")), bias=-128.0, scale=0.25)
    x0 = send(False)
    ts(A("tf"), A("ioC"), col(2), ALU.mult, col(3), ALU.add)
    cpy(A("lstU"), A("sigI"))
    cpy(A("ta"), A("tf"))
    act(A("Lq", 0, V), A("debtI"), bias=-128.0, scale=0.25)
    cpy(A("vinit", 0, 256), A("ta"))
    act(A("tb"), A("sigI", 0, 224), bias=-0.375, scale=0.25)
    act(A("P6", 0, 224), A("sigI", 0, 224), bias=-3.0 * V)
    ts(A("vinit", 256, 512), A("vinit", 0, 256), A("colB", 0, 1), ALU.add)
    ts(A("vinit", 512, 1024), A("vinit", 0, 512), A("colB", 1, 2), ALU.add)
    tt(A("tb"), A("tb"), A("P6", 0, 224), ALU.max)
    cpy(A("atO"), A("tb"))
    act(A("e16"), A("cashI"))
    for lo, hi in SHIFTED:
        if lo >= CMV:
            ts(A("cm", lo, hi), A("colS", lo, hi), -128.0, ALU.add)
        else:
            act(A("cm", lo, hi), A("colS", lo, hi), bias=-128.0)
    act(A("vinit", 1024, 2048), A("vinit", 0, 1024), bias=col(6))
    act(col(8), oh(7), bias=col(2), scale=0.75)
    act(col(9), col(8), bias=-0.5, scale=0.5)
    act(col(10), col(4), bias=oh(6), scale=14.0)
    act(col(12), oh(4), bias=col(10), scale=4.0)
    act(col(11), oh(0), bias=col(12))
    act(A("tf"), A("ioC"), bias=col(9), scale=col(8))
    for lo in (2048, 2816):
        act(A("vinit", lo, lo + 768), A("vinit", lo - 2048, lo - 1280), bias=col(7))
    cpy(A("ta"), A("tf"))
    cpy(A("blkT"), A("ta"))
    act(A("vinit", NC, NC + 256), A("blkT"), bias=col(10))
    act(A("vinit", NC + 256, NX), A("blkT", 0, 128), bias=col(11))
    for c in range(0, 248, PIECE):
        cpy(IND(A("invT", DM, DM + NX), A("lstU", c, min(c + PIECE, 248))), A("vinit", 16 * c, 16 * min(c + PIECE, 248)))
    cpy(A("sc", 0, NA), A("atO"))
    for j, (op, c) in enumerate(((ALU.arith_shift_right, 4), (ALU.bitwise_and, 15))):
        ts(A("sd"), A("sc", 0, DM), c, op)
        act(A("se", DM * j, DM * j + DM), A("sd"))
    for row, j in ((2, 0), (0, 1), (3, 2), (1, 3)):
        dma("y", A("sigT", DM, DM + NC) + (row,), A("se", NA * j, NA * j + NA))
    diag("nIb", -1.0)
    diag("qIb", 0.25)
    act(A("Lh"), A("Lq", 0, V))
    iota(A("one"), [[0, VH]], 1, 0)
    for h, (lo, hi) in enumerate(HALF):
        o = A("P%d" % h, 0, hi - lo)
        mm(o, A("qIh"), A("e16", lo, hi), True, False)
        for k in range(4):
            mm(o, A("qIb"), A("colS", 4 * lo + k, 4 * hi, 4), False, False)
        mm(o, A("nIb"), A("Lh", lo, hi), False, True)
        act(A("LB", lo, hi), o, scale=-4.0, bias=512.0)
    fill(A("mats", 992, 1120), 1.0)
    for w, rows in (("EX", ((0, 256), (1, 1))), ("EE", ((4, 64), (7, 1))), ("EW", ((0, 256), (5, 4))),
                    ("KI", ((0, 16), (2, 1), (3, -4096), (5, 1024))), ("KS", ((0, 1), (1, 256))),
                    ("XS", ((0, 16), (1, 1))), ("ES", ((2, 16), (3, 1))), ("EP", ((0, 16), (2, 1), (3, -3584), (5, 896)))):
        for r, c in rows:
            select(A(w, 15, 143, 16), [[-16, 8]], ALU.not_equal, float(c), -r, 1)
    select(A("NE"), [[-16, 8], [0, 16]], ALU.not_equal, -64.0, -6, 1)
    select(A("blk"), [[-16, 8], [0, 16]], ALU.is_ge, 0.0, 0, 1)
    select(A("blk"), [[16, 8], [0, 16]], ALU.is_ge, 0.0, 15, -1)
    iota(A("i9", 0, 112), [[0, 2], [4, 56]], 0, 0)
    iota(A("i9", 112, 126), [[16, 14]], 0, 0)
    iota(A("kc"), [[1, 4], [0, 14]], 0, 0)

    def claim_sweep(win, out, pieces, wide):
        for h, (lo, hi) in enumerate(HALF):
            mm(A("P%d" % h, 0, hi - lo), A("qIh"), A("e16", lo, hi), True, False)
        bank = 2
        for j, (how, lo, hi) in enumerate(pieces):
            y, x, c = A("y16", lo, hi), IND(win, A("atO", lo // 16, hi // 16)), A("cm", lo, hi)
            o = pb(("P0", "P1"), lo // 4, hi // 4)
            w, val = "qIh", "y16"
            if how == "v":
                tt(y, x, c, ALU.max)
            else:
                p = A("P%d" % bank, 0, hi - lo)
                bank += 1
                act(y, x)
                if how == "t":
                    mm(p, A("Ib"), c, True, True)
                    tt(y, y, p, ALU.max)
                else:
                    for k in range(4):
                        mm(o, A("qIb"), A("cm", lo + k, hi, 4), False, False)
                    mm(p, A("nIb"), c, True, False)
                    mm(p, A("Ih"), y, False, True)
                    if wide:
                        w, val = "c2", "R"
                    act(A(val, lo, hi), p, AF.Relu)
            last = all((lo < NV) != (a < NV) for _, a, b in pieces[j + 1:])
            for k in range(4):
                mm(o, A(w), A(val, lo + k, hi, 4), False, last and k == 3)
            if last:
                a, b = HALF[lo >= NV]
                tt(A(out, a, b), A("P%d" % (lo >= NV), 0, b - a), A("Lq", a, b), ALU.min)

    def sum32(win, lst, first, out, bank, w):
        for k in range(4):
            for lo, hi in ((0, 256), (256, VC)):
                tt(A(out, lo, hi), IND(win, part(lst, k, lo, hi)), A(out if k else first, lo, hi), ALU.add)
        n = V - VC
        for k, lo, hi in ((0, 0, 192), (0, 192, n), (1, 0, n), (2, 0, n), (3, 0, 256), (3, 256, n)):
            r = A("Rs", n * k + lo, n * k + hi)
            act(r, IND(win, part(lst, k, VC + lo, VC + hi)))
            mm(A(bank, lo, hi), A(w), r, False, k == 3 and hi == n)

    def base(banks, w, x):
        for h, (lo, hi) in enumerate(HALF):
            mm(A(banks[h], 0, hi - lo), A(w), A(x, lo, hi) if x != "one" else A(x, 0, hi - lo), True, False)

    def gather(win, lst, pieces, out, scale, banks, w, planes):
        for j, (q, lo, hi) in enumerate(pieces):
            x = IND(win, A(lst, lo // 16, hi // 16))
            if q == "v":
                ts(A(out, lo, hi), x, scale, ALU.mult, 0.0, ALU.max)
            else:
                act(A(out, lo, hi), x, AF.Relu, scale=scale)
            last = all((lo < NV) != (a < NV) for _, a, b in pieces[j + 1:])
            n = planes[lo >= NV]
            for k in range(n):
                mm(pb(banks, lo // 4, hi // 4), A(w), A(out, lo + k, hi, 4), False, last and k == n - 1)

    def spread(out, other, off, banks, op, side):
        for h, (lo, hi) in enumerate(HALF):
            cut = 4 - len(side[0][h])
            for k in range(cut):
                tt(A(out, 4 * lo + k, 4 * hi, 4), A(banks[h], 0, hi - lo), A(other, off + 4 * lo + k, off + 4 * hi, 4), op)
            for k in range(cut, 4):
                o = A(side[0][h][k - cut], 0, hi - lo)
                for j, (w, x, wide) in enumerate(side[1]):
                    src = A(x, wide[0] + 4 * lo + k, wide[0] + 4 * hi, 4) if wide else A(x, lo, hi)
                    mm(o, A(w), src, j == 0, j == len(side[1]) - 1)
                act(A(out, 4 * lo + k, 4 * hi, 4), o, side[2], bias=side[3])

    def masked_out(x, mask, w, bias):
        mm(A("P7", 0, E), A(w), A(mask), True, False)
        cpy(A("cw", 0, 192), IND(x, A("wbU", 0, 12)))
        act(A("cw", 192, E), IND(x, A("wbU", 12, 24)))
        mm(A("P7", 0, E), A("Bb"), A("cw"), False, True)
        act(A(snd()), A("P7", 0, E), AF.Relu, bias=bias)
        return send(True)

    def threats(win, out, banks, mout, mask, first):
        if first:
            mm(A("P7", 0, E), A("sIb"), A(mask), True, False)
            for q, lo, hi in CHW:
                (cpy if q == "v" else act)(A("zW", lo, hi), IND(A(win), A("invW", lo // 16, hi // 16)))
                for l in range(4):
                    mm(A("P7", lo // 4, hi // 4), A("qBb"), A("zW", lo + l, hi, 4), False, hi == 4 * E and l == 3)
            act(A(snd()), A("P7", 0, E), AF.Relu, bias=-15.0)
            x = send(True)
        gather(A(win), "invL", CH16, out, 1.0, banks, "qIb", (4, 4))
        for h, (lo, hi) in enumerate(HALF):
            if mout == "mb2" or not first or SIDE1[h]:
                (act if h or EVAC else cpy)(A(mout, lo, hi), A(banks[h], 0, hi - lo))
        return x if first else masked_out(A(mout, 0, V), mask, "sIb", -16.0)

    act(A("Lq", V, V + E), turn(x0, "Fh"))
    claim_sweep(A("Lq"), "q1", CH1, False)
    act(A(snd()), IND(A("q1", 0, V), A("xbU")))
    x1 = send(False)
    act(A("S14", NA, NA + VH), A("P0"))
    act(A("S14", NA + VH, NA + V), A("P1", 0, V - VH))
    zero(A("c01"))
    select(A("c01"), [[-1, 16]], ALU.is_ge, 1.0, 0, 0)
    for w, c, shift in (("If", 1.0, 0), ("aIb", 2.0 ** 27, 0), ("Bb", 1.0, -16), ("sIb", 16.0, 0), ("qBb", 0.25, -16),
                        ("dIb", 0.375, 0), ("Bf", 1.0, -16), ("c15", 2.0 ** -15, 0),
                        ("c2", 0.25, 0), ("uIb", 2.0 ** 11, 0), ("mIb", -2.0 ** 19, 0), ("pIb", 2.0 ** 19, 0),
                        ("pBb", 2.0 ** 19, -16)):
        diag(w, c, shift)
    for w, lo, hi in (("cp", 0, DM), ("sigT", 0, DM), ("sigT", DM + NC, DM + NX), ("S14", 0, NA), ("q1w", 0, NA), ("S14", NA + V, NA + V + E),
                      ("actW", 0, 16), ("actW", NA, 240), ("mb2", V, V + 16), ("w5", 0, 16), ("okF", 0, DM), ("okF", DM, V)):
        zero(A(w, lo, hi))
    act(A("E4", 15, 143, 16), A("blk", 0, 128, 16), scale=4.0)
    ts(A("pJ", 0, 1), A("pI"), 2, ALU.arith_shift_right, 3, ALU.bitwise_and)
    ts(A("pJ", 1, 2), A("pI"), 3, ALU.bitwise_and)
    cpy(A("col", 13, 15), A("pJ"))
    act(A("thr"), A("thI"), bias=15.0, scale=1.0 / 64)

    for t in range(RO + 1):
        close = t == RO
        r0 = 4 * (3 - t)
        act(A("q1", V, V + E), turn(x1, "Fh"))
        if t == 0:
            for lo, hi in ((0, 128), (128, 248)):
                extract(A("P7", lo, hi), "EX", "invT", lambda r: DM + 16 * lo + r, hi - lo, 16)
                cpy(A("invL", lo, hi), A("P7", lo, hi))
            for j, c in enumerate(range(0, 248, 32)):
                end = min(c + 32, 248)
                o, x = A("cp", DM + 16 * c, DM + 16 * end), IND(A("colS"), A("invL", c, end))
                if j in CPV:
                    ts(o, x, -128.0, ALU.add)
                else:
                    act(o, x, bias=-128.0)
        else:
            extract(A("P7", 0, NA), "XS", "sigT", lambda r: DM + NA * r, NA, 1)
            cpy(A("sigL"), A("P7", 0, NA))
        claim_sweep(A("q1"), "q2", CH2[min(t, 1)], True)
        export(A("q2"), "xbU")
        x2 = send(False)
        for h, (lo, hi) in enumerate(HALF):
            act(A("P%d" % h, 0, hi - lo), A("q2", lo, hi))
        base(("P2", "P3"), "aIb", "LB")
        spread("W", "cp", DM, ("P0", "P1"), ALU.subtract, (SIDEW[min(t, 1)], (("If", "q2", None), ("nIb", "cp", (DM,))), AF.Identity, 0.0))
        extract(A("P6", 256, 280), "EE", "invT", lambda r: DM + NC + r, 24, 16)
        cpy(A("wbU"), A("P6", 256, 280))
        if not close and max(FIRST[t]):
            extract(A("P6", 288, 384), "EW", "invT", lambda r: DM + NC + (r >> 2), 96, 4)
            ts(A("w4U"), A("P6", 288, 384), col(14), ALU.add)
            for c in range(0, 96, 32):
                act(A("gT", 16 * c, 16 * c + 512), IND(A("invT", DM, DM + NX), A("w4U", c, c + 32)))
        if close:
            cpy(A("invL", 0, NA), shares("P6", "invT"))
            act(A("b1", 0, VC), A("valS", 0, VC), scale=2.0 ** 13)
        elif t > 0:
            extract(A("P6", 0, NA), "EX", "invT", lambda r: DM + r, NA, 16)
            cpy(A("invL", 0, NA), A("P6", 0, NA))
        for x, lo, hi in halves(x2, "Ff", "P0", *READY[0]):
            tt(A("W", lo, hi), x, A("cp", DM + lo, DM + hi), ALU.subtract)
        gather(A("W"), "sigL" if t else "lstU", CH3, "R", 2.0 ** 27, ("P2", "P3"), "nIf", ADD3)
        if close:
            act(A("rw"), A("W", NC, NX), AF.Relu, scale=2.0 ** 27)
            tt(A("vw"), IND(A("valS"), A("wbU")), A("rw"), ALU.min)
            mm(A("P7", 0, E), A("Bf"), A("vw"), True, False)
        else:
            act(A("mw"), A("W", NC, NX), AF.Sign)
            if max(FIRST[t]):
                extract(A("P6", 0, 96), "EX", "gT", lambda r: r, 96, 16)
                cpy(A("invW"), A("P6", 0, 96))
        for h, (lo, hi) in enumerate(HALF):
            o = A("P%d" % (2 + h), 0, hi - lo)
            for k in range(ADD3[h], 3):
                tt(o, o, A("R", 4 * lo + k, 4 * hi, 4), ALU.subtract)
            tt(A("Db", lo, hi), o, A("R", 4 * lo + 3, 4 * hi, 4), ALU.is_gt)
        if close:
            ts(A("cw", 0, 192), IND(A("Db"), A("wbU", 0, 12)), -1.0, ALU.add)
            act(A("cw", 192, E), IND(A("Db"), A("wbU", 12, 24)), bias=-1.0)
            mm(A("P7", 0, E), A("pBb"), A("cw"), False, True)
            act(A(snd()), A("P7", 0, E), AF.Relu, scale=2.0 ** 11)
            x3 = send(True)
        else:
            x3 = masked_out(A("Db"), "mw", "Bb", -1.0)
        for h, (lo, hi) in enumerate(HALF):
            mm(A("P%d" % h, 0, hi - lo), A("uIb" if close else "Ib"), A("Db", lo, hi), True, True)

        if close:
            rest = A("P1", 0, V - VH)
            tt(rest, rest, A("valS", VH, V), ALU.mult)
            tt(A("P0"), A("P0"), A("valS", 0, VH), ALU.mult)
            act(A("u0", VH, V), rest)
            for k in range(4):
                tt(A("Cf", k, NV, 4), A("P0"), A("R", k, NV, 4), ALU.min)
                if k < SF:
                    act(A("nM", k, NS, 4), A("R", NV + k, NC, 4), AF.Relu, bias=1.0, scale=-1.0)
                    o = A("P%d" % (4 + 2 * (k & 1)), 0, V - VH)
                    mm(o, A("mIb"), A("nM", k, NS, 4), True, False)
                    mm(o, A("If"), A("u0", VH, V), False, True)
                    act(A("Cf", NV + k, NC, 4), o, AF.Relu)
                else:
                    tt(A("Cf", NV + k, NC, 4), rest, A("R", NV + k, NC, 4), ALU.min)
            arrive(x3)
            win = "Cf"
            for sw, (bank, w, c, wa, first) in enumerate((("P5", "c15", 2.0 ** -15, "c2", "b1"), ("P1", "c2", 0.25, "c2", "valS"),
                                                          ("P5", "If", 1.0, "If", "valS"))):
                rest, mine = A(bank, 0, V - VC), A("P0", 0, VC)
                if sw == 2:
                    mm(mine, A("Ib"), A("Db", 0, VC), True, True)
                    mm(rest, A("pIb"), A("Db", VC, V), True, False)
                    mm(rest, A("mIb"), A("one", 0, V - VC), False, False)
                mm(rest, A(wa), A("valS", VC, V), sw < 2, False)
                sum32(A(win), "invL", first, "mf", bank, w)
                if sw == 2:
                    act(A("mf", VC, V), rest, AF.Relu)
                    dma("y", ("out", "mu", VC, V), A("mf", VC, V))
                    for q, lo, hi in (("y", 0, 256), ("s", 256, VC)):
                        tt(A("mf", lo, hi), A("P0", lo, hi), A("mf", lo, hi), ALU.mult)
                        dma(q, ("out", "mu", lo, hi), A("mf", lo, hi))
                    break
                act(A("mf", VC, V), rest, scale=1.0 / c)
                export(A("mf"), "wbU", c)
                xm = send(True)
                act(mine, A("mf", 0, VC), scale=c)
                if sw == 0:
                    for k in range(SW):
                        act(A("nM", 4 * VC + k, NC, 4), A("Cf", 4 * VC + k, NC, 4), AF.Relu, bias=1.0, scale=-1.0)
                for k in range(4):
                    tt(A("W", k, 4 * VC, 4), mine, A("Cf", k, 4 * VC, 4), ALU.min)
                for k in range(SW, 4):
                    tt(A("W", 4 * VC + k, NC, 4), rest, A("Cf", 4 * VC + k, NC, 4), ALU.min)
                for k in range(SW):
                    o = A("P%d" % (4 + 2 * (k & 1)), 0, V - VC)
                    mm(o, A("mIb"), A("nM", 4 * VC + k, NC, 4), True, False)
                    mm(o, A(w), A("mf", VC, V), False, True)
                    act(A("W", 4 * VC + k, NC, 4), o, AF.Relu)
                for h, (lo, hi) in enumerate(HALF):
                    o = A("P%d" % (2 + h), 0, hi - lo)
                    if sw == 0:
                        tt(o, o, A("R", 4 * lo + 3, 4 * hi, 4), ALU.subtract)
                        act(o, o, AF.Relu, scale=2.0 ** -27)
                    else:
                        tt(A("pO", lo, hi), A("debtI", lo, hi), o, ALU.subtract)
                if sw == 1:
                    dma("y", ("out", "pay", 0, V), A("pO"))
                for x, lo, hi in halves(xm, "Bf", "P6"):
                    tt(A("W", lo, hi), x, A("Cf", lo, hi), ALU.min)
                win = "W"
            break

        base(("P4", "P5"), "Ib", "one")
        for h, (lo, hi) in enumerate(HALF):
            for k in range(4 - len(SIDE0[h]), 4):
                act(A("nM", 4 * lo + k, 4 * hi, 4), A("R", 4 * lo + k, 4 * hi, 4), AF.Relu, bias=1.0, scale=-1.0)
        spread("C0b", "R", 0, ("P0", "P1"), ALU.min, (SIDE0, (("Ib", "Db", None), ("nIb", "nM", (0,))), AF.Relu, 0.0))
        if t == 0:
            act(A("i9", 0, 112), A("i9", 0, 112), bias=col(13))
            act(A("i9", 112, 126), A("i9", 112, 126), bias=col(0))
            act(A("iB"), A("i9", 112, 126))
            act(col(15), col(14), bias=float(DM), scale=float(NA))
            act(A("rIh"), A("Ib"), scale=-0.25)
        act(A("vF", 0, 14), A("i9", 112, 126), bias=float(3 - t), scale=4.0)
        act(A("vF", 14, 28), A("i9", 112, 126), bias=float(NA * r0))
        act(A("kk"), A("i9"), bias=float(1 - 256 * r0), scale=0.0)
        port0 = lambda r: DM + 16 * r + r0
        port4 = lambda r: DM + 16 * (r >> 2) + r0
        ports = lambda r: DM + 16 * (r >> 2) + r0 + (r & 3)
        for k in range(4):
            act(A("MA", NA * k, NA * k + NA), A("R", r0 + k, NC, 16), AF.Sign)
        arrive(x3)
        extract(A("P6", 0, 56), "EP", "invT", port4, 56, 64)
        extract(A("P6", 56, 70), "EE", "invT", port0, 14, 256)
        x4 = threats("C0b", "Z", ("P4", "P5"), "mb1", "snd%d" % x3, FIRST[t][0])
        ts(A("g4U"), A("P6", 0, 56), col(15), ALU.add)
        tt(A("vdU"), A("P6", 56, 70), A("vF", 0, 14), ALU.not_equal)
        cpy(A("wU"), A("P6", 56, 70))
        act(A("xw"), A("P6", 56, 70), bias=float(NA))
        extract(A("P0", 56, 70), "EP", "invT", port0, 14, 256)
        extract(A("P0", 0, 56), "E4", "MA", lambda r: r, 56, 16)
        extract(A("P1", 0, 56), "EE", "invT", ports, 56, 64)
        ts(A("aU"), A("P1", 0, 56), V, ALU.min)
        ts(A("aW"), A("P1", 0, 56), 16 - V, ALU.add, 0, ALU.max)
        for c in (0, 28):
            (cpy if c < 28 * GWV else act)(A("gw", 16 * c, 16 * c + DM), IND(A("sigT"), A("g4U", c, c + 28)))
        act(A("vdR"), IND(A("c01"), A("vdU")))
        for l in range(4):
            hand(A("mk", l, V, 4), A("Z", r0 + l, NC, 16))
        mm(A("P6", 0, 126), A("If"), A("kk"), True, False)
        extract(A("P6", 0, 56), "KS", "sigT", lambda r: DM + NA * (r0 + (r & 3)) + (r >> 2), 56, 4, False, False)
        tt(A("kI"), A("P0", 0, 56), A("kc"), ALU.add)
        tt(A("kI", 0, 28), A("kI", 0, 28), A("kI", 28, 56), ALU.min)
        tt(A("kI", 0, 14), A("kI", 0, 14), A("kI", 14, 28), ALU.min)
        ts(A("kI", 14, 28), A("kI", 0, 14), 3, ALU.bitwise_and)
        ts(A("kI", 0, 14), A("kI", 14, 28), NA, ALU.mult)
        tt(A("rF", 0, 14), A("kI", 0, 14), A("vF", 14, 28), ALU.add)
        tt(A("rF", 14, 28), A("P0", 56, 70), A("kI", 0, 14), ALU.add)
        cpy(A("rU"), A("rF"))
        act(A("vS"), IND(A("sigT", DM, DM + NX), A("rU")))
        extract(A("P6", 112, 126), "KI", "invT", port0, 14, 256, False, False)
        extract(A("P6", 56, 112), "KS", "gw", lambda r: r, 56, 16, False)
        extract(A("P1", 28, 56), "ES", "vS", lambda r: r, 28, 16)
        extract(A("P1", 0, 28), "XS", "vS", lambda r: r, 28, 16)
        tt(A("n1"), A("P6", 0, 126), A("i9"), ALU.is_le)
        tt(A("n2"), A("P6", 0, 126), A("n1"), ALU.mult)
        cpy(A("cU"), A("n2"))
        cpy(A("sU"), A("P1", 0, 56))
        act(A("xx", 28, 42), A("P1", 14, 28), bias=float(DM))
        act(A("xx", 42, 56), A("P1", 0, 14), bias=float(DM))
        act(A("vC"), IND(A("cp", DM, DM + NX), A("sU", 0, 28)))
        act(A("vL"), IND(A("Lq"), A("sU", 28, 56)))
        mm(A("P6", 0, 14), A("Ib"), A("iB"), True, False)
        mm(A("P0", 0, DM), A("nIb"), A("vC"), True, False)
        mm(A("P0", 0, NA), A("Ih"), A("vL", NA, DM), False, False)
        mm(A("P0", NA, DM), A("Ih"), A("vL", 0, NA), False, True)
        act(A("yn"), A("P0", 0, DM), AF.Relu)
        mm(A("P1", 0, DM), A("nIb"), A("vC"), True, False)
        mm(A("P1", 0, DM), A("Ih"), A("vL"), False, True)
        act(A("yo"), A("P1", 0, DM), AF.Relu, scale=1.0)
        mm(A("P0", 0, DM), A("qIh"), A("yn"), True, False)
        mm(A("P0", 0, DM), A("rIh"), A("yo"), False, True)
        act(A("dv"), A("P0", 0, NA), bias=12.0 / 128, scale=1.0 / 128)
        act(A("dw"), A("P0", NA, DM))
        tt(A("nw"), IND(A("S14", NA, NA + V + E), A("wU")), A("dw"), ALU.add)
        tt(A("nq"), IND(A("Lq"), A("wU")), A("nw"), ALU.min)
        spread("C1b", "C0b", 0, ("P4", "P5"), ALU.mult, (SIDE1, (("Ib", "mb1", None), ("sIb", "C0b", (0,))), AF.Relu, -16.0))
        arrive(x4, *READY[1])
        base(("P2", "P3"), "Ib", "one")
        x5 = threats("C1b", "Z2", ("P2", "P3"), "mb2", "snd%d" % x3, FIRST[t][1])
        mm(A("P5", 0, NA), A("sIb"), A("Db", 3 - t, V, 4), True, False)
        mm(A("P4", 0, NA), A("sIb"), A("vdR"), True, False)
        mm(A("P4", 0, NA), A("NE"), A("invT", DM + r0, DM + NC, 16), False, False)
        for lo, hi in ((0, DM), (DM, V)):
            tt(A("z3", lo, hi), IND(A("mb2"), A("aU", lo // 16, hi // 16)), A("mk", lo, hi), ALU.mult)
        for l in range(4):
            mm(A("P5", 0, NA), A("qIb"), A("z3", l, V, 4), False, False)
        arrive(x5, *READY[2])
        for q, lo, hi in (("v", 0, DM), ("s", DM, V)):
            (cpy if q == "v" else act)(A("MA", lo, hi), IND(A("w5"), A("aW", lo // 16, hi // 16)))
            for l in range(4):
                mm(A("P5", lo // 4, hi // 4), A("qIb"), A("MA", lo + l, hi, 4), False, l == 3 and hi == V)
        ts(A("vote"), A("P5", 0, NA), A("thr"), ALU.is_ge)
        mm(A("P4", 0, NA), A("blk"), A("vote"), False, True)
        ts(A("actW", 1, NA + 1), A("P4", 0, NA), 24.5, ALU.is_ge)
        mm(A("P2", 0, NA), A("sIb"), A("actW", 1, NA + 1), True, False)
        act(A("cg", 2 * V, 9 * NA), IND(A("actW"), A("cU", 112, 126)))
        mm(A("P2", 0, NA), A("nIb"), A("cg", 2 * V, 2 * V + NA), False, False)
        for q, lo, hi in CHG:
            (cpy if q == "v" else act)(A("cg", lo, hi), IND(A("actW"), A("cU", lo // 16, hi // 16)))
            for j in range(4):
                mm(A("P2", (lo % V) // 4, ((hi - 1) % V + 1) // 4), A("nIb"), A("cg", lo + j, hi, 4), False, hi == 2 * V and j == 3)
        okv = A("okF", 3 - t, V, 4)
        ts(okv, A("P2", 0, NA), 15.5, ALU.is_ge, 128.0, ALU.mult)
        extract(A("P6", 0, 14), "E4", "okF", lambda r: 4 * r + 3 - t, 14, 64, False)
        mm(A("P5", 0, NA), A("Ib"), okv, True, True)
        tt(A("P5", 0, NA), A("P5", 0, NA), A("dv"), ALU.mult)
        sv = A("S14", NA + 3 - t, NA + V, 4)
        tt(A("P5", 0, NA), A("P5", 0, NA), sv, ALU.add)
        tt(A("q1", 3 - t, V, 4), A("P5", 0, NA), A("Lq", 3 - t, V, 4), ALU.min)
        tt(A("owU"), A("P6", 0, 14), A("xw"), ALU.min)
        cpy(IND(A("q1w"), A("owU")), A("nq"))
        export(A("q1", 0, V), "xbU")
        x1 = send(False)
        if t + 1 < RO:
            act(sv, A("P5", 0, NA))
            cpy(IND(A("S14"), A("owU")), A("nw"))
        act(A("xx", 0, 14), A("rF", 14, 28), bias=float(DM))
        act(A("xx", 14, 28), A("rF", 0, 14), bias=float(DM))
        for j in range(4):
            act(A("o4", 14 * j, 14 * j + 14), A("P6", 0, 14), bias=float(NA * (j & 1)))
        act(A("vN"), IND(A("invT", DM, DM + NX), A("sU", 0, 28)))
        tt(A("oU"), A("o4"), A("xx"), ALU.min)
        cpy(IND(A("sigT"), A("oU", 0, 28)), A("vS"))
        for b, w, x, c in (("P7", "Ih", "e16", 1.0), ("P4", "nIb", "LB", -1.0)):
            mm(A(b, 0, NA), A("dIb"), okv, True, False)
            mm(A(b, 0, NA), A(w), A(x, 3 - t, V, 4), False, True)
            act(A(x, 3 - t, V, 4), A(b, 0, NA), scale=c)
        for b, lo, hi in (("P5", 0, 96), ("P6", 96, NA)):
            extract(A(b, lo, hi), "ES", "sigT", lambda r: DM + NA * r + lo, hi - lo, 1)
            cpy(A("atO", lo, hi), A(b, lo, hi))
        for w, x in (("cp", "vC"), ("invT", "vN")):
            for c in (0, 14):
                cpy(IND(A(w), A("oU", 28 + c, 42 + c)), A(x, 16 * c, 16 * c + NA))
    return ops


def order(ops):
    seen = {}
    deps = []
    for n, (q, kind, args, rd, wr) in enumerate(ops):
        need = set()
        dma = kind in ("dma", "send")
        for acc, is_w in ((rd, False), (wr, True)):
            for name, lo, hi, step in acc:
                psum = SCRATCH[name][0] == "psum"
                for m, mlo, mhi, mstep, m_w in seen.get(name, ()):
                    same = ops[m][0] == q and not dma and ops[m][1] not in ("dma", "send", "arrive")
                    hit = mlo < hi and lo < mhi and (lo - mlo) % math.gcd(step, mstep) == 0 and (m_w or is_w)
                    if same and kind == "mm":
                        hit = hit and args[3]
                    if hit or (psum and not same):
                        need.add(m)
        for acc, is_w in ((rd, False), (wr, True)):
            for name, lo, hi, step in acc:
                seen.setdefault(name, []).append((n, lo, hi, step, is_w))
        deps.append(need)
    return deps


def cost(op, c):
    q, kind, a = op[:3]

    def wide(x):
        return 4 if SCRATCH[x[1]][2] in (F32, I32) else 2

    def count(x):
        return 16 * (x[2][3] - x[2][2]) if x[0] == "ind" else len(range(x[2], x[3], x[4]))

    def psum(x):
        return SCRATCH[x[1]][0] == "psum"

    if kind == "arrive":
        return 0.0, 0.0
    if kind == "send":
        return 500.0, c["flight"]
    if kind == "dma":
        x = a[0] if a[0][0] == "ap" else a[1]
        return 60.0, 2000.0 + 0.21 * count(x) * wide(x)
    if kind == "mm":
        t = max(64, count(a[2])) * (4 if wide(a[2]) == 4 else 1) * c["pe"] + 5
        return t, t
    k = count(a[0])
    if a[0][0] == "ind":
        t = k * c["scatter"]
    elif kind in ("iota", "sel"):
        t = 130 + 2 * k
    elif kind == "fill":
        t = k * wide(a[0]) / 4
    elif a[1][0] == "ind":
        t = k * max(c["gather"], c.get("fused", 0) if kind == "tt" else 0)
    elif kind == "tt":
        t = k * (1 if psum(a[1]) or psum(a[2]) else 2)
    elif kind == "act":
        t = k
    else:
        t = k * (0.5 if wide(a[0]) == 2 and wide(a[1]) == 2 else 1)
    t = max(t, 64) + c["call"] * (1.3 if q == "s" else 1.0)
    return t, t


def links(ops, deps):
    out = []
    last = {}
    for n, op in enumerate(ops):
        keys = []
        if op[1] == "mm":
            keys = [("bank", op[4][0][0])] + ([op[2][5]] if op[2][5] else [])
        elif op[1] == "send":
            keys = [("x", op[2][0]), "xs"]
        more = set(last[k] for k in keys if k in last)
        if op[1] == "arrive":
            more.add(last[("x", op[2][0])])
        for k in keys:
            last[k] = n
        out.append(set(m for m in deps[n] if ops[m][1] != "send") | more)
    return out


def plan():
    ops = build()
    deps = order(ops)
    pre = links(ops, deps)
    one = [cost(op, COST) for op in ops]
    unit, members, tm = [], [], []
    for n, op in enumerate(ops):
        m = n - 1
        if (op[1] == "mm" and ops[m][1] == "mm" and op[2][0][1] == ops[m][2][0][1] and op[2][2][1] == ops[m][2][2][1]
                and tm[-1][0] + one[n][0] <= LUMP and not op[2][3] and deps[n] <= deps[members[-1][0]]):
            members[-1].append(n)
            tm[-1] = (tm[-1][0] + one[n][0],) * 2
        else:
            members.append([n])
            tm.append((max(one[n][0], 0.001), one[n][1]))
        unit.append(len(members) - 1)
    size = len(members)
    line_of = [ops[ms[0]][0] for ms in members]
    gap = []
    above = []
    for u, ms in enumerate(members):
        d = {}
        for n in ms:
            for m in pre[n]:
                if unit[m] != u:
                    w = tm[unit[m]][1] + COST["hop"] if m in deps[n] or ops[n][1] == "arrive" else tm[unit[m]][0] + 0.001
                    d[unit[m]] = max(d.get(unit[m], 0.0), w)
        far = 0
        for m in d:
            far |= above[m]
        gap.append({m: w for m, w in d.items() if not far >> m & 1 or ops[members[m][0]][1] == "send"})
        for m in d:
            far |= 1 << m
        above.append(far)
    post = [{} for n in range(size)]
    for n in range(size):
        for m, d in gap[n].items():
            post[m][n] = d
    sends = [u for u in range(size) if ops[members[u][0]][1] == "send"]

    def place(turn, before, back):
        busy = {q: ([], []) for q in set(line_of)}
        at = [0.0] * size
        for n in turn:
            need = tm[n][0]
            if back:
                t = tm[n][1] - need
                for m, d in before[n].items():
                    if at[m] + tm[m][0] + d - need > t:
                        t = at[m] + tm[m][0] + d - need
            else:
                t = 0.0
                for m, d in before[n].items():
                    if at[m] + d > t:
                        t = at[m] + d
            first, end = busy[line_of[n]]
            j = len(end)
            while j > 0 and end[j - 1] > t:
                j -= 1
            while j < len(end) and t + need > first[j]:
                if end[j] > t:
                    t = end[j]
                j += 1
            first.insert(j, t)
            end.insert(j, t + need)
            at[n] = t
        if back:
            return [-(at[n] + tm[n][0]) for n in range(size)]
        return at

    other = dict(COST)
    other.update(COST2)
    tm2 = []
    for ms in members:
        c = [cost(ops[n], other) for n in ms]
        tm2.append((max(sum(x[0] for x in c), 0.001), c[0][1] if len(ms) == 1 else sum(x[0] for x in c)))
    gap2 = [[(m, tm2[m][1] + other["hop"] if d > tm[m][0] + 0.01 else tm2[m][0]) for m, d in gap[n].items()] for n in range(size)]

    def worth(at):
        free = {q: 0.0 for q in set(line_of)}
        at2 = [0.0] * size
        for n in sorted(range(size), key=lambda k: at[k]):
            t = free[line_of[n]]
            for m, d in gap2[n]:
                if at2[m] + d > t:
                    t = at2[m] + d
            at2[n] = t
            free[line_of[n]] = t + tm2[n][0]
        return sum(w * (max(a[n] + c[n][1] for n in range(size)) + EARLY * sum(a[n] for n in sends))
                   for a, c, w in ((at, tm, 1.0), (at2, tm2, SECOND)))

    way = [t[1] for t in tm]
    for n in range(size - 1, -1, -1):
        for m, d in gap[n].items():
            way[m] = max(way[m], d + way[n])
    start = place(sorted(range(size), key=lambda k: (-way[k], k)), gap, False)
    best = worth(start)
    now = start
    for rep in range(ROUNDS):
        late = place(sorted(range(size), key=lambda k: (-now[k], -k)), post, True)
        now = place(sorted(range(size), key=lambda k: (late[k], k)), gap, False)
        if worth(now) < best:
            best, start = worth(now), now
    seed = [12345]

    def draw(k):
        seed[0] = (seed[0] * 1103515245 + 12345) % 2147483648
        return (seed[0] >> 8) * k >> 23

    def held(at):
        before = {}
        last = {}
        for n in sorted(range(size), key=lambda k: at[k]):
            before[n] = last.get(line_of[n])
            last[line_of[n]] = n
        out = []
        seen = set()
        for n in sends + [max(range(size), key=lambda k: at[k] + tm[k][1])]:
            while n is not None and n not in seen:
                seen.add(n)
                ready, by = 0.0, None
                for m, d in gap[n].items():
                    if at[m] + d > ready:
                        ready, by = at[m] + d, m
                if at[n] > ready + 0.01:
                    by = m = before[n]
                    while m is not None and at[m] + tm[m][0] > ready:
                        out.append((n, m))
                        m = before[m]
                n = by
        return out

    first, mark = start, best
    for rep in range(TRIES):
        if rep % (TRIES // RUNS) == 0:
            here, level = (first, mark) if rep + TRIES // RUNS < TRIES else (start, best)
            pairs = held(here)
        key = list(here)
        for more in range(1 + draw(2)):
            n, m = pairs[draw(len(pairs))]
            how = draw(8)
            if how < 4:
                key[m] = key[n] + 0.5 + (tm[n][0] + 3000.0 * draw(3)) * draw(2)
            elif how < 6:
                n = (n, m)[draw(2)]
                last = max([k for k in sends if here[k] < here[n]] + [0])
                mine = (above[n] | 1 << n) & ~above[last]
                step = 1000.0 * (1 + draw(8))
                for k in range(n + 1):
                    if mine >> k & 1:
                        key[k] -= step
                for k in range(n, -1, -1):
                    for j in post[k]:
                        if key[j] <= key[k]:
                            key[k] = key[j] - 0.0001
            else:
                key[n] = key[m] - 0.5
                for k in range(n, -1, -1):
                    for j in post[k]:
                        if key[j] <= key[k]:
                            key[k] = key[j] - 0.0001
        for k in range(size):
            for j in gap[k]:
                if key[j] >= key[k]:
                    key[k] = key[j] + 0.0001
        now = place(sorted(range(size), key=lambda k: (key[k], k)), gap, False)
        good = worth(now)
        if good <= level + SLACK:
            here, level = now, good
            pairs = held(here)
            if good < best:
                best, start = good, now
    seq = [n for u in sorted(range(size), key=lambda k: (start[k], k)) for n in members[u]]
    new = {m: j for j, m in enumerate(seq)}
    return [ops[m] for m in seq], [set(new[k] for k in deps[m]) for m in seq]


_PLAN = []


def rank_program(g, core, T, topo):
    rank = T.rank_of(core)
    if rank is None:
        return
    n_r = len(T.cores)
    if not _PLAN:
        _PLAN.extend(plan())
    ops, deps = _PLAN
    queue = {"v": g.vector, "s": g.scalar, "p": g.tensor, "g": g, "y": g.sync}
    own = {"v": "sv", "s": "ss", "p": "sp", "g": "sg"}
    known = {k: {} for k in queue}
    cover = {}
    waits = []
    for n, need in enumerate(deps):
        q = ops[n][0]
        if ops[n][1] == "arrive":
            waits.append([])
            cover[n] = {n: n}
            continue
        keep = []
        for m in sorted(need, reverse=True):
            if ops[m][1] == "send":
                continue
            key = ops[m][0] if ops[m][1] not in ("dma", "arrive") else m
            if known[q].get(key, -1) >= m:
                continue
            keep.append(m)
            for k, c in cover[m].items():
                known[q][k] = max(known[q].get(k, -1), c)
        waits.append(keep)
        cover[n] = dict(known[q])
        cover[n][q if ops[n][1] != "dma" else n] = n
    wanted = set(m for keep in waits for m in keep)

    def ap(x):
        if not isinstance(x, tuple):
            return x
        if x[0] == "ap" and len(x) == 6:
            return T[x[1]][x[5]:128:16, x[2]:x[3]]
        if x[0] == "ap":
            return T[x[1]][:, x[2]:x[3]:x[4]] if x[4] != 1 else T[x[1]][:, x[2]:x[3]]
        if x[0] == "ind":
            return ap(x[1]).indirect(ap(x[2]))
        if len(x) == 2:
            return T[x[1]][:]
        return T[x[1]][:, x[2]:x[3]]

    count = {k: 0 for k in own}
    mark = {}
    waited = {k: {} for k in queue}
    total = {}
    for n, (q, kind, args, rd, wr) in enumerate(ops):
        if kind == "arrive":
            mark[n] = ("arr%d" % args[0], total["arr%d" % args[0]])
            continue
        e = queue[q]
        need = {}
        for m in waits[n]:
            s, c = mark[m]
            need[s] = max(need.get(s, 0), c)
        for s, c in need.items():
            if waited[q].get(s, 0) < c:
                e.wait_ge(T.sem[s], c)
                waited[q][s] = c
        if kind == "send":
            x, back = args
            tr = []
            for d in range(1, n_r):
                dst = T.cores[(rank - d if back else rank + d) % n_r]
                eng = topo.engines(core, dst)
                k = len(eng) // 4
                part = eng[0::2][k * (d - 1):k * d] if d < n_r - 1 else eng[1::2]
                mask = 0
                for b in part:
                    mask |= 1 << b
                rid, pid, _ = topo.addr(dst)
                tr.append(RemoteDMATransfer(dst_ids=[DstId(rid=rid, pnc=pid)], dma_engine_mask=mask, remote_sem=T.sem["arr%d" % x],
                                            src=ap(A("snd%d" % x, X * (d - 1), X * d)), dst=ap(A("lnd%d" % x, X * (d - 1), X * d))))
                total["arr%d" % x] = total.get("arr%d" % x, 0) + len(part)
                total["sent"] = total.get("sent", 0) + len(part)
            g.remote_dma_fused(tr, local_sem=T.sem["sent"])
            continue
        if kind == "dma":
            e.dma_start(ap(args[0]), ap(args[1])).then_inc(T.sem[args[2]], 16)
            mark[n] = (args[2], 16)
            total[args[2]] = 16
            continue
        a = [ap(x) for x in args]
        if kind == "copy":
            ins = e.tensor_copy(a[0], a[1])
        elif kind == "ts":
            if a[5] is None:
                ins = e.tensor_scalar(a[0], a[1], a[2], None, a[4])
            else:
                ins = e.tensor_scalar(a[0], a[1], a[2], a[3], a[4], a[5])
        elif kind == "tt":
            ins = e.tensor_tensor(a[0], a[1], a[2], a[3])
        elif kind == "act":
            ins = e.activation(a[0], a[1], a[2], bias=a[3], scale=a[4])
        elif kind == "mm":
            ins = e.matmul(a[0], a[1], a[2], a[3], a[4])
        elif kind == "fill":
            ins = e.memset(a[0], a[1])
        elif kind == "sel":
            ins = e.affine_select(a[0], a[6], a[1], a[2], a[3], a[4], a[5])
        elif SCRATCH[args[0][1]][2] == I32:
            ins = e.iota(a[0], a[1], a[2], a[3])
        else:
            ins = e.iota(a[0], a[1], a[2], a[3], allow_small_or_imprecise_dtypes=True)
        if n in wanted:
            ins.then_inc(T.sem[own[q]], 1)
            count[q] += 1
            mark[n] = (own[q], count[q])
    for q in own:
        total[own[q]] = count[q]
    for s, c in total.items():
        if c and max(w.get(s, 0) for w in waited.values()) < c:
            g.wait_ge(T.sem[s], c)
